import numpy as np
import ml_dtypes


def mxq(x, axis, fmt="e4m3"):
    dtype, down = {"e4m3": (ml_dtypes.float8_e4m3fn, 7), "e5m2": (ml_dtypes.float8_e5m2, 14)}[fmt]
    v = np.moveaxis(np.asarray(x, np.float32).astype(ml_dtypes.bfloat16).astype(np.float64), axis, -1)
    blocks = v.reshape(v.shape[:-1] + (-1, 32))
    amax = np.abs(blocks).max(-1, keepdims=True)
    byte = np.maximum(np.where(amax > 0, np.frexp(amax)[1] - 1 + 127, 0) - down, 1)
    scale = np.exp2(byte - 127.0)
    codes = (blocks / scale).astype(np.float32).astype(dtype).astype(np.float64)
    return np.moveaxis((codes * scale).reshape(v.shape), -1, axis)


WIDE = False


def mx_kscale(k):
    if not WIDE:
        return np.ones(k)
    levels = np.array([10, -10, 5, -5, 0])
    if k % 512:
        return np.exp2(np.random.permutation(np.resize(levels, k // 32))).repeat(32)
    a = np.empty((k // 512, 16))
    for p in range(k // 512):
        a[p, :8] = np.random.permutation(np.resize(levels, 8))
        for g in range(8):
            far = levels[np.abs(levels - a[p, g]) >= 10]
            a[p, g + 8] = far[np.random.randint(len(far))]
    return np.exp2(a.ravel()).repeat(32)


BF16 = ml_dtypes.bfloat16


def bf(x):
    return np.asarray(x, np.float32).astype(BF16)


def f64(x):
    return np.asarray(x).astype(np.float64)


E2M1 = np.array([0.0, 0.5, 1.0, 1.5, 2.0, 3.0, 4.0, 6.0, -0.0, -0.5, -1.0, -1.5, -2.0, -3.0, -4.0, -6.0])


def pack_weight(w, fmt):
    k, n = w.shape
    w = f64(bf(w)).reshape(k // 32, 32, n)
    amax = np.abs(w).max(1)
    if fmt == "e4m3":
        byte = np.frexp(amax)[1] - 1 + 127 - 7
    else:
        mant, ex = np.frexp(amax / 6.0)
        byte = np.where(mant > 0.5, ex, ex - 1) + 127
    byte = np.clip(np.where(amax > 0, byte, 1), 1, 254)
    scaled = (w * np.exp2(127.0 - byte)[:, None, :]).reshape(k, n).astype(np.float32)
    by_word = np.ascontiguousarray(scaled.reshape(k // 512, 128, 4, n).transpose(0, 1, 3, 2))
    if fmt == "e4m3":
        words = by_word.astype(ml_dtypes.float8_e4m3fn).view(np.uint8)
    else:
        c = by_word.astype(ml_dtypes.float4_e2m1fn).view(np.uint8) & 0xF
        words = c[..., 0::2] | (c[..., 1::2] << 4)
    return np.ascontiguousarray(words), np.ascontiguousarray(byte.astype(np.uint8).reshape(k // 512, 16, n))


def unpack_weight(words, scales, fmt):
    g, p, n, _ = words.shape
    if fmt == "e4m3":
        vals = np.ascontiguousarray(words).view(ml_dtypes.float8_e4m3fn).astype(np.float64)
    else:
        nib = np.empty((g, p, n, 4), np.uint8)
        nib[..., 0::2] = words & 0xF
        nib[..., 1::2] = words >> 4
        vals = E2M1[nib]
    vals = vals * np.repeat(np.exp2(scales.astype(np.float64) - 127.0), 8, axis=1)[..., None]
    return vals.transpose(0, 1, 3, 2).reshape(g * 512, n)
def pack4(w):
    words, scales = pack_weight(w, "e2m1")
    return words.reshape(words.shape[0], 128, -1), scales


def unpack4(words, scales):
    return unpack_weight(words.reshape(words.shape[0], 128, -1, 2), scales, "e2m1")


D, J, T, L, R = 1024, 512, 1024, 1024, 1024


def draw0():
    s = mx_kscale(J)
    v = mx_kscale(L)
    t = mx_kscale(T)
    phase = np.random.uniform(0.0, 2.0 * np.pi, (D, J))
    cs = np.concatenate([np.cos(phase), np.sin(phase)], axis=0)
    h = np.random.standard_normal((J, T)) * np.sqrt(2.0 / J) / T ** 0.25
    echo = np.random.standard_normal((T, L))
    w = np.random.standard_normal((L, R)) / np.sqrt(L) / T ** 0.25
    taper = np.random.uniform(0.5, 1.5, T)
    w_words, w_scales = pack4(w / v[:, None])
    return {"cs": bf(cs * s),
            "h": bf(h / s[:, None] * t),
            "echo": bf(echo * v),
            "w_words": w_words,
            "w_scales": w_scales,
            "taper": bf(taper / t)}


def core(cs, h, echo, w_words, w_scales, taper):
    f = mxq(f64(cs), 1, "e4m3") @ mxq(f64(h), 0, "e4m3")
    p = mxq(f64(echo), 1, "e4m3") @ unpack4(w_words, w_scales)
    z = p * f64(taper)[:, None]
    y = mxq(f, 1, "e4m3") @ mxq(z, 0, "e4m3")
    e = np.square(y)
    return e[:D] + e[D:]


def e4m3fn_bytes(y):
    return np.clip(np.asarray(y, np.float64), -448.0, 448.0).astype(np.float32).astype(ml_dtypes.float8_e4m3fn).view(np.uint8)


def e4m3fn_values(b):
    return np.asarray(b, np.uint8).view(ml_dtypes.float8_e4m3fn).astype(np.float64)


def setup_inputs():
    d = draw0()
    x0 = np.asarray(d['echo']).astype(np.float64)
    s = (np.max(np.abs(x0), axis=(0,), keepdims=True) / 448.0).astype(np.float32)
    out = {}
    for k, v in d.items():
        if k == 'echo':
            out['echo_bytes'] = e4m3fn_bytes(x0 / s.astype(np.float64))
            out['echo_scale'] = s
        else:
            out[k] = v
    return out


def reference(cs, h, echo_bytes, echo_scale, w_words, w_scales, taper):
    return core(cs, h, e4m3fn_values(echo_bytes) * echo_scale.astype(np.float64), w_words, w_scales, taper)

@@ -1,0 +1,400 @@
+from contextlib import ExitStack
+
+import concourse.mybir as mybir
+from concourse.masks import make_identity
+
+D, J, T, L, R = 1024, 512, 1024, 1024, 1024
+
+F32 = mybir.dt.float32
+BF16 = mybir.dt.bfloat16
+I32 = mybir.dt.int32
+U32 = mybir.dt.uint32
+U8 = mybir.dt.uint8
+FP8 = mybir.dt.float8_e4m3fn
+FP8X4 = mybir.dt.float8_e4m3fn_x4
+FP4X4 = mybir.dt.float4_e2m1fn_x4
+ACT = mybir.ActivationFunctionType
+ALU = mybir.AluOpType
+
+P = 128
+CH = 4
+W512 = 512
+
+FLOPS = 2 * (2 * D * J * T + T * L * R + 2 * D * T * R)
+
+
+def tile_isar_split_real_image_s11_kernel(
+    tc, cs, h, echo_bytes, echo_scale, w_words, w_scales, taper, out
+):
+    nc = tc.nc
+    with ExitStack() as ctx:
+        keep = ctx.enter_context(tc.tile_pool(name="keep", bufs=1))
+        work = ctx.enter_context(tc.tile_pool(name="work", bufs=4))
+        outs = ctx.enter_context(tc.tile_pool(name="outs", bufs=4))
+        psum = ctx.enter_context(tc.psum_pool(name="psum", bufs=8))
+
+        ident = keep.tile([P, P], F32, name="ident", align_bytes=64)
+        ident_bf = keep.tile([P, P], BF16, name="ident_bf", align_bytes=64)
+        scale_p8 = keep.tile([P, 2, 4], F32, name="scale_p8")
+        scale_bc = keep.tile([P, L], F32, name="scale_bc", align_bytes=64)
+        taper_bf = keep.tile([P, 2, 4], BF16, name="taper_bf")
+        taper_f = keep.tile([P, 2, 4], F32, name="taper_f")
+        idle = keep.tile([P, W512], BF16, name="idle", align_bytes=64)
+        warm = keep.tile([P, 1], F32, name="warm")
+        cs_raw = [keep.tile([P, 4, J], BF16, name="cs_raw%d" % c, align_bytes=64) for c in range(CH)]
+        cs_grp = [keep.tile([P, W512, 4], BF16, name="cs_grp%d" % c, align_bytes=64) for c in range(CH)]
+        cs_q = [keep.tile([P, W512], U32, name="cs_q%d" % c, align_bytes=64) for c in range(CH)]
+        cs_s = [keep.tile([P, W512], U8, name="cs_s%d" % c, align_bytes=64) for c in range(CH)]
+        h_raw = [keep.tile([P, 4, W512], BF16, name="h_raw%d" % g, align_bytes=64) for g in range(2)]
+        h_grp = [keep.tile([P, W512, 4], BF16, name="h_grp%d" % g, align_bytes=64) for g in range(2)]
+        h_q = [keep.tile([P, W512], U32, name="h_q%d" % g, align_bytes=64) for g in range(2)]
+        h_s = [keep.tile([P, W512], U8, name="h_s%d" % g, align_bytes=64) for g in range(2)]
+        e_bytes = [keep.tile([P, 4, L], U8, name="e_bytes%d" % g, align_bytes=64) for g in range(2)]
+        e_grp = [keep.tile([P, 2, W512, 4], BF16, name="e_grp%d" % g, align_bytes=64) for g in range(2)]
+        e_q = [keep.tile([P, 2, W512], U32, name="e_q%d" % g, align_bytes=64) for g in range(2)]
+        e_s = [keep.tile([P, 2, W512], U8, name="e_s%d" % g, align_bytes=64) for g in range(2)]
+        w_q = keep.tile([P, 2, 2 * R], U8, name="w_q", align_bytes=64)
+        w_s = keep.tile([P, 2, R], U8, name="w_s", align_bytes=64)
+        f_q = [[keep.tile([P, W512], U32, name="f_q%d%d" % (c, g), align_bytes=64) for g in range(2)] for c in range(CH)]
+        f_s = [[keep.tile([P, W512], U8, name="f_s%d%d" % (c, g), align_bytes=64) for g in range(2)] for c in range(CH)]
+        z_q = [[keep.tile([P, W512], U32, name="z_q%d%d" % (g, r), align_bytes=64) for r in range(2)] for g in range(2)]
+        z_s = [[keep.tile([P, W512], U8, name="z_s%d%d" % (g, r), align_bytes=64) for r in range(2)] for g in range(2)]
+        e_sc = {}
+        f_grp = {}
+        z_grp = {}
+        banks = {}
+
+        def bank():
+            t = psum.tile([P, W512], F32, name="bank")
+            return t
+
+        ctx.enter_context(tc.manual_schedule())
+        make_identity(nc, ident[:])
+        make_identity(nc, ident_bf[:])
+        nc.gpsimd.memset(w_s[:].bitcast(I32), 0)
+        nc.vector.memset(idle[:], 0.0)
+        nc.vector.memset(warm[:], 0.0)
+        nc.scalar.dma_start(out=scale_p8[:], in_=echo_scale.rearrange("o (a p c) -> p (o a) c", a=2, c=4))
+        nc.scalar.dma_start(out=taper_bf[:], in_=taper.rearrange("(g p t) -> p g t", p=P, t=4))
+        nc.scalar.activation(out=warm[:], in_=warm[:], func=ACT.Square)
+
+        def load_cs(c, part):
+            row = part * D + c * 256
+            nc.sync.dma_start(
+                out=cs_raw[c][:, 2 * part : 2 * part + 2, :],
+                in_=cs[row : row + 256, :].rearrange("(p j) k -> p j k", j=2),
+            )
+
+        def load_h(g):
+            nc.sync.dma_start(
+                out=h_raw[g][:],
+                in_=h.rearrange("(p j) w -> p j w", j=4)[:, :, g * W512 : (g + 1) * W512],
+            )
+
+        def load_e(g, half):
+            nc.sync.dma_start(
+                out=e_bytes[g][:, 2 * half : 2 * half + 2, :],
+                in_=echo_bytes[g * W512 : (g + 1) * W512, :].rearrange("(m t) k -> m t k", t=4)[
+                    :, 2 * half : 2 * half + 2, :
+                ],
+            )
+
+        def load_w():
+            nc.sync.dma_start(out=w_q[:].bitcast(I32), in_=w_words.bitcast(I32).rearrange("g p n -> p g n"))
+            for q in range(4):
+                nc.sync.dma_start(
+                    out=w_s[32 * q : 32 * q + 4, :, :].bitcast(I32),
+                    in_=w_scales[:, 4 * q : 4 * q + 4, :].bitcast(I32).rearrange("g q n -> q g n"),
+                )
+
+        load_e(0, 0)
+        load_cs(0, 0)
+        load_cs(0, 1)
+        load_h(0)
+        load_e(0, 1)
+        load_e(1, 0)
+        load_e(1, 1)
+        load_cs(1, 0)
+        load_cs(1, 1)
+        load_h(1)
+        load_cs(2, 0)
+        load_cs(2, 1)
+        load_w()
+        load_cs(3, 0)
+        load_cs(3, 1)
+
+        def spin(b, n):
+            for r in range(n):
+                nc.tensor.matmul(out=b[:], lhsT=idle[:, 0:P], rhs=idle[:], start=True, stop=True)
+
+        spins = {("s", 0): 2}
+
+        def scale_spread():
+            for a in range(2):
+                b = bank()
+                spin(b, spins.get(("s", a), 0))
+                for c in range(4):
+                    nc.tensor.transpose(
+                        b[:, c * P : (c + 1) * P],
+                        scale_p8[:, a, c : c + 1].to_broadcast([P, P]),
+                        ident[:],
+                    )
+                dst = scale_bc[:, a * W512 : (a + 1) * W512].rearrange("p (n c) -> p n c", c=4)
+                src = b[:].rearrange("p (c n) -> p n c", c=4)
+                if a == 0:
+                    nc.vector.tensor_copy(out=dst, in_=src)
+                else:
+                    nc.scalar.copy(out=dst, in_=src)
+
+        def c_turn(c):
+            for part in range(2):
+                b = bank()
+                banks["c", c, part] = b
+                spin(b, spins.get(("c", c), 0) if part == 0 else 0)
+                for j in range(2):
+                    words = cs_raw[c][:, 2 * part + j, :].bitcast(F32)
+                    for u in range(2):
+                        nc.tensor.transpose(
+                            b[:, (2 * j + u) * P : (2 * j + u + 1) * P], words[:, u : 2 * P : 2], ident[:]
+                        )
+
+        def c_out(c):
+            for part in range(2):
+                b = banks["c", c, part]
+                dst = cs_grp[c][:, 256 * part : 256 * part + 256, :].rearrange("p n t -> p (n t)").bitcast(F32)
+                nc.scalar.copy(
+                    out=dst.rearrange("p (j m u) -> p j m u", j=2, u=2),
+                    in_=b[:].rearrange("p (j u m) -> p j m u", j=2, u=2),
+                )
+
+        def c_quant(c):
+            nc.vector.quantize_mx(
+                out=cs_q[c][:].bitcast(FP8X4), scales=cs_s[c][:], in_=cs_grp[c][:].rearrange("p n t -> p (n t)")
+            )
+
+        def h_pass(g, halves=(0, 1)):
+            for half in halves:
+                b = psum.tile([P, 2 * W512], BF16, name="bank")
+                banks["h", g, half] = b
+                for j in range(4):
+                    nc.tensor.matmul(
+                        out=b[:, 256 * j : 256 * (j + 1)],
+                        lhsT=ident_bf[:],
+                        rhs=h_raw[g][:, j, 256 * half : 256 * (half + 1)],
+                        start=True,
+                        stop=True,
+                    )
+
+        def h_out(g, halves=(0, 1)):
+            for half in halves:
+                dst = h_grp[g][:].rearrange("p (t m) j -> p t m j", t=4)[:, :, 64 * half : 64 * (half + 1), :]
+                nc.scalar.copy(out=dst, in_=banks["h", g, half][:].rearrange("p (j m t) -> p t m j", j=4, t=4))
+
+        def h_quant(g):
+            nc.vector.quantize_mx(
+                out=h_q[g][:].bitcast(FP8X4), scales=h_s[g][:], in_=h_grp[g][:].rearrange("p n t -> p (n t)")
+            )
+
+        def e_scale(i):
+            g, t = divmod(i, 4)
+            s = work.tile([P, L], BF16, name="e_sc", bufs=8, align_bytes=64)
+            e_sc[i] = s
+            width = W512 if i == 0 else L
+            for k in range(0, L, width):
+                ks = slice(k, k + width)
+                nc.vector.tensor_tensor(
+                    out=s[:, ks], in0=e_bytes[g][:, t, ks].bitcast(FP8), in1=scale_bc[:, ks], op=ALU.mult
+                )
+
+        def e_turn(i):
+            b = bank()
+            banks["e", i] = b
+            spin(b, spins.get(("e", i), 0))
+            words = e_sc[i][:].bitcast(F32)
+            for k in range(2):
+                for u in range(2):
+                    nc.tensor.transpose(
+                        b[:, (2 * k + u) * P : (2 * k + u + 1) * P],
+                        words[:, 2 * P * k + u : 2 * P * (k + 1) : 2],
+                        ident[:],
+                    )
+
+        def e_out(i):
+            g, t = divmod(i, 4)
+            b = banks["e", i]
+            dst = e_grp[g][:].rearrange("p k n t -> p (k n t)").bitcast(F32)
+            dst = dst.rearrange("p (k n u) -> p k n u", k=2, u=2)[:, :, t * P : (t + 1) * P, :]
+            nc.scalar.copy(out=dst, in_=b[:].rearrange("p (k u m) -> p k m u", k=2, u=2))
+
+        def e_quant(g):
+            for k in range(2):
+                nc.vector.quantize_mx(
+                    out=e_q[g][:, k, :].bitcast(FP8X4),
+                    scales=e_s[g][:, k, :],
+                    in_=e_grp[g][:, k, :, :].rearrange("p n t -> p (n t)"),
+                )
+
+        def f_mm(c, g, b):
+            t_ = bank()
+            banks["f", c, g, b] = t_
+            cols = slice(b * P, (b + 1) * P)
+            for t in range(4):
+                st = slice(t * P, (t + 1) * P)
+                nc.tensor.matmul_mx(
+                    out=t_[:, st],
+                    lhsT=h_q[g][:, st].bitcast(FP8X4),
+                    lhsT_scale=h_s[g][:, st],
+                    rhs=cs_q[c][:, cols].bitcast(FP8X4),
+                    rhs_scale=cs_s[c][:, cols],
+                    start=True,
+                    stop=True,
+                )
+
+        def f_out(c, g, b, eng):
+            if (c, g) not in f_grp:
+                f_new = work.tile([P, W512, 4], BF16, name="f_grp", bufs=6, align_bytes=64)
+                f_grp[c, g] = f_new
+            dst = f_grp[c, g][:, b * P : (b + 1) * P, :]
+            src = banks["f", c, g, b][:].rearrange("p (t n) -> p n t", t=4)
+            if eng == "v":
+                nc.vector.tensor_copy(out=dst, in_=src)
+            else:
+                nc.scalar.copy(out=dst, in_=src)
+
+        def f_quant(c, g):
+            nc.vector.quantize_mx(
+                out=f_q[c][g][:].bitcast(FP8X4), scales=f_s[c][g][:], in_=f_grp[c, g][:].rearrange("p n t -> p (n t)")
+            )
+
+        def f_bank(c, g, b):
+            f_mm(c, g, b)
+            f_out(c, g, b, "v" if (c == 3 and b > 0) or (c == 2 and b == 3) else "s")
+
+        def z_mm(g, rb):
+            t_ = bank()
+            banks["z", g, rb] = t_
+            cols = slice(rb * P, (rb + 1) * P)
+            for t in range(4):
+                st = slice(t * P, (t + 1) * P)
+                for k in range(2):
+                    nc.tensor.matmul_mx(
+                        out=t_[:, st],
+                        lhsT=e_q[g][:, k, st].bitcast(FP8X4),
+                        lhsT_scale=e_s[g][:, k, st],
+                        rhs=w_q[:, k, 2 * rb * P : 2 * (rb + 1) * P].bitcast(FP4X4),
+                        rhs_scale=w_s[:, k, cols],
+                        start=(k == 0),
+                        stop=(k == 1),
+                    )
+
+        def z_out(g, rb):
+            half, q = divmod(rb, 4)
+            if (g, half) not in z_grp:
+                z_new = work.tile([P, W512, 4], BF16, name="z_grp", align_bytes=64)
+                z_grp[g, half] = z_new
+            nc.vector.tensor_tensor(
+                out=z_grp[g, half][:, q * P : (q + 1) * P, :],
+                in0=banks["z", g, rb][:].rearrange("p (t n) -> p n t", t=4),
+                in1=taper_f[:, g : g + 1, :].to_broadcast([P, P, 4]),
+                op=ALU.mult,
+            )
+
+        def z_quant(g, half):
+            nc.vector.quantize_mx(
+                out=z_q[g][half][:].bitcast(FP8X4),
+                scales=z_s[g][half][:],
+                in_=z_grp[g, half][:].rearrange("p n t -> p (n t)"),
+            )
+
+        def y_unit(c, j, half, pieces=1):
+            width = W512 // pieces
+            rows = out[c * 256 : (c + 1) * 256, :].rearrange("(p j) r -> p j r", j=2)
+            for i in range(pieces):
+                rc = slice(i * width, (i + 1) * width)
+                sq = []
+                for part in range(2):
+                    b = bank()
+                    cols = slice((2 * part + j) * P, (2 * part + j + 1) * P)
+                    for g in range(2):
+                        nc.tensor.matmul_mx(
+                            out=b[:, 0:width],
+                            lhsT=f_q[c][g][:, cols].bitcast(FP8X4),
+                            lhsT_scale=f_s[c][g][:, cols],
+                            rhs=z_q[g][half][:, rc].bitcast(FP8X4),
+                            rhs_scale=z_s[g][half][:, rc],
+                            start=(g == 0),
+                            stop=(g == 1),
+                        )
+                    s = outs.tile([P, W512], F32, name="sq%d" % part, align_bytes=64)
+                    nc.scalar.activation(out=s[:, 0:width], in_=b[:, 0:width], func=ACT.Square)
+                    sq.append(s)
+                res = outs.tile([P, W512], F32, name="res", align_bytes=64)
+                nc.vector.tensor_tensor(out=res[:, 0:width], in0=sq[0][:, 0:width], in1=sq[1][:, 0:width], op=ALU.add)
+                at = half * W512 + i * width
+                nc.sync.dma_start(out=rows[:, j, at : at + width], in_=res[:, 0:width])
+
+        scale_spread()
+        for i in range(8):
+            e_scale(i)
+        nc.vector.tensor_copy(out=taper_f[:], in_=taper_bf[:])
+
+        def e_pair(i):
+            for n in (i, i + 1):
+                e_turn(n)
+            for n in (i, i + 1):
+                e_out(n)
+
+        c_turn(0)
+        c_out(0)
+        for i in range(2):
+            h_pass(0, (i,))
+            h_out(0, (i,))
+            e_turn(i)
+            e_out(i)
+        e_pair(2)
+        c_turn(1)
+        e_pair(4)
+        c_out(1)
+        h_pass(1)
+        h_out(1)
+        e_pair(6)
+        c_quant(0)
+        h_quant(0)
+        c_turn(2)
+        c_out(2)
+        e_quant(0)
+        h_quant(1)
+        e_quant(1)
+
+        z_list = [(g, rb) for half in range(2) for g in range(2) for rb in range(4 * half, 4 * half + 4)]
+        f_list = [(c, g, b) for c in range(CH) for g in range(2) for b in range(4)]
+        f_run = (4, 2, 2, 3, 3, 3, 3, 4)
+        after = {
+            1: (lambda: c_quant(1), lambda: c_quant(2), lambda: f_quant(0, 0)),
+            2: (lambda: c_turn(3), lambda: c_out(3), lambda: z_quant(0, 0)),
+            3: (lambda: f_quant(0, 1),),
+            4: (lambda: z_quant(1, 0), lambda: c_quant(3)),
+            5: (lambda: f_quant(1, 0),),
+            6: (lambda: z_quant(0, 1), lambda: f_quant(1, 1)),
+        }
+        for s in range(8):
+            for n in range(f_run[s]):
+                f_bank(*f_list[0])
+                f_list = f_list[1:]
+            for z in z_list[2 * s : 2 * s + 2]:
+                z_mm(*z)
+                z_out(*z)
+            for step in after.get(s, ()):
+                step()
+        z_quant(1, 1)
+        f_quant(2, 0)
+        f_quant(2, 1)
+        y_list = [(c, j, half) for c, half in ((0, 0), (1, 0), (0, 1), (1, 1), (2, 0), (2, 1), (3, 0), (3, 1)) for j in range(2)]
+        for n, y in enumerate(y_list):
+            y_unit(*y, pieces=2 if n == len(y_list) - 1 else 1)
+            if n >= 1 and f_list:
+                c, g, b = f_list[0]
+                f_bank(c, g, b)
+                f_list = f_list[1:]
+                if b == 3:
+                    f_quant(c, g)

@@ -34,14 +34,11 @@ def tile_isar_split_real_image_s11_kernel(
         psum = ctx.enter_context(tc.psum_pool(name="psum", bufs=8))
 
         ident = keep.tile([P, P], F32, name="ident", align_bytes=64)
-        ident_bf = keep.tile([P, P], BF16, name="ident_bf", align_bytes=64)
         scale_p8 = keep.tile([P, 2, 4], F32, name="scale_p8")
         scale_bc = keep.tile([P, L], F32, name="scale_bc", align_bytes=64)
         taper_bf = keep.tile([P, 2, 4], BF16, name="taper_bf")
         taper_f = keep.tile([P, 2, 4], F32, name="taper_f")
-        idle = keep.tile([P, W512], BF16, name="idle", align_bytes=64)
-        warm = keep.tile([P, 1], F32, name="warm")
-        cs_raw = [keep.tile([P, 4, J], BF16, name="cs_raw%d" % c, align_bytes=64) for c in range(CH)]
+        cs_raw = [[keep.tile([P, 2, J], BF16, name="cs_raw%d%d" % (c, a), align_bytes=64) for a in range(2)] for c in range(CH)]
         cs_grp = [keep.tile([P, W512, 4], BF16, name="cs_grp%d" % c, align_bytes=64) for c in range(CH)]
         cs_q = [keep.tile([P, W512], U32, name="cs_q%d" % c, align_bytes=64) for c in range(CH)]
         cs_s = [keep.tile([P, W512], U8, name="cs_s%d" % c, align_bytes=64) for c in range(CH)]
@@ -49,11 +46,11 @@ def tile_isar_split_real_image_s11_kernel(
         h_grp = [keep.tile([P, W512, 4], BF16, name="h_grp%d" % g, align_bytes=64) for g in range(2)]
         h_q = [keep.tile([P, W512], U32, name="h_q%d" % g, align_bytes=64) for g in range(2)]
         h_s = [keep.tile([P, W512], U8, name="h_s%d" % g, align_bytes=64) for g in range(2)]
-        e_bytes = [keep.tile([P, 4, L], U8, name="e_bytes%d" % g, align_bytes=64) for g in range(2)]
-        e_grp = [keep.tile([P, 2, W512, 4], BF16, name="e_grp%d" % g, align_bytes=64) for g in range(2)]
-        e_q = [keep.tile([P, 2, W512], U32, name="e_q%d" % g, align_bytes=64) for g in range(2)]
-        e_s = [keep.tile([P, 2, W512], U8, name="e_s%d" % g, align_bytes=64) for g in range(2)]
-        w_q = keep.tile([P, 2, 2 * R], U8, name="w_q", align_bytes=64)
+        e_bytes = [keep.tile([P, 2, L], U8, name="e_bytes%d" % n, align_bytes=64) for n in range(4)]
+        e_grp = [keep.tile([P, 2 * P, 4], BF16, name="e_grp%d" % i, align_bytes=64) for i in range(8)]
+        e_q = [keep.tile([P, 2 * P], U32, name="e_q%d" % i, align_bytes=64) for i in range(8)]
+        e_s = [keep.tile([P, 2 * P], U8, name="e_s%d" % i, align_bytes=64) for i in range(8)]
+        w_q = [keep.tile([P, 2, R], U8, name="w_q%d" % r, align_bytes=64) for r in range(2)]
         w_s = keep.tile([P, 2, R], U8, name="w_s", align_bytes=64)
         f_q = [[keep.tile([P, W512], U32, name="f_q%d%d" % (c, g), align_bytes=64) for g in range(2)] for c in range(CH)]
         f_s = [[keep.tile([P, W512], U8, name="f_s%d%d" % (c, g), align_bytes=64) for g in range(2)] for c in range(CH)]
@@ -63,27 +60,15 @@ def tile_isar_split_real_image_s11_kernel(
         f_grp = {}
         z_grp = {}
         banks = {}
+        squares = {}
 
-        def bank():
+        def bank(tag):
             t = psum.tile([P, W512], F32, name="bank")
             return t
 
-        ctx.enter_context(tc.manual_schedule())
-        make_identity(nc, ident[:])
-        make_identity(nc, ident_bf[:])
-        nc.gpsimd.memset(w_s[:].bitcast(I32), 0)
-        nc.vector.memset(idle[:], 0.0)
-        nc.vector.memset(warm[:], 0.0)
-        nc.scalar.dma_start(out=scale_p8[:], in_=echo_scale.rearrange("o (a p c) -> p (o a) c", a=2, c=4))
-        nc.scalar.dma_start(out=taper_bf[:], in_=taper.rearrange("(g p t) -> p g t", p=P, t=4))
-        nc.scalar.activation(out=warm[:], in_=warm[:], func=ACT.Square)
-
         def load_cs(c, part):
             row = part * D + c * 256
-            nc.sync.dma_start(
-                out=cs_raw[c][:, 2 * part : 2 * part + 2, :],
-                in_=cs[row : row + 256, :].rearrange("(p j) k -> p j k", j=2),
-            )
+            nc.sync.dma_start(out=cs_raw[c][part][:], in_=cs[row : row + 256, :].rearrange("(p j) k -> p j k", j=2))
 
         def load_h(g):
             nc.sync.dma_start(
@@ -91,125 +76,96 @@ def tile_isar_split_real_image_s11_kernel(
                 in_=h.rearrange("(p j) w -> p j w", j=4)[:, :, g * W512 : (g + 1) * W512],
             )
 
-        def load_e(g, half):
+        def load_e(n):
+            g, half = divmod(n, 2)
+            rows = echo_bytes[g * W512 : (g + 1) * W512, :].rearrange("(m t) k -> m t k", t=4)
+            nc.sync.dma_start(out=e_bytes[n][:], in_=rows[:, 2 * half : 2 * half + 2, :])
+
+        def load_w(r):
             nc.sync.dma_start(
-                out=e_bytes[g][:, 2 * half : 2 * half + 2, :],
-                in_=echo_bytes[g * W512 : (g + 1) * W512, :].rearrange("(m t) k -> m t k", t=4)[
-                    :, 2 * half : 2 * half + 2, :
-                ],
+                out=w_q[r][:].bitcast(I32),
+                in_=w_words[:, :, r * R : (r + 1) * R].bitcast(I32).rearrange("g p n -> p g n"),
             )
 
-        def load_w():
-            nc.sync.dma_start(out=w_q[:].bitcast(I32), in_=w_words.bitcast(I32).rearrange("g p n -> p g n"))
+        def load_ws():
             for q in range(4):
                 nc.sync.dma_start(
                     out=w_s[32 * q : 32 * q + 4, :, :].bitcast(I32),
                     in_=w_scales[:, 4 * q : 4 * q + 4, :].bitcast(I32).rearrange("g q n -> q g n"),
                 )
 
-        load_e(0, 0)
-        load_cs(0, 0)
-        load_cs(0, 1)
-        load_h(0)
-        load_e(0, 1)
-        load_e(1, 0)
-        load_e(1, 1)
-        load_cs(1, 0)
-        load_cs(1, 1)
-        load_h(1)
-        load_cs(2, 0)
-        load_cs(2, 1)
-        load_w()
-        load_cs(3, 0)
-        load_cs(3, 1)
+        def load_taper():
+            nc.sync.dma_start(out=taper_bf[:], in_=taper.rearrange("(g p t) -> p g t", p=P, t=4))
 
-        def spin(b, n):
-            for r in range(n):
-                nc.tensor.matmul(out=b[:], lhsT=idle[:, 0:P], rhs=idle[:], start=True, stop=True)
+        def copy(eng, dst, src):
+            if eng == "v":
+                nc.vector.tensor_copy(out=dst, in_=src)
+            else:
+                nc.scalar.copy(out=dst, in_=src)
 
-        spins = {("s", 0): 2}
-
-        def scale_spread():
-            for a in range(2):
-                b = bank()
-                spin(b, spins.get(("s", a), 0))
-                for c in range(4):
-                    nc.tensor.transpose(
-                        b[:, c * P : (c + 1) * P],
-                        scale_p8[:, a, c : c + 1].to_broadcast([P, P]),
-                        ident[:],
-                    )
-                dst = scale_bc[:, a * W512 : (a + 1) * W512].rearrange("p (n c) -> p n c", c=4)
-                src = b[:].rearrange("p (c n) -> p n c", c=4)
-                if a == 0:
-                    nc.vector.tensor_copy(out=dst, in_=src)
-                else:
-                    nc.scalar.copy(out=dst, in_=src)
-
-        def c_turn(c):
-            for part in range(2):
-                b = bank()
-                banks["c", c, part] = b
-                spin(b, spins.get(("c", c), 0) if part == 0 else 0)
-                for j in range(2):
-                    words = cs_raw[c][:, 2 * part + j, :].bitcast(F32)
-                    for u in range(2):
-                        nc.tensor.transpose(
-                            b[:, (2 * j + u) * P : (2 * j + u + 1) * P], words[:, u : 2 * P : 2], ident[:]
-                        )
-
-        def c_out(c):
-            for part in range(2):
-                b = banks["c", c, part]
-                dst = cs_grp[c][:, 256 * part : 256 * part + 256, :].rearrange("p n t -> p (n t)").bitcast(F32)
-                nc.scalar.copy(
-                    out=dst.rearrange("p (j m u) -> p j m u", j=2, u=2),
-                    in_=b[:].rearrange("p (j u m) -> p j m u", j=2, u=2),
+        def scale_spread(a, eng):
+            b = bank("rb")
+            for c in range(4):
+                nc.tensor.transpose(
+                    b[:, c * P : (c + 1) * P], scale_p8[:, a, c : c + 1].to_broadcast([P, P]), ident[:]
                 )
+            dst = scale_bc[:, a * W512 : (a + 1) * W512].rearrange("p (n c) -> p n c", c=4)
+            copy(eng, dst, b[:].rearrange("p (c n) -> p n c", c=4))
+
+        def c_turn(c, part):
+            b = bank("rb")
+            banks["c", c, part] = b
+            for j in range(2):
+                words = cs_raw[c][part][:, j, :].bitcast(F32)
+                for u in range(2):
+                    nc.tensor.transpose(
+                        b[:, (2 * j + u) * P : (2 * j + u + 1) * P], words[:, u : 2 * P : 2], ident[:]
+                    )
+
+        def c_out(c, part, eng="s"):
+            dst = cs_grp[c][:, 256 * part : 256 * part + 256, :].rearrange("p n t -> p (n t)").bitcast(F32)
+            copy(
+                eng,
+                dst.rearrange("p (j m u) -> p j m u", j=2, u=2),
+                banks["c", c, part][:].rearrange("p (j u m) -> p j m u", j=2, u=2),
+            )
+
+        def quant(q, s, grp):
+            nc.vector.quantize_mx(out=q[:].bitcast(FP8X4), scales=s[:], in_=grp[:].rearrange("p n t -> p (n t)"))
 
         def c_quant(c):
-            nc.vector.quantize_mx(
-                out=cs_q[c][:].bitcast(FP8X4), scales=cs_s[c][:], in_=cs_grp[c][:].rearrange("p n t -> p (n t)")
+            quant(cs_q[c], cs_s[c], cs_grp[c])
+
+        def h_weave(g, eng, ts=slice(0, 4)):
+            copy(
+                eng,
+                h_grp[g][:].rearrange("p (t m) j -> p t m j", t=4)[:, ts],
+                h_raw[g][:].rearrange("p j (m t) -> p t m j", t=4)[:, ts],
             )
 
-        def h_pass(g, halves=(0, 1)):
-            for half in halves:
-                b = psum.tile([P, 2 * W512], BF16, name="bank")
-                banks["h", g, half] = b
-                for j in range(4):
-                    nc.tensor.matmul(
-                        out=b[:, 256 * j : 256 * (j + 1)],
-                        lhsT=ident_bf[:],
-                        rhs=h_raw[g][:, j, 256 * half : 256 * (half + 1)],
-                        start=True,
-                        stop=True,
-                    )
+        def cs_part(c, part):
+            c_turn(c, part)
+            c_out(c, part)
 
-        def h_out(g, halves=(0, 1)):
-            for half in halves:
-                dst = h_grp[g][:].rearrange("p (t m) j -> p t m j", t=4)[:, :, 64 * half : 64 * (half + 1), :]
-                nc.scalar.copy(out=dst, in_=banks["h", g, half][:].rearrange("p (j m t) -> p t m j", j=4, t=4))
+        def e_part(i):
+            e_turn(i)
+            e_out(i)
 
         def h_quant(g):
-            nc.vector.quantize_mx(
-                out=h_q[g][:].bitcast(FP8X4), scales=h_s[g][:], in_=h_grp[g][:].rearrange("p n t -> p (n t)")
-            )
+            quant(h_q[g], h_s[g], h_grp[g])
 
-        def e_scale(i):
-            g, t = divmod(i, 4)
-            s = work.tile([P, L], BF16, name="e_sc", bufs=8, align_bytes=64)
+        def e_scale(i, width=L):
+            s = work.tile([P, L], BF16, name="e_sc", align_bytes=64)
             e_sc[i] = s
-            width = W512 if i == 0 else L
             for k in range(0, L, width):
                 ks = slice(k, k + width)
                 nc.vector.tensor_tensor(
-                    out=s[:, ks], in0=e_bytes[g][:, t, ks].bitcast(FP8), in1=scale_bc[:, ks], op=ALU.mult
+                    out=s[:, ks], in0=e_bytes[i // 2][:, i % 2, ks].bitcast(FP8), in1=scale_bc[:, ks], op=ALU.mult
                 )
 
         def e_turn(i):
-            b = bank()
+            b = bank("rb")
             banks["e", i] = b
-            spin(b, spins.get(("e", i), 0))
             words = e_sc[i][:].bitcast(F32)
             for k in range(2):
                 for u in range(2):
@@ -219,29 +175,25 @@ def tile_isar_split_real_image_s11_kernel(
                         ident[:],
                     )
 
-        def e_out(i):
-            g, t = divmod(i, 4)
-            b = banks["e", i]
-            dst = e_grp[g][:].rearrange("p k n t -> p (k n t)").bitcast(F32)
-            dst = dst.rearrange("p (k n u) -> p k n u", k=2, u=2)[:, :, t * P : (t + 1) * P, :]
-            nc.scalar.copy(out=dst, in_=b[:].rearrange("p (k u m) -> p k m u", k=2, u=2))
+        def e_out(i, eng="s"):
+            dst = e_grp[i][:].rearrange("p n t -> p (n t)").bitcast(F32)
+            copy(
+                eng,
+                dst.rearrange("p (k m u) -> p k m u", k=2, u=2),
+                banks["e", i][:].rearrange("p (k u m) -> p k m u", k=2, u=2),
+            )
 
-        def e_quant(g):
-            for k in range(2):
-                nc.vector.quantize_mx(
-                    out=e_q[g][:, k, :].bitcast(FP8X4),
-                    scales=e_s[g][:, k, :],
-                    in_=e_grp[g][:, k, :, :].rearrange("p n t -> p (n t)"),
-                )
+        def e_quant(i):
+            quant(e_q[i], e_s[i], e_grp[i])
 
-        def f_mm(c, g, b):
-            t_ = bank()
-            banks["f", c, g, b] = t_
+        def f_mm(c, g, b, tag="rb"):
+            acc = bank(tag)
+            banks["f", c, g, b] = acc
             cols = slice(b * P, (b + 1) * P)
             for t in range(4):
                 st = slice(t * P, (t + 1) * P)
                 nc.tensor.matmul_mx(
-                    out=t_[:, st],
+                    out=acc[:, st],
                     lhsT=h_q[g][:, st].bitcast(FP8X4),
                     lhsT_scale=h_s[g][:, st],
                     rhs=cs_q[c][:, cols].bitcast(FP8X4),
@@ -250,47 +202,47 @@ def tile_isar_split_real_image_s11_kernel(
                     stop=True,
                 )
 
-        def f_out(c, g, b, eng):
+        def f_out(c, g, b, eng="s"):
             if (c, g) not in f_grp:
-                f_new = work.tile([P, W512, 4], BF16, name="f_grp", bufs=6, align_bytes=64)
+                f_new = work.tile([P, W512, 4], BF16, name="f_grp", align_bytes=64)
                 f_grp[c, g] = f_new
-            dst = f_grp[c, g][:, b * P : (b + 1) * P, :]
-            src = banks["f", c, g, b][:].rearrange("p (t n) -> p n t", t=4)
-            if eng == "v":
-                nc.vector.tensor_copy(out=dst, in_=src)
-            else:
-                nc.scalar.copy(out=dst, in_=src)
+            copy(eng, f_grp[c, g][:, b * P : (b + 1) * P, :], banks["f", c, g, b][:].rearrange("p (t n) -> p n t", t=4))
+
+        def f_bank(c, g, b, eng="s", tag="rb"):
+            f_mm(c, g, b, tag)
+            f_out(c, g, b, eng)
 
         def f_quant(c, g):
-            nc.vector.quantize_mx(
-                out=f_q[c][g][:].bitcast(FP8X4), scales=f_s[c][g][:], in_=f_grp[c, g][:].rearrange("p n t -> p (n t)")
-            )
+            quant(f_q[c][g], f_s[c][g], f_grp[c, g])
 
-        def f_bank(c, g, b):
-            f_mm(c, g, b)
-            f_out(c, g, b, "v" if (c == 3 and b > 0) or (c == 2 and b == 3) else "s")
+        def z_mm(g, t, rb, tag="zb"):
+            if ("z", g, rb) not in banks:
+                banks["z", g, rb] = bank(tag)
+            half, q = divmod(rb, 4)
+            for k in range(2):
+                st = slice(k * P, (k + 1) * P)
+                nc.tensor.matmul_mx(
+                    out=banks["z", g, rb][:, t * P : (t + 1) * P],
+                    lhsT=e_q[4 * g + t][:, st].bitcast(FP8X4),
+                    lhsT_scale=e_s[4 * g + t][:, st],
+                    rhs=w_q[half][:, k, 2 * q * P : 2 * (q + 1) * P].bitcast(FP4X4),
+                    rhs_scale=w_s[:, k, rb * P : (rb + 1) * P],
+                    start=(k == 0),
+                    stop=(k == 1),
+                )
 
-        def z_mm(g, rb):
-            t_ = bank()
-            banks["z", g, rb] = t_
-            cols = slice(rb * P, (rb + 1) * P)
+        def z_slice(g, t, half):
+            for q in range(4):
+                z_mm(g, t, 4 * half + q)
+
+        def z_bank(g, rb, tag="zb"):
             for t in range(4):
-                st = slice(t * P, (t + 1) * P)
-                for k in range(2):
-                    nc.tensor.matmul_mx(
-                        out=t_[:, st],
-                        lhsT=e_q[g][:, k, st].bitcast(FP8X4),
-                        lhsT_scale=e_s[g][:, k, st],
-                        rhs=w_q[:, k, 2 * rb * P : 2 * (rb + 1) * P].bitcast(FP4X4),
-                        rhs_scale=w_s[:, k, cols],
-                        start=(k == 0),
-                        stop=(k == 1),
-                    )
+                z_mm(g, t, rb, tag)
 
         def z_out(g, rb):
             half, q = divmod(rb, 4)
             if (g, half) not in z_grp:
-                z_new = work.tile([P, W512, 4], BF16, name="z_grp", align_bytes=64)
+                z_new = work.tile([P, W512, 4], BF16, name="z_grp", bufs=3, align_bytes=64)
                 z_grp[g, half] = z_new
             nc.vector.tensor_tensor(
                 out=z_grp[g, half][:, q * P : (q + 1) * P, :],
@@ -300,101 +252,129 @@ def tile_isar_split_real_image_s11_kernel(
             )
 
         def z_quant(g, half):
-            nc.vector.quantize_mx(
-                out=z_q[g][half][:].bitcast(FP8X4),
-                scales=z_s[g][half][:],
-                in_=z_grp[g, half][:].rearrange("p n t -> p (n t)"),
-            )
+            quant(z_q[g][half], z_s[g][half], z_grp[g, half])
 
-        def y_unit(c, j, half, pieces=1):
-            width = W512 // pieces
+        def y_mm(c, j, at, width, *tags):
+            half, first = divmod(at, W512)
+            rc = slice(first, first + width)
+            for part in range(2):
+                b = bank(tags[part])
+                cols = slice((2 * part + j) * P, (2 * part + j + 1) * P)
+                for g in range(2):
+                    nc.tensor.matmul_mx(
+                        out=b[:, 0:width],
+                        lhsT=f_q[c][g][:, cols].bitcast(FP8X4),
+                        lhsT_scale=f_s[c][g][:, cols],
+                        rhs=z_q[g][half][:, rc].bitcast(FP8X4),
+                        rhs_scale=z_s[g][half][:, rc],
+                        start=(g == 0),
+                        stop=(g == 1),
+                    )
+                s = outs.tile([P, W512], F32, name="sq%d" % part, align_bytes=64)
+                nc.scalar.activation(out=s[:, 0:width], in_=b[:, 0:width], func=ACT.Square)
+                squares[c, j, at, part] = s
+
+        def y_sum(c, j, at, width):
             rows = out[c * 256 : (c + 1) * 256, :].rearrange("(p j) r -> p j r", j=2)
-            for i in range(pieces):
-                rc = slice(i * width, (i + 1) * width)
-                sq = []
-                for part in range(2):
-                    b = bank()
-                    cols = slice((2 * part + j) * P, (2 * part + j + 1) * P)
-                    for g in range(2):
-                        nc.tensor.matmul_mx(
-                            out=b[:, 0:width],
-                            lhsT=f_q[c][g][:, cols].bitcast(FP8X4),
-                            lhsT_scale=f_s[c][g][:, cols],
-                            rhs=z_q[g][half][:, rc].bitcast(FP8X4),
-                            rhs_scale=z_s[g][half][:, rc],
-                            start=(g == 0),
-                            stop=(g == 1),
-                        )
-                    s = outs.tile([P, W512], F32, name="sq%d" % part, align_bytes=64)
-                    nc.scalar.activation(out=s[:, 0:width], in_=b[:, 0:width], func=ACT.Square)
-                    sq.append(s)
-                res = outs.tile([P, W512], F32, name="res", align_bytes=64)
-                nc.vector.tensor_tensor(out=res[:, 0:width], in0=sq[0][:, 0:width], in1=sq[1][:, 0:width], op=ALU.add)
-                at = half * W512 + i * width
-                nc.sync.dma_start(out=rows[:, j, at : at + width], in_=res[:, 0:width])
+            res = outs.tile([P, W512], F32, name="res", bufs=6, align_bytes=64)
+            nc.vector.tensor_tensor(
+                out=res[:, 0:width],
+                in0=squares[c, j, at, 0][:, 0:width],
+                in1=squares[c, j, at, 1][:, 0:width],
+                op=ALU.add,
+            )
+            nc.sync.dma_start(out=rows[:, j, at : at + width], in_=res[:, 0:width])
 
-        scale_spread()
-        for i in range(8):
+        ctx.enter_context(tc.manual_schedule())
+        make_identity(nc, ident[:])
+        nc.vector.memset(w_s[:].bitcast(I32), 0)
+        nc.scalar.dma_start(out=taper_bf[:], in_=taper.rearrange("(g p t) -> p g t", p=P, t=4))
+        nc.sync.dma_start(out=scale_p8[:], in_=echo_scale.rearrange("o (a p c) -> p (o a) c", a=2, c=4))
+        load_cs(0, 0)
+        load_e(0)
+        load_cs(0, 1)
+        load_cs(1, 0)
+        load_e(1)
+        load_cs(1, 1)
+        load_cs(2, 0)
+        load_e(2)
+        load_h(0)
+        load_cs(2, 1)
+        load_cs(3, 0)
+        load_cs(3, 1)
+        load_w(0)
+        load_ws()
+        load_e(3)
+        load_h(1)
+        load_w(1)
+        nc.scalar.activation(out=taper_f[:], in_=taper_bf[:], func=ACT.Copy)
+        scale_spread(0, "v")
+        scale_spread(1, "s")
+        e_scale(0, W512)
+        cs_part(0, 0)
+        cs_part(0, 1)
+        cs_part(1, 0)
+        for i in range(1, 6):
             e_scale(i)
-        nc.vector.tensor_copy(out=taper_f[:], in_=taper_bf[:])
-
-        def e_pair(i):
-            for n in (i, i + 1):
-                e_turn(n)
-            for n in (i, i + 1):
-                e_out(n)
-
-        c_turn(0)
-        c_out(0)
-        for i in range(2):
-            h_pass(0, (i,))
-            h_out(0, (i,))
-            e_turn(i)
-            e_out(i)
-        e_pair(2)
-        c_turn(1)
-        e_pair(4)
-        c_out(1)
-        h_pass(1)
-        h_out(1)
-        e_pair(6)
+            e_part(i - 1)
+            if i == 3:
+                h_weave(0, "s", slice(0, 2))
+            cs_part(*divmod(i + 2, 2))
+        h_weave(0, "v", slice(2, 4))
         c_quant(0)
         h_quant(0)
-        c_turn(2)
-        c_out(2)
-        e_quant(0)
+        e_part(5)
+        for i in range(4):
+            e_quant(i)
+        e_scale(6)
+        e_scale(7)
+        for q in range(4):
+            f_bank(0, 0, q)
+        h_weave(1, "s")
+        for q in range(4):
+            z_bank(0, q)
+            z_out(0, q)
+        e_part(6)
+        e_part(7)
+        c_quant(1)
+        e_quant(4)
+        e_quant(5)
         h_quant(1)
-        e_quant(1)
-
-        z_list = [(g, rb) for half in range(2) for g in range(2) for rb in range(4 * half, 4 * half + 4)]
-        f_list = [(c, g, b) for c in range(CH) for g in range(2) for b in range(4)]
-        f_run = (4, 2, 2, 3, 3, 3, 3, 4)
-        after = {
-            1: (lambda: c_quant(1), lambda: c_quant(2), lambda: f_quant(0, 0)),
-            2: (lambda: c_turn(3), lambda: c_out(3), lambda: z_quant(0, 0)),
-            3: (lambda: f_quant(0, 1),),
-            4: (lambda: z_quant(1, 0), lambda: c_quant(3)),
-            5: (lambda: f_quant(1, 0),),
-            6: (lambda: z_quant(0, 1), lambda: f_quant(1, 1)),
-        }
-        for s in range(8):
-            for n in range(f_run[s]):
-                f_bank(*f_list[0])
-                f_list = f_list[1:]
-            for z in z_list[2 * s : 2 * s + 2]:
-                z_mm(*z)
-                z_out(*z)
-            for step in after.get(s, ()):
-                step()
+        z_quant(0, 0)
+        for q in range(4):
+            z_bank(0, 4 + q)
+            f_bank(1, 0, q)
+            z_out(0, 4 + q)
+            if q == 1:
+                e_quant(6)
+                e_quant(7)
+        f_quant(0, 0)
+        c_quant(2)
+        for q in range(4):
+            f_bank(0, 1, q)
+            z_bank(1, q)
+            z_out(1, q)
+        z_quant(0, 1)
+        f_quant(1, 0)
+        z_quant(1, 0)
+        f_quant(0, 1)
+        for q in range(4):
+            f_bank(1, 1, q)
+            z_bank(1, 4 + q)
+        units = [(c, j, W512 * half, W512) for c, half in ((0, 0), (1, 0), (0, 1), (1, 1), (2, 0), (2, 1), (3, 0), (3, 1)) for j in range(2)]
+        units = units[:-1] + [(3, 1, 512, 256), (3, 1, 768, 128), (3, 1, 896, 128)]
+        rest = [(c, g, b) for c in (2, 3) for g in range(2) for b in range(4)]
+        for q in range(4):
+            z_out(1, 4 + q)
+        f_quant(1, 1)
+        c_quant(3)
         z_quant(1, 1)
-        f_quant(2, 0)
-        f_quant(2, 1)
-        y_list = [(c, j, half) for c, half in ((0, 0), (1, 0), (0, 1), (1, 1), (2, 0), (2, 1), (3, 0), (3, 1)) for j in range(2)]
-        for n, y in enumerate(y_list):
-            y_unit(*y, pieces=2 if n == len(y_list) - 1 else 1)
-            if n >= 1 and f_list:
-                c, g, b = f_list[0]
-                f_bank(c, g, b)
-                f_list = f_list[1:]
-                if b == 3:
-                    f_quant(c, g)
+        for n, y in enumerate(units):
+            y_mm(*y, "rb", "rb")
+            if n >= 1:
+                y_sum(*units[n - 1])
+            for k, fb in enumerate(rest[2 * n : 2 * n + 2]):
+                f_bank(*fb, "s" if k == 0 else "v")
+            if n >= 2 and n % 2 == 0 and 2 * n - 4 < len(rest):
+                f_quant(*rest[2 * n - 4][:2])
+        y_sum(*units[-1])

@@ -59,6 +59,7 @@ def tile_isar_split_real_image_s11_kernel(
         e_sc = {}
         f_grp = {}
         z_grp = {}
+        z_rows = {}
         banks = {}
         squares = {}
 
@@ -215,40 +216,35 @@ def tile_isar_split_real_image_s11_kernel(
         def f_quant(c, g):
             quant(f_q[c][g], f_s[c][g], f_grp[c, g])
 
-        def z_mm(g, t, rb, tag="zb"):
-            if ("z", g, rb) not in banks:
-                banks["z", g, rb] = bank(tag)
-            half, q = divmod(rb, 4)
+        def z_wide(g, t, half, eng="s"):
+            acc = bank("rb")
             for k in range(2):
                 st = slice(k * P, (k + 1) * P)
                 nc.tensor.matmul_mx(
-                    out=banks["z", g, rb][:, t * P : (t + 1) * P],
+                    out=acc[:],
                     lhsT=e_q[4 * g + t][:, st].bitcast(FP8X4),
                     lhsT_scale=e_s[4 * g + t][:, st],
-                    rhs=w_q[half][:, k, 2 * q * P : 2 * (q + 1) * P].bitcast(FP4X4),
-                    rhs_scale=w_s[:, k, rb * P : (rb + 1) * P],
+                    rhs=w_q[half][:, k, :].bitcast(FP4X4),
+                    rhs_scale=w_s[:, k, half * W512 : (half + 1) * W512],
                     start=(k == 0),
                     stop=(k == 1),
                 )
+            if (g, half) not in z_rows:
+                rows_new = work.tile([P, 4, W512], BF16, name="z_rows", bufs=2, align_bytes=64)
+                z_rows[g, half] = rows_new
+            gain = taper_f[:, g, t : t + 1]
+            if eng == "v":
+                nc.vector.tensor_scalar(out=z_rows[g, half][:, t, :], in0=acc[:], scalar1=gain, scalar2=None, op0=ALU.mult)
+            else:
+                nc.scalar.activation(out=z_rows[g, half][:, t, :], in_=acc[:], func=ACT.Copy, scale=gain)
 
-        def z_slice(g, t, half):
-            for q in range(4):
-                z_mm(g, t, 4 * half + q)
-
-        def z_bank(g, rb, tag="zb"):
-            for t in range(4):
-                z_mm(g, t, rb, tag)
-
-        def z_out(g, rb):
-            half, q = divmod(rb, 4)
-            if (g, half) not in z_grp:
-                z_new = work.tile([P, W512, 4], BF16, name="z_grp", bufs=3, align_bytes=64)
-                z_grp[g, half] = z_new
-            nc.vector.tensor_tensor(
-                out=z_grp[g, half][:, q * P : (q + 1) * P, :],
-                in0=banks["z", g, rb][:].rearrange("p (t n) -> p n t", t=4),
-                in1=taper_f[:, g : g + 1, :].to_broadcast([P, P, 4]),
-                op=ALU.mult,
+        def z_weave(g, half, eng="v"):
+            z_new = work.tile([P, W512, 4], BF16, name="z_grp", bufs=2, align_bytes=64)
+            z_grp[g, half] = z_new
+            copy(
+                eng,
+                z_new[:].rearrange("p (c i) t -> p c t i", i=4),
+                z_rows[g, half][:].rearrange("p t (c i) -> p c t i", i=4),
             )
 
         def z_quant(g, half):
@@ -274,10 +270,10 @@ def tile_isar_split_real_image_s11_kernel(
                 nc.scalar.activation(out=s[:, 0:width], in_=b[:, 0:width], func=ACT.Square)
                 squares[c, j, at, part] = s
 
-        def y_sum(c, j, at, width):
+        def y_sum(c, j, at, width, eng="v"):
             rows = out[c * 256 : (c + 1) * 256, :].rearrange("(p j) r -> p j r", j=2)
             res = outs.tile([P, W512], F32, name="res", bufs=6, align_bytes=64)
-            nc.vector.tensor_tensor(
+            (nc.vector if eng == "v" else nc.gpsimd).tensor_tensor(
                 out=res[:, 0:width],
                 in0=squares[c, j, at, 0][:, 0:width],
                 in1=squares[c, j, at, 1][:, 0:width],
@@ -330,43 +326,42 @@ def tile_isar_split_real_image_s11_kernel(
         e_scale(7)
         for q in range(4):
             f_bank(0, 0, q)
-        h_weave(1, "s")
-        for q in range(4):
-            z_bank(0, q)
-            z_out(0, q)
+        for t in range(4):
+            z_wide(0, t, 0)
+        c_quant(1)
+        h_weave(1, "v")
         e_part(6)
         e_part(7)
-        c_quant(1)
         e_quant(4)
         e_quant(5)
         h_quant(1)
-        z_quant(0, 0)
+        z_weave(0, 0)
         for q in range(4):
-            z_bank(0, 4 + q)
-            f_bank(1, 0, q)
-            z_out(0, 4 + q)
+            z_wide(0, q, 1)
+            f_bank(1, 0, q, "v" if q < 2 else "s")
             if q == 1:
                 e_quant(6)
                 e_quant(7)
+                z_quant(0, 0)
         f_quant(0, 0)
+        for q in range(4):
+            z_wide(1, q, 0)
+            f_bank(0, 1, q, "v" if q < 1 else "s")
+        z_weave(0, 1)
         c_quant(2)
-        for q in range(4):
-            f_bank(0, 1, q)
-            z_bank(1, q)
-            z_out(1, q)
-        z_quant(0, 1)
         f_quant(1, 0)
-        z_quant(1, 0)
+        z_weave(1, 0)
         f_quant(0, 1)
+        z_quant(1, 0)
         for q in range(4):
-            f_bank(1, 1, q)
-            z_bank(1, 4 + q)
+            z_wide(1, q, 1)
+            f_bank(1, 1, q, "v" if q < 1 else "s")
+        z_quant(0, 1)
         units = [(c, j, W512 * half, W512) for c, half in ((0, 0), (1, 0), (0, 1), (1, 1), (2, 0), (2, 1), (3, 0), (3, 1)) for j in range(2)]
         units = units[:-1] + [(3, 1, 512, 256), (3, 1, 768, 128), (3, 1, 896, 128)]
         rest = [(c, g, b) for c in (2, 3) for g in range(2) for b in range(4)]
-        for q in range(4):
-            z_out(1, 4 + q)
         f_quant(1, 1)
+        z_weave(1, 1)
         c_quant(3)
         z_quant(1, 1)
         for n, y in enumerate(units):
@@ -374,7 +369,7 @@ def tile_isar_split_real_image_s11_kernel(
             if n >= 1:
                 y_sum(*units[n - 1])
             for k, fb in enumerate(rest[2 * n : 2 * n + 2]):
-                f_bank(*fb, "s" if k == 0 else "v")
+                f_bank(*fb, "s" if k == 0 and n < 4 else "v")
             if n >= 2 and n % 2 == 0 and 2 * n - 4 < len(rest):
                 f_quant(*rest[2 * n - 4][:2])
         y_sum(*units[-1])

@@ -95,9 +95,6 @@ def tile_isar_split_real_image_s11_kernel(
                     in_=w_scales[:, 4 * q : 4 * q + 4, :].bitcast(I32).rearrange("g q n -> q g n"),
                 )
 
-        def load_taper():
-            nc.sync.dma_start(out=taper_bf[:], in_=taper.rearrange("(g p t) -> p g t", p=P, t=4))
-
         def copy(eng, dst, src):
             if eng == "v":
                 nc.vector.tensor_copy(out=dst, in_=src)
@@ -230,7 +227,7 @@ def tile_isar_split_real_image_s11_kernel(
                     stop=(k == 1),
                 )
             if (g, half) not in z_rows:
-                rows_new = work.tile([P, 4, W512], BF16, name="z_rows", bufs=2, align_bytes=64)
+                rows_new = work.tile([P, 4, W512], BF16, name="z_rows", bufs=3, align_bytes=64)
                 z_rows[g, half] = rows_new
             gain = taper_f[:, g, t : t + 1]
             if eng == "v":
@@ -284,92 +281,108 @@ def tile_isar_split_real_image_s11_kernel(
         ctx.enter_context(tc.manual_schedule())
         make_identity(nc, ident[:])
         nc.vector.memset(w_s[:].bitcast(I32), 0)
-        nc.scalar.dma_start(out=taper_bf[:], in_=taper.rearrange("(g p t) -> p g t", p=P, t=4))
         nc.sync.dma_start(out=scale_p8[:], in_=echo_scale.rearrange("o (a p c) -> p (o a) c", a=2, c=4))
-        load_cs(0, 0)
+        nc.scalar.dma_start(out=taper_bf[:], in_=taper.rearrange("(g p t) -> p g t", p=P, t=4))
         load_e(0)
-        load_cs(0, 1)
-        load_cs(1, 0)
+        load_cs(0, 0)
         load_e(1)
-        load_cs(1, 1)
-        load_cs(2, 0)
-        load_e(2)
+        load_cs(0, 1)
         load_h(0)
-        load_cs(2, 1)
-        load_cs(3, 0)
-        load_cs(3, 1)
+        load_e(2)
+        load_cs(1, 0)
+        load_cs(1, 1)
         load_w(0)
         load_ws()
         load_e(3)
         load_h(1)
         load_w(1)
+        for c in (2, 3):
+            load_cs(c, 0)
+            load_cs(c, 1)
         nc.scalar.activation(out=taper_f[:], in_=taper_bf[:], func=ACT.Copy)
         scale_spread(0, "v")
         scale_spread(1, "s")
         e_scale(0, W512)
         cs_part(0, 0)
-        cs_part(0, 1)
-        cs_part(1, 0)
-        for i in range(1, 6):
+        for i in range(1, 4):
             e_scale(i)
-            e_part(i - 1)
             if i == 3:
                 h_weave(0, "s", slice(0, 2))
-            cs_part(*divmod(i + 2, 2))
+            e_part(i - 1)
+            if i == 1:
+                cs_part(0, 1)
         h_weave(0, "v", slice(2, 4))
         c_quant(0)
         h_quant(0)
-        e_part(5)
+        e_part(3)
+        cs_part(1, 0)
+        cs_part(1, 1)
+        e_scale(4)
+        e_scale(5)
         for i in range(4):
             e_quant(i)
+        for q in range(4):
+            f_bank(0, 0, q)
+        e_part(4)
+        e_part(5)
         e_scale(6)
         e_scale(7)
         for q in range(4):
-            f_bank(0, 0, q)
-        for t in range(4):
-            z_wide(0, t, 0)
-        c_quant(1)
+            z_wide(0, q, 0)
         h_weave(1, "v")
         e_part(6)
         e_part(7)
         e_quant(4)
         e_quant(5)
-        h_quant(1)
-        z_weave(0, 0)
+        c_quant(1)
         for q in range(4):
             z_wide(0, q, 1)
-            f_bank(1, 0, q, "v" if q < 2 else "s")
-            if q == 1:
-                e_quant(6)
-                e_quant(7)
-                z_quant(0, 0)
-        f_quant(0, 0)
+        h_quant(1)
+        e_quant(6)
+        e_quant(7)
+        z_weave(0, 0)
+        for q in range(4):
+            f_bank(1, 0, q, "sv"[q // 2])
         for q in range(4):
             z_wide(1, q, 0)
-            f_bank(0, 1, q, "v" if q < 1 else "s")
-        z_weave(0, 1)
-        c_quant(2)
+        z_quant(0, 0)
+        f_quant(0, 0)
         f_quant(1, 0)
+        for q in range(4):
+            f_bank(0, 1, q)
         z_weave(1, 0)
-        f_quant(0, 1)
-        z_quant(1, 0)
+        cs_part(2, 0)
+        cs_part(2, 1)
+        for q in range(4):
+            f_bank(1, 1, q, "v")
+            if q == 0:
+                z_quant(1, 0)
+                f_quant(0, 1)
         for q in range(4):
             z_wide(1, q, 1)
-            f_bank(1, 1, q, "v" if q < 1 else "s")
+        z_weave(0, 1)
+        f_quant(1, 1)
+        c_quant(2)
         z_quant(0, 1)
         units = [(c, j, W512 * half, W512) for c, half in ((0, 0), (1, 0), (0, 1), (1, 1), (2, 0), (2, 1), (3, 0), (3, 1)) for j in range(2)]
         units = units[:-1] + [(3, 1, 512, 256), (3, 1, 768, 128), (3, 1, 896, 128)]
         rest = [(c, g, b) for c in (2, 3) for g in range(2) for b in range(4)]
-        f_quant(1, 1)
-        z_weave(1, 1)
-        c_quant(3)
-        z_quant(1, 1)
         for n, y in enumerate(units):
             y_mm(*y, "rb", "rb")
+            if n == 0:
+                z_weave(1, 1)
+            if n == 1:
+                z_quant(1, 1)
+                for part in range(2):
+                    c_turn(3, part)
+                    c_out(3, part)
             if n >= 1:
                 y_sum(*units[n - 1])
-            for k, fb in enumerate(rest[2 * n : 2 * n + 2]):
-                f_bank(*fb, "s" if k == 0 and n < 4 else "v")
-            if n >= 2 and n % 2 == 0 and 2 * n - 4 < len(rest):
-                f_quant(*rest[2 * n - 4][:2])
+            if n == 2:
+                c_quant(3)
+            if 2 <= n < 10:
+                for k, fb in enumerate(rest[2 * n - 4 : 2 * n - 2]):
+                    f_bank(*fb, "sv"[k])
+            if n in (4, 6, 8, 10):
+                f_quant(*rest[2 * n - 8][:2])
         y_sum(*units[-1])

@@ -17,8 +17,9 @@ ACT = mybir.ActivationFunctionType
 ALU = mybir.AluOpType
 
 P = 128
-CH = 4
+STRIPS = 8
 W512 = 512
+E_LOADS = ((0, 1), (1, 2), (3, 1), (4, 2), (6, 2))
 
 FLOPS = 2 * (2 * D * J * T + T * L * R + 2 * D * T * R)
 
@@ -35,41 +36,49 @@ def tile_isar_split_real_image_s11_kernel(
 
         ident = keep.tile([P, P], F32, name="ident", align_bytes=64)
         scale_p8 = keep.tile([P, 2, 4], F32, name="scale_p8")
-        scale_bc = keep.tile([P, L], F32, name="scale_bc", align_bytes=64)
+        ones = keep.tile([P, 1], F32, name="ones")
         taper_bf = keep.tile([P, 2, 4], BF16, name="taper_bf")
         taper_f = keep.tile([P, 2, 4], F32, name="taper_f")
-        cs_raw = [[keep.tile([P, 2, J], BF16, name="cs_raw%d%d" % (c, a), align_bytes=64) for a in range(2)] for c in range(CH)]
-        cs_grp = [keep.tile([P, W512, 4], BF16, name="cs_grp%d" % c, align_bytes=64) for c in range(CH)]
-        cs_q = [keep.tile([P, W512], U32, name="cs_q%d" % c, align_bytes=64) for c in range(CH)]
-        cs_s = [keep.tile([P, W512], U8, name="cs_s%d" % c, align_bytes=64) for c in range(CH)]
+        cs_first = [keep.tile([P, 2, J], BF16, name="cs_first%d" % j, align_bytes=64) for j in range(2)]
+        cs_pair = [keep.tile([P, 2, 2, J], BF16, name="cs_pair%d" % c, align_bytes=64) for c in range(1, 4)]
+        cs_raw = [cs_first[0][:], cs_first[1][:]] + [cs_pair[c][:, :, j, :] for c in range(3) for j in range(2)]
+        cs_grp = [keep.tile([P, 2 * P, 4], BF16, name="cs_grp%d" % s, align_bytes=64) for s in range(STRIPS)]
+        cs_q = [keep.tile([P, 2 * P], U32, name="cs_q%d" % s, align_bytes=64) for s in range(STRIPS)]
+        cs_s = [keep.tile([P, 2 * P], U8, name="cs_s%d" % s, align_bytes=64) for s in range(STRIPS)]
         h_raw = [keep.tile([P, 4, W512], BF16, name="h_raw%d" % g, align_bytes=64) for g in range(2)]
         h_grp = [keep.tile([P, W512, 4], BF16, name="h_grp%d" % g, align_bytes=64) for g in range(2)]
         h_q = [keep.tile([P, W512], U32, name="h_q%d" % g, align_bytes=64) for g in range(2)]
         h_s = [keep.tile([P, W512], U8, name="h_s%d" % g, align_bytes=64) for g in range(2)]
-        e_bytes = [keep.tile([P, 2, L], U8, name="e_bytes%d" % n, align_bytes=64) for n in range(4)]
+        e_bytes = [keep.tile([P, n, L], U8, name="e_bytes%d" % i, align_bytes=64) for i, n in E_LOADS]
+        e_in = [e_bytes[x][:, j, :] for x, (i, n) in enumerate(E_LOADS) for j in range(n)]
         e_grp = [keep.tile([P, 2 * P, 4], BF16, name="e_grp%d" % i, align_bytes=64) for i in range(8)]
         e_q = [keep.tile([P, 2 * P], U32, name="e_q%d" % i, align_bytes=64) for i in range(8)]
         e_s = [keep.tile([P, 2 * P], U8, name="e_s%d" % i, align_bytes=64) for i in range(8)]
         w_q = [keep.tile([P, 2, R], U8, name="w_q%d" % r, align_bytes=64) for r in range(2)]
         w_s = keep.tile([P, 2, R], U8, name="w_s", align_bytes=64)
-        f_q = [[keep.tile([P, W512], U32, name="f_q%d%d" % (c, g), align_bytes=64) for g in range(2)] for c in range(CH)]
-        f_s = [[keep.tile([P, W512], U8, name="f_s%d%d" % (c, g), align_bytes=64) for g in range(2)] for c in range(CH)]
+        f_q = [[keep.tile([P, 2 * P], U32, name="f_q%d%d" % (s, g), align_bytes=64) for g in range(2)] for s in range(STRIPS)]
+        f_s = [[keep.tile([P, 2 * P], U8, name="f_s%d%d" % (s, g), align_bytes=64) for g in range(2)] for s in range(STRIPS)]
         z_q = [[keep.tile([P, W512], U32, name="z_q%d%d" % (g, r), align_bytes=64) for r in range(2)] for g in range(2)]
         z_s = [[keep.tile([P, W512], U8, name="z_s%d%d" % (g, r), align_bytes=64) for r in range(2)] for g in range(2)]
         e_sc = {}
+        sorted_words = {}
         f_grp = {}
         z_grp = {}
         z_rows = {}
         banks = {}
         squares = {}
 
-        def bank(tag):
+        def bank():
             t = psum.tile([P, W512], F32, name="bank")
             return t
 
-        def load_cs(c, part):
-            row = part * D + c * 256
-            nc.sync.dma_start(out=cs_raw[c][part][:], in_=cs[row : row + 256, :].rearrange("(p j) k -> p j k", j=2))
+        def load_strip(j):
+            rows = cs.rearrange("(a c p j) k -> c j p a k", a=2, p=P, j=2)
+            nc.sync.dma_start(out=cs_first[j][:], in_=rows[0, j])
+
+        def load_pair(c):
+            rows = cs.rearrange("(a c p j) k -> c p a (j k)", a=2, p=P, j=2)
+            nc.sync.dma_start(out=cs_pair[c - 1][:].rearrange("p a j k -> p a (j k)"), in_=rows[c])
 
         def load_h(g):
             nc.sync.dma_start(
@@ -77,10 +86,11 @@ def tile_isar_split_real_image_s11_kernel(
                 in_=h.rearrange("(p j) w -> p j w", j=4)[:, :, g * W512 : (g + 1) * W512],
             )
 
-        def load_e(n):
-            g, half = divmod(n, 2)
+        def load_e(x):
+            i, n = E_LOADS[x]
+            g, t = divmod(i, 4)
             rows = echo_bytes[g * W512 : (g + 1) * W512, :].rearrange("(m t) k -> m t k", t=4)
-            nc.sync.dma_start(out=e_bytes[n][:], in_=rows[:, 2 * half : 2 * half + 2, :])
+            nc.sync.dma_start(out=e_bytes[x][:], in_=rows[:, t : t + n, :])
 
         def load_w(r):
             nc.sync.dma_start(
@@ -89,11 +99,20 @@ def tile_isar_split_real_image_s11_kernel(
             )
 
         def load_ws():
-            for q in range(4):
+            for q in (0, 2, 1, 3):
                 nc.sync.dma_start(
                     out=w_s[32 * q : 32 * q + 4, :, :].bitcast(I32),
                     in_=w_scales[:, 4 * q : 4 * q + 4, :].bitcast(I32).rearrange("g q n -> q g n"),
                 )
+
+        def load_scale():
+            nc.sync.dma_start(out=scale_p8[:], in_=echo_scale.rearrange("o (a p c) -> p (o a) c", a=2, c=4))
+
+        def load_taper():
+            nc.sync.dma_start(out=taper_bf[:], in_=taper.rearrange("(g p t) -> p g t", p=P, t=4))
+
+        def taper_widen():
+            nc.scalar.activation(out=taper_f[:], in_=taper_bf[:], func=ACT.Copy)
 
         def copy(eng, dst, src):
             if eng == "v":
@@ -101,38 +120,33 @@ def tile_isar_split_real_image_s11_kernel(
             else:
                 nc.scalar.copy(out=dst, in_=src)
 
-        def scale_spread(a, eng):
-            b = bank("rb")
-            for c in range(4):
-                nc.tensor.transpose(
-                    b[:, c * P : (c + 1) * P], scale_p8[:, a, c : c + 1].to_broadcast([P, P]), ident[:]
-                )
-            dst = scale_bc[:, a * W512 : (a + 1) * W512].rearrange("p (n c) -> p n c", c=4)
-            copy(eng, dst, b[:].rearrange("p (c n) -> p n c", c=4))
-
-        def c_turn(c, part):
-            b = bank("rb")
-            banks["c", c, part] = b
-            for j in range(2):
-                words = cs_raw[c][part][:, j, :].bitcast(F32)
+        def c_turn(s):
+            b = bank()
+            banks["c", s] = b
+            for part in range(2):
+                words = cs_raw[s][:, part, :].bitcast(F32)
                 for u in range(2):
                     nc.tensor.transpose(
-                        b[:, (2 * j + u) * P : (2 * j + u + 1) * P], words[:, u : 2 * P : 2], ident[:]
+                        b[:, (2 * part + u) * P : (2 * part + u + 1) * P], words[:, u : 2 * P : 2], ident[:]
                     )
 
-        def c_out(c, part, eng="s"):
-            dst = cs_grp[c][:, 256 * part : 256 * part + 256, :].rearrange("p n t -> p (n t)").bitcast(F32)
+        def c_out(s, eng="s"):
+            dst = cs_grp[s][:].rearrange("p n t -> p (n t)").bitcast(F32)
             copy(
                 eng,
-                dst.rearrange("p (j m u) -> p j m u", j=2, u=2),
-                banks["c", c, part][:].rearrange("p (j u m) -> p j m u", j=2, u=2),
+                dst.rearrange("p (a m u) -> p a m u", a=2, u=2),
+                banks["c", s][:].rearrange("p (a u m) -> p a m u", a=2, u=2),
             )
+
+        def cs_part(s, eng="s"):
+            c_turn(s)
+            c_out(s, eng)
 
         def quant(q, s, grp):
             nc.vector.quantize_mx(out=q[:].bitcast(FP8X4), scales=s[:], in_=grp[:].rearrange("p n t -> p (n t)"))
 
-        def c_quant(c):
-            quant(cs_q[c], cs_s[c], cs_grp[c])
+        def c_quant(s):
+            quant(cs_q[s], cs_s[s], cs_grp[s])
 
         def h_weave(g, eng, ts=slice(0, 4)):
             copy(
@@ -141,80 +155,68 @@ def tile_isar_split_real_image_s11_kernel(
                 h_raw[g][:].rearrange("p j (m t) -> p t m j", t=4)[:, ts],
             )
 
-        def cs_part(c, part):
-            c_turn(c, part)
-            c_out(c, part)
-
-        def e_part(i):
-            e_turn(i)
-            e_out(i)
-
         def h_quant(g):
             quant(h_q[g], h_s[g], h_grp[g])
 
-        def e_scale(i, width=L):
-            s = work.tile([P, L], BF16, name="e_sc", align_bytes=64)
+        def e_wide(i, eng="v"):
+            s = work.tile([P, L], BF16, name="e_sc", bufs=8, align_bytes=64)
             e_sc[i] = s
-            for k in range(0, L, width):
-                ks = slice(k, k + width)
-                nc.vector.tensor_tensor(
-                    out=s[:, ks], in0=e_bytes[i // 2][:, i % 2, ks].bitcast(FP8), in1=scale_bc[:, ks], op=ALU.mult
+            sorted_words[i] = eng == "v"
+            if eng == "v":
+                nc.vector.tensor_scalar(
+                    out=s[:].rearrange("p (u w e) -> p w u e", u=2, e=2),
+                    in0=e_in[i].bitcast(FP8).rearrange("p (w u e) -> p w u e", u=2, e=2),
+                    scalar1=ones[:],
+                    scalar2=None,
+                    op0=ALU.mult,
                 )
+            else:
+                nc.scalar.copy(out=s[:], in_=e_in[i].bitcast(FP8))
 
         def e_turn(i):
-            b = bank("rb")
+            b = bank()
             banks["e", i] = b
             words = e_sc[i][:].bitcast(F32)
-            for k in range(2):
-                for u in range(2):
-                    nc.tensor.transpose(
-                        b[:, (2 * k + u) * P : (2 * k + u + 1) * P],
-                        words[:, 2 * P * k + u : 2 * P * (k + 1) : 2],
-                        ident[:],
-                    )
+            for q in range(4):
+                u, k = divmod(q, 2)
+                src = words[:, q * P : (q + 1) * P] if sorted_words[i] else words[:, 2 * P * k + u : 2 * P * (k + 1) : 2]
+                nc.tensor.transpose(b[:, q * P : (q + 1) * P], src, ident[:])
 
-        def e_out(i, eng="s"):
-            dst = e_grp[i][:].rearrange("p n t -> p (n t)").bitcast(F32)
-            copy(
-                eng,
-                dst.rearrange("p (k m u) -> p k m u", k=2, u=2),
-                banks["e", i][:].rearrange("p (k u m) -> p k m u", k=2, u=2),
+        def e_out(i):
+            nc.vector.tensor_tensor(
+                out=e_grp[i][:].rearrange("p (k m) (u e) -> p k m u e", k=2, u=2),
+                in0=banks["e", i][:].bitcast(BF16).rearrange("p (u k m e) -> p k m u e", u=2, k=2, e=2),
+                in1=scale_p8[:].rearrange("p k (u e) -> p k u e", u=2).unsqueeze(2).to_broadcast([P, 2, P, 2, 2]),
+                op=ALU.mult,
             )
 
         def e_quant(i):
             quant(e_q[i], e_s[i], e_grp[i])
 
-        def f_mm(c, g, b, tag="rb"):
-            acc = bank(tag)
-            banks["f", c, g, b] = acc
-            cols = slice(b * P, (b + 1) * P)
+        def f_bank(s, g, part, eng="s"):
+            acc = bank()
+            cols = slice(part * P, (part + 1) * P)
             for t in range(4):
                 st = slice(t * P, (t + 1) * P)
                 nc.tensor.matmul_mx(
                     out=acc[:, st],
                     lhsT=h_q[g][:, st].bitcast(FP8X4),
                     lhsT_scale=h_s[g][:, st],
-                    rhs=cs_q[c][:, cols].bitcast(FP8X4),
-                    rhs_scale=cs_s[c][:, cols],
+                    rhs=cs_q[s][:, cols].bitcast(FP8X4),
+                    rhs_scale=cs_s[s][:, cols],
                     start=True,
                     stop=True,
                 )
+            if (s, g) not in f_grp:
+                f_new = work.tile([P, 2 * P, 4], BF16, name="f_grp", bufs=8, align_bytes=64)
+                f_grp[s, g] = f_new
+            copy(eng, f_grp[s, g][:, cols, :], acc[:].rearrange("p (t n) -> p n t", t=4))
 
-        def f_out(c, g, b, eng="s"):
-            if (c, g) not in f_grp:
-                f_new = work.tile([P, W512, 4], BF16, name="f_grp", align_bytes=64)
-                f_grp[c, g] = f_new
-            copy(eng, f_grp[c, g][:, b * P : (b + 1) * P, :], banks["f", c, g, b][:].rearrange("p (t n) -> p n t", t=4))
-
-        def f_bank(c, g, b, eng="s", tag="rb"):
-            f_mm(c, g, b, tag)
-            f_out(c, g, b, eng)
-
-        def f_quant(c, g):
-            quant(f_q[c][g], f_s[c][g], f_grp[c, g])
+        def f_quant(s, g):
+            quant(f_q[s][g], f_s[s][g], f_grp[s, g])
 
         def z_wide(g, t, half, eng="s"):
-            acc = bank("rb")
+            acc = bank()
             for k in range(2):
                 st = slice(k * P, (k + 1) * P)
                 nc.tensor.matmul_mx(
@@ -227,7 +229,7 @@ def tile_isar_split_real_image_s11_kernel(
                     stop=(k == 1),
                 )
             if (g, half) not in z_rows:
-                rows_new = work.tile([P, 4, W512], BF16, name="z_rows", bufs=3, align_bytes=64)
+                rows_new = work.tile([P, 4, W512], BF16, name="z_rows", align_bytes=64)
                 z_rows[g, half] = rows_new
             gain = taper_f[:, g, t : t + 1]
             if eng == "v":
@@ -247,142 +249,157 @@ def tile_isar_split_real_image_s11_kernel(
         def z_quant(g, half):
             quant(z_q[g][half], z_s[g][half], z_grp[g, half])
 
-        def y_mm(c, j, at, width, *tags):
+        def y_mm(s, at, width):
             half, first = divmod(at, W512)
             rc = slice(first, first + width)
             for part in range(2):
-                b = bank(tags[part])
-                cols = slice((2 * part + j) * P, (2 * part + j + 1) * P)
+                b = bank()
+                cols = slice(part * P, (part + 1) * P)
                 for g in range(2):
                     nc.tensor.matmul_mx(
                         out=b[:, 0:width],
-                        lhsT=f_q[c][g][:, cols].bitcast(FP8X4),
-                        lhsT_scale=f_s[c][g][:, cols],
+                        lhsT=f_q[s][g][:, cols].bitcast(FP8X4),
+                        lhsT_scale=f_s[s][g][:, cols],
                         rhs=z_q[g][half][:, rc].bitcast(FP8X4),
                         rhs_scale=z_s[g][half][:, rc],
                         start=(g == 0),
                         stop=(g == 1),
                     )
-                s = outs.tile([P, W512], F32, name="sq%d" % part, align_bytes=64)
-                nc.scalar.activation(out=s[:, 0:width], in_=b[:, 0:width], func=ACT.Square)
-                squares[c, j, at, part] = s
+                sq = outs.tile([P, W512], F32, name="sq%d" % part, bufs=7, align_bytes=64)
+                nc.scalar.activation(out=sq[:, 0:width], in_=b[:, 0:width], func=ACT.Square)
+                squares[s, at, part] = sq
 
-        def y_sum(c, j, at, width, eng="v"):
-            rows = out[c * 256 : (c + 1) * 256, :].rearrange("(p j) r -> p j r", j=2)
+        def y_sum(s, at, width, eng="v"):
+            rows = out.rearrange("(c p j) r -> c j p r", p=P, j=2)[s // 2, s % 2]
             res = outs.tile([P, W512], F32, name="res", bufs=6, align_bytes=64)
             (nc.vector if eng == "v" else nc.gpsimd).tensor_tensor(
                 out=res[:, 0:width],
-                in0=squares[c, j, at, 0][:, 0:width],
-                in1=squares[c, j, at, 1][:, 0:width],
+                in0=squares[s, at, 0][:, 0:width],
+                in1=squares[s, at, 1][:, 0:width],
                 op=ALU.add,
             )
-            nc.sync.dma_start(out=rows[:, j, at : at + width], in_=res[:, 0:width])
+            nc.sync.dma_start(out=rows[:, at : at + width], in_=res[:, 0:width])
 
         ctx.enter_context(tc.manual_schedule())
         make_identity(nc, ident[:])
+        nc.vector.memset(ones[:], 1.0)
         nc.vector.memset(w_s[:].bitcast(I32), 0)
-        nc.sync.dma_start(out=scale_p8[:], in_=echo_scale.rearrange("o (a p c) -> p (o a) c", a=2, c=4))
-        nc.scalar.dma_start(out=taper_bf[:], in_=taper.rearrange("(g p t) -> p g t", p=P, t=4))
-        load_e(0)
-        load_cs(0, 0)
-        load_e(1)
-        load_cs(0, 1)
-        load_h(0)
-        load_e(2)
-        load_cs(1, 0)
-        load_cs(1, 1)
+        for x in range(3):
+            load_e(x)
+        load_scale()
+        load_e(3)
+        load_strip(0)
+        load_e(4)
+        load_strip(1)
+        load_taper()
         load_w(0)
         load_ws()
-        load_e(3)
-        load_h(1)
+        load_h(0)
         load_w(1)
-        for c in (2, 3):
-            load_cs(c, 0)
-            load_cs(c, 1)
-        nc.scalar.activation(out=taper_f[:], in_=taper_bf[:], func=ACT.Copy)
-        scale_spread(0, "v")
-        scale_spread(1, "s")
-        e_scale(0, W512)
-        cs_part(0, 0)
-        for i in range(1, 4):
-            e_scale(i)
-            if i == 3:
-                h_weave(0, "s", slice(0, 2))
-            e_part(i - 1)
-            if i == 1:
-                cs_part(0, 1)
-        h_weave(0, "v", slice(2, 4))
-        c_quant(0)
-        h_quant(0)
-        e_part(3)
-        cs_part(1, 0)
-        cs_part(1, 1)
-        e_scale(4)
-        e_scale(5)
-        for i in range(4):
-            e_quant(i)
-        for q in range(4):
-            f_bank(0, 0, q)
-        e_part(4)
-        e_part(5)
-        e_scale(6)
-        e_scale(7)
-        for q in range(4):
-            z_wide(0, q, 0)
-        h_weave(1, "v")
-        e_part(6)
-        e_part(7)
+        load_pair(1)
+        load_h(1)
+        load_pair(2)
+        load_pair(3)
+        e_wide(0)
+        e_wide(2, "s")
+        e_wide(1)
+        e_wide(3)
+        e_wide(4, "s")
+        e_wide(5, "s")
+        e_wide(6, "s")
+        e_wide(7, "s")
+        taper_widen()
+        for i in (0, 1, 2, 3, 4):
+            e_turn(i)
+        e_out(0)
+        e_out(1)
+        e_quant(0)
+        e_out(2)
+        e_quant(1)
+        cs_part(0)
+        e_turn(5)
+        cs_part(1)
+        e_out(3)
+        e_quant(2)
+        z_wide(0, 0, 0)
+        z_wide(0, 1, 0)
+        e_out(4)
+        e_quant(3)
+        e_turn(6)
+        e_turn(7)
+        h_weave(0, "s", slice(0, 2))
+        e_out(5)
         e_quant(4)
+        z_wide(0, 2, 0)
+        z_wide(0, 0, 1)
+        z_wide(0, 3, 0)
+        h_weave(0, "s", slice(2, 4))
+        z_wide(0, 1, 1)
+        e_out(6)
         e_quant(5)
-        c_quant(1)
-        for q in range(4):
-            z_wide(0, q, 1)
-        h_quant(1)
+        cs_part(2)
+        cs_part(3)
+        e_out(7)
         e_quant(6)
+        c_quant(0)
         e_quant(7)
+        h_quant(0)
+        for t in range(4):
+            z_wide(1, t, 0)
+        h_weave(1, "v")
+        c_quant(1)
+        h_quant(1)
+        z_wide(0, 2, 1)
+        z_wide(0, 3, 1)
         z_weave(0, 0)
-        for q in range(4):
-            f_bank(1, 0, q, "sv"[q // 2])
-        for q in range(4):
-            z_wide(1, q, 0)
-        z_quant(0, 0)
-        f_quant(0, 0)
-        f_quant(1, 0)
-        for q in range(4):
-            f_bank(0, 1, q)
-        z_weave(1, 0)
-        cs_part(2, 0)
-        cs_part(2, 1)
-        for q in range(4):
-            f_bank(1, 1, q, "v")
-            if q == 0:
-                z_quant(1, 0)
-                f_quant(0, 1)
-        for q in range(4):
-            z_wide(1, q, 1)
-        z_weave(0, 1)
-        f_quant(1, 1)
+        f_bank(0, 0, 0)
+        f_bank(0, 0, 1)
         c_quant(2)
+        z_quant(0, 0)
+        cs_part(4)
+        cs_part(5)
+        z_weave(1, 0)
+        f_bank(0, 1, 0, "v")
+        f_quant(0, 0)
+        f_bank(0, 1, 1, "v")
+        z_quant(1, 0)
+        for t in range(4):
+            z_wide(1, t, 1)
+        f_bank(1, 0, 0, "v")
+        f_bank(1, 0, 1, "v")
+        f_quant(0, 1)
+        f_bank(1, 1, 0, "v")
+        f_bank(1, 1, 1, "v")
+        f_quant(1, 0)
+        c_quant(3)
+        f_quant(1, 1)
+        z_weave(0, 1)
+        units = [(0, 0), (1, 0), (2, 0), (0, 1), (1, 1), (2, 1)] + [(s, half) for s in range(3, 8) for half in range(2)]
+        units = [(s, W512 * half, W512) for s, half in units]
+        units = units[:-1] + [(7, 512, 256), (7, 768, 128), (7, 896, 128)]
+        rest = [(s, g, part) for s in range(2, 8) for g in range(2) for part in range(2)]
+        for g in range(2):
+            for part in range(2):
+                f_bank(2, g, part)
+        cs_part(6)
+        cs_part(7)
+        f_quant(2, 0)
         z_quant(0, 1)
-        units = [(c, j, W512 * half, W512) for c, half in ((0, 0), (1, 0), (0, 1), (1, 1), (2, 0), (2, 1), (3, 0), (3, 1)) for j in range(2)]
-        units = units[:-1] + [(3, 1, 512, 256), (3, 1, 768, 128), (3, 1, 896, 128)]
-        rest = [(c, g, b) for c in (2, 3) for g in range(2) for b in range(4)]
+        f_quant(2, 1)
+        z_weave(1, 1)
+        c_quant(4)
+        z_quant(1, 1)
         for n, y in enumerate(units):
-            y_mm(*y, "rb", "rb")
-            if n == 0:
-                z_weave(1, 1)
-            if n == 1:
-                z_quant(1, 1)
-                for part in range(2):
-                    c_turn(3, part)
-                    c_out(3, part)
-            if n >= 1:
-                y_sum(*units[n - 1])
-            if n == 2:
-                c_quant(3)
-            if 2 <= n < 10:
-                for k, fb in enumerate(rest[2 * n - 4 : 2 * n - 2]):
-                    f_bank(*fb, "sv"[k])
-            if n in (4, 6, 8, 10):
-                f_quant(*rest[2 * n - 8][:2])
-        y_sum(*units[-1])
+            y_mm(*y)
+            if n < 3:
+                c_quant(n + 5)
+            if 1 <= n < 11:
+                s, g = divmod(n + 5, 2)
+                f_bank(s, g, 0, "s" if n % 3 else "v")
+                f_bank(s, g, 1, "v")
+            if n >= 2:
+                y_sum(*units[n - 2])
+            if 2 <= n < 12:
+                f_quant(*divmod(n + 4, 2))
+        for y in units[-2:]:
+            y_sum(*y)

@@ -36,7 +36,6 @@ def tile_isar_split_real_image_s11_kernel(
 
         ident = keep.tile([P, P], F32, name="ident", align_bytes=64)
         scale_p8 = keep.tile([P, 2, 4], F32, name="scale_p8")
-        ones = keep.tile([P, 1], F32, name="ones")
         taper_bf = keep.tile([P, 2, 4], BF16, name="taper_bf")
         taper_f = keep.tile([P, 2, 4], F32, name="taper_f")
         cs_first = [keep.tile([P, 2, J], BF16, name="cs_first%d" % j, align_bytes=64) for j in range(2)]
@@ -61,7 +60,6 @@ def tile_isar_split_real_image_s11_kernel(
         z_q = [[keep.tile([P, W512], U32, name="z_q%d%d" % (g, r), align_bytes=64) for r in range(2)] for g in range(2)]
         z_s = [[keep.tile([P, W512], U8, name="z_s%d%d" % (g, r), align_bytes=64) for r in range(2)] for g in range(2)]
         e_sc = {}
-        sorted_words = {}
         f_grp = {}
         z_grp = {}
         z_rows = {}
@@ -161,17 +159,7 @@ def tile_isar_split_real_image_s11_kernel(
         def e_wide(i, eng="v"):
             s = work.tile([P, L], BF16, name="e_sc", bufs=8, align_bytes=64)
             e_sc[i] = s
-            sorted_words[i] = eng == "v"
-            if eng == "v":
-                nc.vector.tensor_scalar(
-                    out=s[:].rearrange("p (u w e) -> p w u e", u=2, e=2),
-                    in0=e_in[i].bitcast(FP8).rearrange("p (w u e) -> p w u e", u=2, e=2),
-                    scalar1=ones[:],
-                    scalar2=None,
-                    op0=ALU.mult,
-                )
-            else:
-                nc.scalar.copy(out=s[:], in_=e_in[i].bitcast(FP8))
+            copy(eng, s[:], e_in[i].bitcast(FP8))
 
         def e_turn(i):
             b = bank()
@@ -179,7 +167,7 @@ def tile_isar_split_real_image_s11_kernel(
             words = e_sc[i][:].bitcast(F32)
             for q in range(4):
                 u, k = divmod(q, 2)
-                src = words[:, q * P : (q + 1) * P] if sorted_words[i] else words[:, 2 * P * k + u : 2 * P * (k + 1) : 2]
+                src = words[:, 2 * P * k + u : 2 * P * (k + 1) : 2]
                 nc.tensor.transpose(b[:, q * P : (q + 1) * P], src, ident[:])
 
         def e_out(i):
@@ -282,7 +270,6 @@ def tile_isar_split_real_image_s11_kernel(
 
         ctx.enter_context(tc.manual_schedule())
         make_identity(nc, ident[:])
-        nc.vector.memset(ones[:], 1.0)
         nc.vector.memset(w_s[:].bitcast(I32), 0)
         for x in range(3):
             load_e(x)

@@ -275,14 +275,14 @@ def tile_isar_split_real_image_s11_kernel(
             load_e(x)
         load_scale()
         load_e(3)
-        load_strip(0)
-        load_e(4)
-        load_strip(1)
-        load_taper()
-        load_w(0)
         load_ws()
+        load_w(0)
+        load_e(4)
+        load_taper()
+        load_strip(0)
         load_h(0)
         load_w(1)
+        load_strip(1)
         load_pair(1)
         load_h(1)
         load_pair(2)
@@ -296,32 +296,31 @@ def tile_isar_split_real_image_s11_kernel(
         e_wide(6, "s")
         e_wide(7, "s")
         taper_widen()
-        for i in (0, 1, 2, 3, 4):
+        for i in (0, 1, 2, 3, 4, 5):
             e_turn(i)
         e_out(0)
         e_out(1)
         e_quant(0)
         e_out(2)
         e_quant(1)
-        cs_part(0)
-        e_turn(5)
-        cs_part(1)
-        e_out(3)
-        e_quant(2)
         z_wide(0, 0, 0)
         z_wide(0, 1, 0)
+        h_weave(0, "s", slice(0, 2))
+        e_out(3)
+        e_quant(2)
+        e_turn(6)
+        cs_part(0)
+        e_turn(7)
+        h_weave(0, "s", slice(2, 4))
         e_out(4)
         e_quant(3)
-        e_turn(6)
-        e_turn(7)
-        h_weave(0, "s", slice(0, 2))
-        e_out(5)
-        e_quant(4)
         z_wide(0, 2, 0)
         z_wide(0, 0, 1)
         z_wide(0, 3, 0)
-        h_weave(0, "s", slice(2, 4))
+        e_out(5)
+        e_quant(4)
         z_wide(0, 1, 1)
+        cs_part(1)
         e_out(6)
         e_quant(5)
         cs_part(2)

@@ -354,7 +354,7 @@ def tile_isar_split_real_image_s11_kernel(
         f_bank(1, 0, 0, "v")
         f_bank(1, 0, 1, "v")
         f_quant(0, 1)
-        f_bank(1, 1, 0, "v")
+        f_bank(1, 1, 0, "s")
         f_bank(1, 1, 1, "v")
         f_quant(1, 0)
         c_quant(3)
@@ -381,7 +381,7 @@ def tile_isar_split_real_image_s11_kernel(
                 c_quant(n + 5)
             if 1 <= n < 11:
                 s, g = divmod(n + 5, 2)
-                f_bank(s, g, 0, "s" if n % 3 else "v")
+                f_bank(s, g, 0, "s")
                 f_bank(s, g, 1, "v")
             if n >= 2:
                 y_sum(*units[n - 2])

@@ -41,9 +41,9 @@ def tile_isar_split_real_image_s11_kernel(
         cs_first = [keep.tile([P, 2, J], BF16, name="cs_first%d" % j, align_bytes=64) for j in range(2)]
         cs_pair = [keep.tile([P, 2, 2, J], BF16, name="cs_pair%d" % c, align_bytes=64) for c in range(1, 4)]
         cs_raw = [cs_first[0][:], cs_first[1][:]] + [cs_pair[c][:, :, j, :] for c in range(3) for j in range(2)]
-        cs_grp = [keep.tile([P, 2 * P, 4], BF16, name="cs_grp%d" % s, align_bytes=64) for s in range(STRIPS)]
-        cs_q = [keep.tile([P, 2 * P], U32, name="cs_q%d" % s, align_bytes=64) for s in range(STRIPS)]
-        cs_s = [keep.tile([P, 2 * P], U8, name="cs_s%d" % s, align_bytes=64) for s in range(STRIPS)]
+        cs_grp = [keep.tile([P, 2, 2 * P, 4], BF16, name="cs_grp%d" % c, align_bytes=64) for c in range(STRIPS // 2)]
+        cs_q = [keep.tile([P, 2, 2 * P], U32, name="cs_q%d" % c, align_bytes=64) for c in range(STRIPS // 2)]
+        cs_s = [keep.tile([P, 2, 2 * P], U8, name="cs_s%d" % c, align_bytes=64) for c in range(STRIPS // 2)]
         h_raw = [keep.tile([P, 4, W512], BF16, name="h_raw%d" % g, align_bytes=64) for g in range(2)]
         h_grp = [keep.tile([P, W512, 4], BF16, name="h_grp%d" % g, align_bytes=64) for g in range(2)]
         h_q = [keep.tile([P, W512], U32, name="h_q%d" % g, align_bytes=64) for g in range(2)]
@@ -55,8 +55,8 @@ def tile_isar_split_real_image_s11_kernel(
         e_s = [keep.tile([P, 2 * P], U8, name="e_s%d" % i, align_bytes=64) for i in range(8)]
         w_q = [keep.tile([P, 2, R], U8, name="w_q%d" % r, align_bytes=64) for r in range(2)]
         w_s = keep.tile([P, 2, R], U8, name="w_s", align_bytes=64)
-        f_q = [[keep.tile([P, 2 * P], U32, name="f_q%d%d" % (s, g), align_bytes=64) for g in range(2)] for s in range(STRIPS)]
-        f_s = [[keep.tile([P, 2 * P], U8, name="f_s%d%d" % (s, g), align_bytes=64) for g in range(2)] for s in range(STRIPS)]
+        f_q = [keep.tile([P, W512], U32, name="f_q%d" % s, align_bytes=64) for s in range(STRIPS)]
+        f_s = [keep.tile([P, W512], U8, name="f_s%d" % s, align_bytes=64) for s in range(STRIPS)]
         z_q = [[keep.tile([P, W512], U32, name="z_q%d%d" % (g, r), align_bytes=64) for r in range(2)] for g in range(2)]
         z_s = [[keep.tile([P, W512], U8, name="z_s%d%d" % (g, r), align_bytes=64) for r in range(2)] for g in range(2)]
         e_sc = {}
@@ -129,7 +129,7 @@ def tile_isar_split_real_image_s11_kernel(
                     )
 
         def c_out(s, eng="s"):
-            dst = cs_grp[s][:].rearrange("p n t -> p (n t)").bitcast(F32)
+            dst = cs_grp[s // 2][:, s % 2].rearrange("p n t -> p (n t)").bitcast(F32)
             copy(
                 eng,
                 dst.rearrange("p (a m u) -> p a m u", a=2, u=2),
@@ -144,13 +144,20 @@ def tile_isar_split_real_image_s11_kernel(
             nc.vector.quantize_mx(out=q[:].bitcast(FP8X4), scales=s[:], in_=grp[:].rearrange("p n t -> p (n t)"))
 
         def c_quant(s):
-            quant(cs_q[s], cs_s[s], cs_grp[s])
+            quant(cs_q[s // 2][:, s % 2], cs_s[s // 2][:, s % 2], cs_grp[s // 2][:, s % 2])
 
-        def h_weave(g, eng, ts=slice(0, 4)):
+        def c_quant_pair(c):
+            quant(
+                cs_q[c][:].rearrange("p j n -> p (j n)"),
+                cs_s[c][:].rearrange("p j n -> p (j n)"),
+                cs_grp[c][:].rearrange("p j n t -> p (j n) t"),
+            )
+
+        def h_weave(g, eng, ms=slice(0, P)):
             copy(
                 eng,
-                h_grp[g][:].rearrange("p (t m) j -> p t m j", t=4)[:, ts],
-                h_raw[g][:].rearrange("p j (m t) -> p t m j", t=4)[:, ts],
+                h_grp[g][:].rearrange("p (t m) j -> p m t j", t=4)[:, ms],
+                h_raw[g][:].rearrange("p j (m t) -> p m t j", t=4)[:, ms],
             )
 
         def h_quant(g):
@@ -190,18 +197,19 @@ def tile_isar_split_real_image_s11_kernel(
                     out=acc[:, st],
                     lhsT=h_q[g][:, st].bitcast(FP8X4),
                     lhsT_scale=h_s[g][:, st],
-                    rhs=cs_q[s][:, cols].bitcast(FP8X4),
-                    rhs_scale=cs_s[s][:, cols],
+                    rhs=cs_q[s // 2][:, s % 2, cols].bitcast(FP8X4),
+                    rhs_scale=cs_s[s // 2][:, s % 2, cols],
                     start=True,
                     stop=True,
                 )
-            if (s, g) not in f_grp:
-                f_new = work.tile([P, 2 * P, 4], BF16, name="f_grp", bufs=8, align_bytes=64)
-                f_grp[s, g] = f_new
-            copy(eng, f_grp[s, g][:, cols, :], acc[:].rearrange("p (t n) -> p n t", t=4))
+            if s not in f_grp:
+                f_new = work.tile([P, W512, 4], BF16, name="f_grp", align_bytes=64)
+                f_grp[s] = f_new
+            at = (2 * g + part) * P
+            copy(eng, f_grp[s][:, at : at + P, :], acc[:].rearrange("p (t n) -> p n t", t=4))
 
-        def f_quant(s, g):
-            quant(f_q[s][g], f_s[s][g], f_grp[s, g])
+        def f_quant(s):
+            quant(f_q[s], f_s[s], f_grp[s])
 
         def z_wide(g, t, half, eng="s"):
             acc = bank()
@@ -226,12 +234,41 @@ def tile_isar_split_real_image_s11_kernel(
                 nc.scalar.activation(out=z_rows[g, half][:, t, :], in_=acc[:], func=ACT.Copy, scale=gain)
 
         def z_weave(g, half, eng="v"):
-            z_new = work.tile([P, W512, 4], BF16, name="z_grp", bufs=2, align_bytes=64)
+            z_new = work.tile([P, W512, 4], BF16, name="z_grp", bufs=3, align_bytes=64)
             z_grp[g, half] = z_new
             copy(
                 eng,
                 z_new[:].rearrange("p (c i) t -> p c t i", i=4),
                 z_rows[g, half][:].rearrange("p t (c i) -> p c t i", i=4),
+            )
+
+        def z_narrow_mm(g, half, rb):
+            acc = bank()
+            banks["z", g, half, rb] = acc
+            for t in range(4):
+                for k in range(2):
+                    st = slice(k * P, (k + 1) * P)
+                    at = half * W512 + rb * P
+                    nc.tensor.matmul_mx(
+                        out=acc[:, t * P : (t + 1) * P],
+                        lhsT=e_q[4 * g + t][:, st].bitcast(FP8X4),
+                        lhsT_scale=e_s[4 * g + t][:, st],
+                        rhs=w_q[half][:, k, 2 * rb * P : 2 * (rb + 1) * P].bitcast(FP4X4),
+                        rhs_scale=w_s[:, k, at : at + P],
+                        start=(k == 0),
+                        stop=(k == 1),
+                    )
+
+        def z_narrow_out(g, half, rb):
+            acc = banks["z", g, half, rb]
+            if (g, half) not in z_grp:
+                z_new = work.tile([P, W512, 4], BF16, name="z_grp", bufs=3, align_bytes=64)
+                z_grp[g, half] = z_new
+            nc.vector.tensor_tensor(
+                out=z_grp[g, half][:, rb * P : (rb + 1) * P, :],
+                in0=acc[:].rearrange("p (t n) -> p n t", t=4),
+                in1=taper_f[:, g, :].unsqueeze(1).to_broadcast([P, P, 4]),
+                op=ALU.mult,
             )
 
         def z_quant(g, half):
@@ -242,12 +279,12 @@ def tile_isar_split_real_image_s11_kernel(
             rc = slice(first, first + width)
             for part in range(2):
                 b = bank()
-                cols = slice(part * P, (part + 1) * P)
                 for g in range(2):
+                    cols = slice((2 * g + part) * P, (2 * g + part + 1) * P)
                     nc.tensor.matmul_mx(
                         out=b[:, 0:width],
-                        lhsT=f_q[s][g][:, cols].bitcast(FP8X4),
-                        lhsT_scale=f_s[s][g][:, cols],
+                        lhsT=f_q[s][:, cols].bitcast(FP8X4),
+                        lhsT_scale=f_s[s][:, cols],
                         rhs=z_q[g][half][:, rc].bitcast(FP8X4),
                         rhs_scale=z_s[g][half][:, rc],
                         start=(g == 0),
@@ -305,13 +342,13 @@ def tile_isar_split_real_image_s11_kernel(
         e_quant(1)
         z_wide(0, 0, 0)
         z_wide(0, 1, 0)
-        h_weave(0, "s", slice(0, 2))
+        h_weave(0, "s", slice(0, P // 2))
         e_out(3)
         e_quant(2)
         e_turn(6)
         cs_part(0)
         e_turn(7)
-        h_weave(0, "s", slice(2, 4))
+        h_weave(0, "s", slice(P // 2, P))
         e_out(4)
         e_quant(3)
         z_wide(0, 2, 0)
@@ -323,6 +360,7 @@ def tile_isar_split_real_image_s11_kernel(
         cs_part(1)
         e_out(6)
         e_quant(5)
+        h_weave(1, "s", slice(P // 2, P))
         cs_part(2)
         cs_part(3)
         e_out(7)
@@ -330,62 +368,58 @@ def tile_isar_split_real_image_s11_kernel(
         c_quant(0)
         e_quant(7)
         h_quant(0)
-        for t in range(4):
-            z_wide(1, t, 0)
-        h_weave(1, "v")
-        c_quant(1)
-        h_quant(1)
         z_wide(0, 2, 1)
         z_wide(0, 3, 1)
+        for rb in range(4):
+            z_narrow_mm(1, 0, rb)
+        h_weave(1, "v", slice(0, P // 2))
+        c_quant(1)
+        h_quant(1)
+        for s in range(2):
+            for part in range(2):
+                f_bank(s, 0, part)
+        for rb in range(4):
+            z_narrow_out(1, 0, rb)
         z_weave(0, 0)
-        f_bank(0, 0, 0)
-        f_bank(0, 0, 1)
-        c_quant(2)
+        for s in range(2):
+            for part in range(2):
+                f_bank(s, 1, part)
+        z_quant(1, 0)
         z_quant(0, 0)
+        f_quant(0)
+        c_quant_pair(1)
         cs_part(4)
         cs_part(5)
-        z_weave(1, 0)
-        f_bank(0, 1, 0, "v")
-        f_quant(0, 0)
-        f_bank(0, 1, 1, "v")
-        z_quant(1, 0)
         for t in range(4):
             z_wide(1, t, 1)
-        f_bank(1, 0, 0, "v")
-        f_bank(1, 0, 1, "v")
-        f_quant(0, 1)
-        f_bank(1, 1, 0, "s")
-        f_bank(1, 1, 1, "v")
-        f_quant(1, 0)
-        c_quant(3)
-        f_quant(1, 1)
         z_weave(0, 1)
-        units = [(0, 0), (1, 0), (2, 0), (0, 1), (1, 1), (2, 1)] + [(s, half) for s in range(3, 8) for half in range(2)]
-        units = [(s, W512 * half, W512) for s, half in units]
-        units = units[:-1] + [(7, 512, 256), (7, 768, 128), (7, 896, 128)]
-        rest = [(s, g, part) for s in range(2, 8) for g in range(2) for part in range(2)]
-        for g in range(2):
-            for part in range(2):
-                f_bank(2, g, part)
+        f_quant(1)
+        z_quant(0, 1)
+        z_weave(1, 1)
         cs_part(6)
         cs_part(7)
-        f_quant(2, 0)
-        z_quant(0, 1)
-        f_quant(2, 1)
-        z_weave(1, 1)
-        c_quant(4)
-        z_quant(1, 1)
+        units = [(0, 0), (1, 0), (0, 1), (1, 1)] + [(s, half) for s in range(2, 8) for half in range(2)]
+        units = [(s, W512 * half, W512) for s, half in units]
+        units = units[:-1] + [(7, 512, 256), (7, 768, 256)]
         for n, y in enumerate(units):
             y_mm(*y)
-            if n < 3:
-                c_quant(n + 5)
-            if 1 <= n < 11:
-                s, g = divmod(n + 5, 2)
+            if n == 1:
+                z_quant(1, 1)
+                for g in range(2):
+                    for part in range(2):
+                        f_bank(2, g, part, "v")
+                c_quant_pair(2)
+                f_quant(2)
+            if n == 2:
+                c_quant_pair(3)
+            if n in (4, 6, 8, 10, 12):
+                f_quant(n // 2 + 1)
+            if 2 <= n < 12:
+                s, g = divmod(n + 4, 2)
                 f_bank(s, g, 0, "s")
                 f_bank(s, g, 1, "v")
-            if n >= 2:
+            if 2 <= n <= 7:
                 y_sum(*units[n - 2])
-            if 2 <= n < 12:
-                f_quant(*divmod(n + 4, 2))
-        for y in units[-2:]:
-            y_sum(*y)
+            if n >= 7:
+                y_sum(*units[n - 1])
+        y_sum(*units[-1])

@@ -60,6 +60,7 @@ def tile_isar_split_real_image_s11_kernel(
         z_q = [[keep.tile([P, W512], U32, name="z_q%d%d" % (g, r), align_bytes=64) for r in range(2)] for g in range(2)]
         z_s = [[keep.tile([P, W512], U8, name="z_s%d%d" % (g, r), align_bytes=64) for r in range(2)] for g in range(2)]
         e_sc = {}
+        cs_sorted = {}
         f_grp = {}
         z_grp = {}
         z_rows = {}
@@ -118,15 +119,19 @@ def tile_isar_split_real_image_s11_kernel(
             else:
                 nc.scalar.copy(out=dst, in_=src)
 
+        def c_sort(s):
+            w = work.tile([P, 2, 2, P], F32, name="cs_sorted", align_bytes=64)
+            cs_sorted[s] = w
+            nc.scalar.copy(out=w[:], in_=cs_raw[s].bitcast(F32).rearrange("p a (m u) -> p a u m", u=2))
+
         def c_turn(s):
             b = bank()
             banks["c", s] = b
             for part in range(2):
                 words = cs_raw[s][:, part, :].bitcast(F32)
                 for u in range(2):
-                    nc.tensor.transpose(
-                        b[:, (2 * part + u) * P : (2 * part + u + 1) * P], words[:, u : 2 * P : 2], ident[:]
-                    )
+                    src = cs_sorted[s][:, part, u, :] if s in cs_sorted else words[:, u : 2 * P : 2]
+                    nc.tensor.transpose(b[:, (2 * part + u) * P : (2 * part + u + 1) * P], src, ident[:])
 
         def c_out(s, eng="s"):
             dst = cs_grp[s // 2][:, s % 2].rearrange("p n t -> p (n t)").bitcast(F32)
@@ -225,22 +230,13 @@ def tile_isar_split_real_image_s11_kernel(
                     stop=(k == 1),
                 )
             if (g, half) not in z_rows:
-                rows_new = work.tile([P, 4, W512], BF16, name="z_rows", align_bytes=64)
+                rows_new = work.tile([P, 4, W512], BF16, name="z_rows", bufs=2, align_bytes=64)
                 z_rows[g, half] = rows_new
             gain = taper_f[:, g, t : t + 1]
             if eng == "v":
                 nc.vector.tensor_scalar(out=z_rows[g, half][:, t, :], in0=acc[:], scalar1=gain, scalar2=None, op0=ALU.mult)
             else:
                 nc.scalar.activation(out=z_rows[g, half][:, t, :], in_=acc[:], func=ACT.Copy, scale=gain)
-
-        def z_weave(g, half, eng="v"):
-            z_new = work.tile([P, W512, 4], BF16, name="z_grp", bufs=3, align_bytes=64)
-            z_grp[g, half] = z_new
-            copy(
-                eng,
-                z_new[:].rearrange("p (c i) t -> p c t i", i=4),
-                z_rows[g, half][:].rearrange("p t (c i) -> p c t i", i=4),
-            )
 
         def z_narrow_mm(g, half, rb):
             acc = bank()
@@ -271,6 +267,17 @@ def tile_isar_split_real_image_s11_kernel(
                 op=ALU.mult,
             )
 
+        def z_weave_gpsimd(g, half, into):
+            z_grp[g, half] = into
+            nc.gpsimd.tensor_scalar(
+                out=into[:],
+                in0=z_rows[g, half][:].rearrange("p t n -> p n t"),
+                scalar1=1.0,
+                scalar2=0.0,
+                op0=ALU.mult,
+                op1=ALU.add,
+            )
+
         def z_quant(g, half):
             quant(z_q[g][half], z_s[g][half], z_grp[g, half])
 
@@ -290,7 +297,7 @@ def tile_isar_split_real_image_s11_kernel(
                         start=(g == 0),
                         stop=(g == 1),
                     )
-                sq = outs.tile([P, W512], F32, name="sq%d" % part, bufs=7, align_bytes=64)
+                sq = outs.tile([P, W512], F32, name="sq%d" % part, bufs=6, align_bytes=64)
                 nc.scalar.activation(out=sq[:, 0:width], in_=b[:, 0:width], func=ACT.Square)
                 squares[s, at, part] = sq
 
@@ -375,36 +382,37 @@ def tile_isar_split_real_image_s11_kernel(
         h_weave(1, "v", slice(0, P // 2))
         c_quant(1)
         h_quant(1)
+        z_weave_gpsimd(0, 0, h_grp[1])
+        for rb in range(4):
+            z_narrow_out(1, 0, rb)
         for s in range(2):
             for part in range(2):
                 f_bank(s, 0, part)
-        for rb in range(4):
-            z_narrow_out(1, 0, rb)
-        z_weave(0, 0)
         for s in range(2):
             for part in range(2):
-                f_bank(s, 1, part)
+                f_bank(s, 1, part, "v" if s + part == 0 else "s")
         z_quant(1, 0)
         z_quant(0, 0)
         f_quant(0)
         c_quant_pair(1)
-        cs_part(4)
-        cs_part(5)
-        for t in range(4):
-            z_wide(1, t, 1)
-        z_weave(0, 1)
         f_quant(1)
-        z_quant(0, 1)
-        z_weave(1, 1)
-        cs_part(6)
-        cs_part(7)
+        z_weave_gpsimd(0, 1, f_grp[1])
+        for rb in range(4):
+            z_narrow_mm(1, 1, rb)
+            z_narrow_out(1, 1, rb)
+        for s in range(4, STRIPS):
+            c_sort(s)
+
         units = [(0, 0), (1, 0), (0, 1), (1, 1)] + [(s, half) for s in range(2, 8) for half in range(2)]
         units = [(s, W512 * half, W512) for s, half in units]
         units = units[:-1] + [(7, 512, 256), (7, 768, 256)]
         for n, y in enumerate(units):
             y_mm(*y)
             if n == 1:
+                for s in range(4, STRIPS):
+                    cs_part(s, "v" if s == 4 else "s")
                 z_quant(1, 1)
+                z_quant(0, 1)
                 for g in range(2):
                     for part in range(2):
                         f_bank(2, g, part, "v")

@@ -17,9 +17,12 @@ ACT = mybir.ActivationFunctionType
 ALU = mybir.AluOpType
 
 P = 128
-STRIPS = 8
-W512 = 512
-E_LOADS = ((0, 1), (1, 2), (3, 1), (4, 2), (6, 2))
+BANK = 512
+STRIPS = D // P
+TILES = T // P
+ECHO_LOADS = ((0, 1), (1, 1), (2, 1), (3, 1), (4, 2), (6, 2))
+EARLY_STRIPS = 3
+SUM_LAG = 2
 
 FLOPS = 2 * (2 * D * J * T + T * L * R + 2 * D * T * R)
 
@@ -31,403 +34,404 @@ def tile_isar_split_real_image_s11_kernel(
     with ExitStack() as ctx:
         keep = ctx.enter_context(tc.tile_pool(name="keep", bufs=1))
         work = ctx.enter_context(tc.tile_pool(name="work", bufs=4))
-        outs = ctx.enter_context(tc.tile_pool(name="outs", bufs=4))
+        outs = ctx.enter_context(tc.tile_pool(name="outs", bufs=6))
         psum = ctx.enter_context(tc.psum_pool(name="psum", bufs=8))
 
         ident = keep.tile([P, P], F32, name="ident", align_bytes=64)
-        scale_p8 = keep.tile([P, 2, 4], F32, name="scale_p8")
+        scale = keep.tile([P, 2, 4], F32, name="scale")
         taper_bf = keep.tile([P, 2, 4], BF16, name="taper_bf")
-        taper_f = keep.tile([P, 2, 4], F32, name="taper_f")
-        cs_first = [keep.tile([P, 2, J], BF16, name="cs_first%d" % j, align_bytes=64) for j in range(2)]
+        gain = keep.tile([P, 2, 4], F32, name="gain")
+        cs_single = [keep.tile([P, 2, J], BF16, name="cs_single%d" % j, align_bytes=64) for j in range(2)]
         cs_pair = [keep.tile([P, 2, 2, J], BF16, name="cs_pair%d" % c, align_bytes=64) for c in range(1, 4)]
-        cs_raw = [cs_first[0][:], cs_first[1][:]] + [cs_pair[c][:, :, j, :] for c in range(3) for j in range(2)]
-        cs_grp = [keep.tile([P, 2, 2 * P, 4], BF16, name="cs_grp%d" % c, align_bytes=64) for c in range(STRIPS // 2)]
-        cs_q = [keep.tile([P, 2, 2 * P], U32, name="cs_q%d" % c, align_bytes=64) for c in range(STRIPS // 2)]
-        cs_s = [keep.tile([P, 2, 2 * P], U8, name="cs_s%d" % c, align_bytes=64) for c in range(STRIPS // 2)]
-        h_raw = [keep.tile([P, 4, W512], BF16, name="h_raw%d" % g, align_bytes=64) for g in range(2)]
-        h_grp = [keep.tile([P, W512, 4], BF16, name="h_grp%d" % g, align_bytes=64) for g in range(2)]
-        h_q = [keep.tile([P, W512], U32, name="h_q%d" % g, align_bytes=64) for g in range(2)]
-        h_s = [keep.tile([P, W512], U8, name="h_s%d" % g, align_bytes=64) for g in range(2)]
-        e_bytes = [keep.tile([P, n, L], U8, name="e_bytes%d" % i, align_bytes=64) for i, n in E_LOADS]
-        e_in = [e_bytes[x][:, j, :] for x, (i, n) in enumerate(E_LOADS) for j in range(n)]
-        e_grp = [keep.tile([P, 2 * P, 4], BF16, name="e_grp%d" % i, align_bytes=64) for i in range(8)]
-        e_q = [keep.tile([P, 2 * P], U32, name="e_q%d" % i, align_bytes=64) for i in range(8)]
-        e_s = [keep.tile([P, 2 * P], U8, name="e_s%d" % i, align_bytes=64) for i in range(8)]
-        w_q = [keep.tile([P, 2, R], U8, name="w_q%d" % r, align_bytes=64) for r in range(2)]
+        cs_raw = [cs_single[0][:], cs_single[1][:]] + [cs_pair[c][:, :, j, :] for c in range(3) for j in range(2)]
+        cs_woven = [keep.tile([P, 2, 2 * P, 4], BF16, name="cs_woven%d" % c, align_bytes=64) for c in range(4)]
+        cs_q = [keep.tile([P, 2, 2 * P], U32, name="cs_q%d" % c, align_bytes=64) for c in range(4)]
+        cs_s = [keep.tile([P, 2, 2 * P], U8, name="cs_s%d" % c, align_bytes=64) for c in range(4)]
+        h_raw = [keep.tile([P, 4, BANK], BF16, name="h_raw%d" % g, align_bytes=64) for g in range(2)]
+        h_woven = [keep.tile([P, BANK, 4], BF16, name="h_woven%d" % g, align_bytes=64) for g in range(2)]
+        h_q = [keep.tile([P, BANK], U32, name="h_q%d" % g, align_bytes=64) for g in range(2)]
+        h_s = [keep.tile([P, BANK], U8, name="h_s%d" % g, align_bytes=64) for g in range(2)]
+        e_bytes = [keep.tile([P, n, L], U8, name="e_bytes%d" % i, align_bytes=64) for i, n in ECHO_LOADS]
+        e_in = [e_bytes[x][:, j, :] for x, (i, n) in enumerate(ECHO_LOADS) for j in range(n)]
+        e_woven = keep.tile([P, TILES * 2 * P, 4], BF16, name="e_woven", align_bytes=64)
+        e_q = keep.tile([P, TILES * 2 * P], U32, name="e_q", align_bytes=64)
+        e_s = keep.tile([P, TILES * 2 * P], U8, name="e_s", align_bytes=64)
+        w_q = [keep.tile([P, 2, R], U8, name="w_q%d" % half, align_bytes=64) for half in range(2)]
         w_s = keep.tile([P, 2, R], U8, name="w_s", align_bytes=64)
-        f_q = [keep.tile([P, W512], U32, name="f_q%d" % s, align_bytes=64) for s in range(STRIPS)]
-        f_s = [keep.tile([P, W512], U8, name="f_s%d" % s, align_bytes=64) for s in range(STRIPS)]
-        z_q = [[keep.tile([P, W512], U32, name="z_q%d%d" % (g, r), align_bytes=64) for r in range(2)] for g in range(2)]
-        z_s = [[keep.tile([P, W512], U8, name="z_s%d%d" % (g, r), align_bytes=64) for r in range(2)] for g in range(2)]
-        e_sc = {}
+        f_q = [keep.tile([P, BANK], U32, name="f_q%d" % s, align_bytes=64) for s in range(STRIPS)]
+        f_s = [keep.tile([P, BANK], U8, name="f_s%d" % s, align_bytes=64) for s in range(STRIPS)]
+        z_q = [[keep.tile([P, BANK], U32, name="z_q%d%d" % (g, r), align_bytes=64) for r in range(2)] for g in range(2)]
+        z_s = [[keep.tile([P, BANK], U8, name="z_s%d%d" % (g, r), align_bytes=64) for r in range(2)] for g in range(2)]
+        e_wide = {}
         cs_sorted = {}
-        f_grp = {}
-        z_grp = {}
+        f_woven = {}
+        z_woven = {}
         z_rows = {}
         banks = {}
         squares = {}
 
-        def bank():
-            t = psum.tile([P, W512], F32, name="bank")
-            return t
+        def bank(*key):
+            if key not in banks:
+                fresh = psum.tile([P, BANK], F32, name="bank")
+                banks[key] = fresh
+            return banks[key]
+
+        def copy(eng, dst, src):
+            if eng == "vector":
+                nc.vector.tensor_copy(out=dst, in_=src)
+            else:
+                nc.scalar.copy(out=dst, in_=src)
+
+        def quantise(codes, scales, woven):
+            nc.vector.quantize_mx(out=codes.bitcast(FP8X4), scales=scales, in_=woven.rearrange("p n t -> p (n t)"))
+
+        def load_echo(x):
+            i, n = ECHO_LOADS[x]
+            g, t = divmod(i, 4)
+            rows = echo_bytes[g * BANK : (g + 1) * BANK, :].rearrange("(m t) k -> m t k", t=4)
+            nc.sync.dma_start(out=e_bytes[x][:], in_=rows[:, t : t + n, :])
 
         def load_strip(j):
             rows = cs.rearrange("(a c p j) k -> c j p a k", a=2, p=P, j=2)
-            nc.sync.dma_start(out=cs_first[j][:], in_=rows[0, j])
+            nc.sync.dma_start(out=cs_single[j][:], in_=rows[0, j])
 
         def load_pair(c):
             rows = cs.rearrange("(a c p j) k -> c p a (j k)", a=2, p=P, j=2)
             nc.sync.dma_start(out=cs_pair[c - 1][:].rearrange("p a j k -> p a (j k)"), in_=rows[c])
 
         def load_h(g):
-            nc.sync.dma_start(
-                out=h_raw[g][:],
-                in_=h.rearrange("(p j) w -> p j w", j=4)[:, :, g * W512 : (g + 1) * W512],
-            )
+            rows = h.rearrange("(p j) w -> p j w", j=4)
+            nc.sync.dma_start(out=h_raw[g][:], in_=rows[:, :, g * BANK : (g + 1) * BANK])
 
-        def load_e(x):
-            i, n = E_LOADS[x]
-            g, t = divmod(i, 4)
-            rows = echo_bytes[g * W512 : (g + 1) * W512, :].rearrange("(m t) k -> m t k", t=4)
-            nc.sync.dma_start(out=e_bytes[x][:], in_=rows[:, t : t + n, :])
+        def load_w(half):
+            words = w_words[:, :, half * R : (half + 1) * R].bitcast(I32)
+            nc.sync.dma_start(out=w_q[half][:].bitcast(I32), in_=words.rearrange("g p n -> p g n"))
 
-        def load_w(r):
-            nc.sync.dma_start(
-                out=w_q[r][:].bitcast(I32),
-                in_=w_words[:, :, r * R : (r + 1) * R].bitcast(I32).rearrange("g p n -> p g n"),
-            )
-
-        def load_ws():
+        def load_w_scales():
             for q in (0, 2, 1, 3):
-                nc.sync.dma_start(
-                    out=w_s[32 * q : 32 * q + 4, :, :].bitcast(I32),
-                    in_=w_scales[:, 4 * q : 4 * q + 4, :].bitcast(I32).rearrange("g q n -> q g n"),
-                )
+                rows = w_scales[:, 4 * q : 4 * q + 4, :].bitcast(I32)
+                nc.sync.dma_start(out=w_s[32 * q : 32 * q + 4, :, :].bitcast(I32), in_=rows.rearrange("g q n -> q g n"))
 
-        def load_scale():
-            nc.sync.dma_start(out=scale_p8[:], in_=echo_scale.rearrange("o (a p c) -> p (o a) c", a=2, c=4))
+        def cs_sort(s):
+            ordered = work.tile([P, 2, 2, P], F32, name="cs_sorted", align_bytes=64)
+            cs_sorted[s] = ordered
+            nc.scalar.copy(out=ordered[:], in_=cs_raw[s].bitcast(F32).rearrange("p a (m u) -> p a u m", u=2))
 
-        def load_taper():
-            nc.sync.dma_start(out=taper_bf[:], in_=taper.rearrange("(g p t) -> p g t", p=P, t=4))
-
-        def taper_widen():
-            nc.scalar.activation(out=taper_f[:], in_=taper_bf[:], func=ACT.Copy)
-
-        def copy(eng, dst, src):
-            if eng == "v":
-                nc.vector.tensor_copy(out=dst, in_=src)
-            else:
-                nc.scalar.copy(out=dst, in_=src)
-
-        def c_sort(s):
-            w = work.tile([P, 2, 2, P], F32, name="cs_sorted", align_bytes=64)
-            cs_sorted[s] = w
-            nc.scalar.copy(out=w[:], in_=cs_raw[s].bitcast(F32).rearrange("p a (m u) -> p a u m", u=2))
-
-        def c_turn(s):
-            b = bank()
-            banks["c", s] = b
+        def cs_turn(s):
             for part in range(2):
                 words = cs_raw[s][:, part, :].bitcast(F32)
                 for u in range(2):
                     src = cs_sorted[s][:, part, u, :] if s in cs_sorted else words[:, u : 2 * P : 2]
-                    nc.tensor.transpose(b[:, (2 * part + u) * P : (2 * part + u + 1) * P], src, ident[:])
+                    at = (2 * part + u) * P
+                    nc.tensor.transpose(bank("cs", s)[:, at : at + P], src, ident[:])
 
-        def c_out(s, eng="s"):
-            dst = cs_grp[s // 2][:, s % 2].rearrange("p n t -> p (n t)").bitcast(F32)
-            copy(
-                eng,
-                dst.rearrange("p (a m u) -> p a m u", a=2, u=2),
-                banks["c", s][:].rearrange("p (a u m) -> p a m u", a=2, u=2),
+        def cs_out(s):
+            dst = cs_woven[s // 2][:, s % 2].rearrange("p n t -> p (n t)").bitcast(F32)
+            nc.scalar.copy(
+                out=dst.rearrange("p (a m u) -> p a m u", a=2, u=2),
+                in_=bank("cs", s)[:].rearrange("p (a u m) -> p a m u", a=2, u=2),
             )
 
-        def cs_part(s, eng="s"):
-            c_turn(s)
-            c_out(s, eng)
+        def cs_pair_woven(c):
+            return cs_woven[c][:].rearrange("p j n t -> p (j n) t")
 
-        def quant(q, s, grp):
-            nc.vector.quantize_mx(out=q[:].bitcast(FP8X4), scales=s[:], in_=grp[:].rearrange("p n t -> p (n t)"))
-
-        def c_quant(s):
-            quant(cs_q[s // 2][:, s % 2], cs_s[s // 2][:, s % 2], cs_grp[s // 2][:, s % 2])
-
-        def c_quant_pair(c):
-            quant(
-                cs_q[c][:].rearrange("p j n -> p (j n)"),
-                cs_s[c][:].rearrange("p j n -> p (j n)"),
-                cs_grp[c][:].rearrange("p j n t -> p (j n) t"),
-            )
+        def cs_quantise(c):
+            flat = "p j n -> p (j n)"
+            quantise(cs_q[c][:].rearrange(flat), cs_s[c][:].rearrange(flat), cs_pair_woven(c))
 
         def h_weave(g, eng, ms=slice(0, P)):
             copy(
                 eng,
-                h_grp[g][:].rearrange("p (t m) j -> p m t j", t=4)[:, ms],
+                h_woven[g][:].rearrange("p (t m) j -> p m t j", t=4)[:, ms],
                 h_raw[g][:].rearrange("p j (m t) -> p m t j", t=4)[:, ms],
             )
 
-        def h_quant(g):
-            quant(h_q[g], h_s[g], h_grp[g])
+        def h_quantise(g):
+            quantise(h_q[g][:], h_s[g][:], h_woven[g][:])
 
-        def e_wide(i, eng="v"):
-            s = work.tile([P, L], BF16, name="e_sc", bufs=8, align_bytes=64)
-            e_sc[i] = s
-            copy(eng, s[:], e_in[i].bitcast(FP8))
+        def echo_widen(i, eng, pieces=1):
+            wide = work.tile([P, L], BF16, name="e_wide", bufs=TILES, align_bytes=64)
+            e_wide[i] = wide
+            for at in range(0, L, L // pieces):
+                ks = slice(at, at + L // pieces)
+                copy(eng, wide[:, ks], e_in[i][:, ks].bitcast(FP8))
 
-        def e_turn(i):
-            b = bank()
-            banks["e", i] = b
-            words = e_sc[i][:].bitcast(F32)
-            for q in range(4):
-                u, k = divmod(q, 2)
-                src = words[:, 2 * P * k + u : 2 * P * (k + 1) : 2]
-                nc.tensor.transpose(b[:, q * P : (q + 1) * P], src, ident[:])
+        def echo_turn(i):
+            words = e_wide[i][:].bitcast(F32)
+            for k in range(2):
+                for u in range(2):
+                    at = (2 * u + k) * P
+                    src = words[:, 2 * P * k + u : 2 * P * (k + 1) : 2]
+                    nc.tensor.transpose(bank("echo", i)[:, at : at + P], src, ident[:])
 
-        def e_out(i):
+        def echo_out(i):
+            dst = e_woven[:, 2 * P * i : 2 * P * (i + 1), :]
             nc.vector.tensor_tensor(
-                out=e_grp[i][:].rearrange("p (k m) (u e) -> p k m u e", k=2, u=2),
-                in0=banks["e", i][:].bitcast(BF16).rearrange("p (u k m e) -> p k m u e", u=2, k=2, e=2),
-                in1=scale_p8[:].rearrange("p k (u e) -> p k u e", u=2).unsqueeze(2).to_broadcast([P, 2, P, 2, 2]),
+                out=dst.rearrange("p (k m) (u e) -> p k m u e", k=2, u=2),
+                in0=bank("echo", i)[:].bitcast(BF16).rearrange("p (u k m e) -> p k m u e", u=2, k=2, e=2),
+                in1=scale[:].rearrange("p k (u e) -> p k u e", u=2).unsqueeze(2).to_broadcast([P, 2, P, 2, 2]),
                 op=ALU.mult,
             )
 
-        def e_quant(i):
-            quant(e_q[i], e_s[i], e_grp[i])
+        def echo_quantise(i, count=1):
+            cols = slice(2 * P * i, 2 * P * (i + count))
+            quantise(e_q[:, cols], e_s[:, cols], e_woven[:, cols, :])
 
-        def f_bank(s, g, part, eng="s"):
-            acc = bank()
-            cols = slice(part * P, (part + 1) * P)
+        def f_bank(s, g, part, eng="scalar"):
+            acc = bank("f", s, g, part)
+            bins = slice(part * P, (part + 1) * P)
             for t in range(4):
-                st = slice(t * P, (t + 1) * P)
+                slot = slice(t * P, (t + 1) * P)
                 nc.tensor.matmul_mx(
-                    out=acc[:, st],
-                    lhsT=h_q[g][:, st].bitcast(FP8X4),
-                    lhsT_scale=h_s[g][:, st],
-                    rhs=cs_q[s // 2][:, s % 2, cols].bitcast(FP8X4),
-                    rhs_scale=cs_s[s // 2][:, s % 2, cols],
+                    out=acc[:, slot],
+                    lhsT=h_q[g][:, slot].bitcast(FP8X4),
+                    lhsT_scale=h_s[g][:, slot],
+                    rhs=cs_q[s // 2][:, s % 2, bins].bitcast(FP8X4),
+                    rhs_scale=cs_s[s // 2][:, s % 2, bins],
                     start=True,
                     stop=True,
                 )
-            if s not in f_grp:
-                f_new = work.tile([P, W512, 4], BF16, name="f_grp", align_bytes=64)
-                f_grp[s] = f_new
+            if s not in f_woven:
+                fresh = work.tile([P, BANK, 4], BF16, name="f_woven", bufs=5, align_bytes=64)
+                f_woven[s] = fresh
             at = (2 * g + part) * P
-            copy(eng, f_grp[s][:, at : at + P, :], acc[:].rearrange("p (t n) -> p n t", t=4))
+            copy(eng, f_woven[s][:, at : at + P, :], acc[:].rearrange("p (t n) -> p n t", t=4))
 
-        def f_quant(s):
-            quant(f_q[s], f_s[s], f_grp[s])
+        def f_quantise(s):
+            quantise(f_q[s][:], f_s[s][:], f_woven[s][:])
 
-        def z_wide(g, t, half, eng="s"):
-            acc = bank()
+        def z_passes(acc, g, t, first, width):
+            half, at = divmod(first, BANK)
             for k in range(2):
-                st = slice(k * P, (k + 1) * P)
+                cols = slice((2 * (4 * g + t) + k) * P, (2 * (4 * g + t) + k + 1) * P)
                 nc.tensor.matmul_mx(
-                    out=acc[:],
-                    lhsT=e_q[4 * g + t][:, st].bitcast(FP8X4),
-                    lhsT_scale=e_s[4 * g + t][:, st],
-                    rhs=w_q[half][:, k, :].bitcast(FP4X4),
-                    rhs_scale=w_s[:, k, half * W512 : (half + 1) * W512],
+                    out=acc,
+                    lhsT=e_q[:, cols].bitcast(FP8X4),
+                    lhsT_scale=e_s[:, cols],
+                    rhs=w_q[half][:, k, 2 * at : 2 * (at + width)].bitcast(FP4X4),
+                    rhs_scale=w_s[:, k, first : first + width],
                     start=(k == 0),
                     stop=(k == 1),
                 )
-            if (g, half) not in z_rows:
-                rows_new = work.tile([P, 4, W512], BF16, name="z_rows", bufs=2, align_bytes=64)
-                z_rows[g, half] = rows_new
-            gain = taper_f[:, g, t : t + 1]
-            if eng == "v":
-                nc.vector.tensor_scalar(out=z_rows[g, half][:, t, :], in0=acc[:], scalar1=gain, scalar2=None, op0=ALU.mult)
-            else:
-                nc.scalar.activation(out=z_rows[g, half][:, t, :], in_=acc[:], func=ACT.Copy, scale=gain)
 
-        def z_narrow_mm(g, half, rb):
-            acc = bank()
-            banks["z", g, half, rb] = acc
-            for t in range(4):
-                for k in range(2):
-                    st = slice(k * P, (k + 1) * P)
-                    at = half * W512 + rb * P
-                    nc.tensor.matmul_mx(
-                        out=acc[:, t * P : (t + 1) * P],
-                        lhsT=e_q[4 * g + t][:, st].bitcast(FP8X4),
-                        lhsT_scale=e_s[4 * g + t][:, st],
-                        rhs=w_q[half][:, k, 2 * rb * P : 2 * (rb + 1) * P].bitcast(FP4X4),
-                        rhs_scale=w_s[:, k, at : at + P],
-                        start=(k == 0),
-                        stop=(k == 1),
-                    )
+        def z_wide_mm(t, half):
+            z_passes(bank("z wide", t, half)[:], 0, t, half * BANK, BANK)
 
-        def z_narrow_out(g, half, rb):
-            acc = banks["z", g, half, rb]
-            if (g, half) not in z_grp:
-                z_new = work.tile([P, W512, 4], BF16, name="z_grp", bufs=3, align_bytes=64)
-                z_grp[g, half] = z_new
-            nc.vector.tensor_tensor(
-                out=z_grp[g, half][:, rb * P : (rb + 1) * P, :],
-                in0=acc[:].rearrange("p (t n) -> p n t", t=4),
-                in1=taper_f[:, g, :].unsqueeze(1).to_broadcast([P, P, 4]),
-                op=ALU.mult,
+        def z_wide_out(t, half):
+            if half not in z_rows:
+                fresh = work.tile([P, 4, BANK], BF16, name="z_rows", bufs=2, align_bytes=64)
+                z_rows[half] = fresh
+            nc.scalar.activation(
+                out=z_rows[half][:, t, :], in_=bank("z wide", t, half)[:], func=ACT.Copy, scale=gain[:, 0, t : t + 1]
             )
 
-        def z_weave_gpsimd(g, half, into):
-            z_grp[g, half] = into
+        def z_wide(t, half):
+            z_wide_mm(t, half)
+            z_wide_out(t, half)
+
+        def z_weave(half, into):
+            z_woven[0, half] = into
             nc.gpsimd.tensor_scalar(
-                out=into[:],
-                in0=z_rows[g, half][:].rearrange("p t n -> p n t"),
+                out=into,
+                in0=z_rows[half][:].rearrange("p t n -> p n t"),
                 scalar1=1.0,
                 scalar2=0.0,
                 op0=ALU.mult,
                 op1=ALU.add,
             )
 
-        def z_quant(g, half):
-            quant(z_q[g][half], z_s[g][half], z_grp[g, half])
+        def z_narrow_mm(half, b, slots=range(4)):
+            for t in slots:
+                z_passes(bank("z narrow", half, b)[:, t * P : (t + 1) * P], 1, t, half * BANK + b * P, P)
 
-        def y_mm(s, at, width):
-            half, first = divmod(at, W512)
-            rc = slice(first, first + width)
+        def z_narrow_out(half, b):
+            if (1, half) not in z_woven:
+                fresh = work.tile([P, BANK, 4], BF16, name="z_woven", bufs=2, align_bytes=64)
+                z_woven[1, half] = fresh[:]
+            nc.vector.tensor_tensor(
+                out=z_woven[1, half][:, b * P : (b + 1) * P, :],
+                in0=bank("z narrow", half, b)[:].rearrange("p (t n) -> p n t", t=4),
+                in1=gain[:, 1, :].unsqueeze(1).to_broadcast([P, P, 4]),
+                op=ALU.mult,
+            )
+
+        def z_quantise(g, half):
+            quantise(z_q[g][half][:], z_s[g][half][:], z_woven[g, half])
+
+        def y_unit(s, first, width):
+            half, at = divmod(first, BANK)
+            cols = slice(at, at + width)
             for part in range(2):
-                b = bank()
+                acc = bank("y", s, first, part)
                 for g in range(2):
-                    cols = slice((2 * g + part) * P, (2 * g + part + 1) * P)
+                    bins = slice((2 * g + part) * P, (2 * g + part + 1) * P)
                     nc.tensor.matmul_mx(
-                        out=b[:, 0:width],
-                        lhsT=f_q[s][:, cols].bitcast(FP8X4),
-                        lhsT_scale=f_s[s][:, cols],
-                        rhs=z_q[g][half][:, rc].bitcast(FP8X4),
-                        rhs_scale=z_s[g][half][:, rc],
+                        out=acc[:, 0:width],
+                        lhsT=f_q[s][:, bins].bitcast(FP8X4),
+                        lhsT_scale=f_s[s][:, bins],
+                        rhs=z_q[g][half][:, cols].bitcast(FP8X4),
+                        rhs_scale=z_s[g][half][:, cols],
                         start=(g == 0),
                         stop=(g == 1),
                     )
-                sq = outs.tile([P, W512], F32, name="sq%d" % part, bufs=6, align_bytes=64)
-                nc.scalar.activation(out=sq[:, 0:width], in_=b[:, 0:width], func=ACT.Square)
-                squares[s, at, part] = sq
+                square = outs.tile([P, BANK], F32, name="square%d" % part, align_bytes=64)
+                nc.scalar.activation(out=square[:, 0:width], in_=acc[:, 0:width], func=ACT.Square)
+                squares[s, first, part] = square
 
-        def y_sum(s, at, width, eng="v"):
+        def y_sum(s, first, width):
             rows = out.rearrange("(c p j) r -> c j p r", p=P, j=2)[s // 2, s % 2]
-            res = outs.tile([P, W512], F32, name="res", bufs=6, align_bytes=64)
-            (nc.vector if eng == "v" else nc.gpsimd).tensor_tensor(
-                out=res[:, 0:width],
-                in0=squares[s, at, 0][:, 0:width],
-                in1=squares[s, at, 1][:, 0:width],
+            total = outs.tile([P, BANK], F32, name="total", align_bytes=64)
+            nc.vector.tensor_tensor(
+                out=total[:, 0:width],
+                in0=squares[s, first, 0][:, 0:width],
+                in1=squares[s, first, 1][:, 0:width],
                 op=ALU.add,
             )
-            nc.sync.dma_start(out=rows[:, at : at + width], in_=res[:, 0:width])
+            nc.sync.dma_start(out=rows[:, first : first + width], in_=total[:, 0:width])
 
         ctx.enter_context(tc.manual_schedule())
         make_identity(nc, ident[:])
         nc.vector.memset(w_s[:].bitcast(I32), 0)
-        for x in range(3):
-            load_e(x)
-        load_scale()
-        load_e(3)
-        load_ws()
-        load_w(0)
-        load_e(4)
-        load_taper()
+
+        for x in range(4):
+            load_echo(x)
+        nc.sync.dma_start(out=scale[:], in_=echo_scale.rearrange("o (g p t) -> p (o g) t", g=2, t=4))
+        load_echo(4)
         load_strip(0)
+        load_echo(5)
+        load_w(0)
+        load_w_scales()
+        nc.sync.dma_start(out=taper_bf[:], in_=taper.rearrange("(g p t) -> p g t", p=P, t=4))
         load_h(0)
-        load_w(1)
         load_strip(1)
+        load_w(1)
         load_pair(1)
         load_h(1)
         load_pair(2)
         load_pair(3)
-        e_wide(0)
-        e_wide(2, "s")
-        e_wide(1)
-        e_wide(3)
-        e_wide(4, "s")
-        e_wide(5, "s")
-        e_wide(6, "s")
-        e_wide(7, "s")
-        taper_widen()
-        for i in (0, 1, 2, 3, 4, 5):
-            e_turn(i)
-        e_out(0)
-        e_out(1)
-        e_quant(0)
-        e_out(2)
-        e_quant(1)
-        z_wide(0, 0, 0)
-        z_wide(0, 1, 0)
-        h_weave(0, "s", slice(0, P // 2))
-        e_out(3)
-        e_quant(2)
-        e_turn(6)
-        cs_part(0)
-        e_turn(7)
-        h_weave(0, "s", slice(P // 2, P))
-        e_out(4)
-        e_quant(3)
-        z_wide(0, 2, 0)
-        z_wide(0, 0, 1)
-        z_wide(0, 3, 0)
-        e_out(5)
-        e_quant(4)
-        z_wide(0, 1, 1)
-        cs_part(1)
-        e_out(6)
-        e_quant(5)
-        h_weave(1, "s", slice(P // 2, P))
-        cs_part(2)
-        cs_part(3)
-        e_out(7)
-        e_quant(6)
-        c_quant(0)
-        e_quant(7)
-        h_quant(0)
-        z_wide(0, 2, 1)
-        z_wide(0, 3, 1)
-        for rb in range(4):
-            z_narrow_mm(1, 0, rb)
-        h_weave(1, "v", slice(0, P // 2))
-        c_quant(1)
-        h_quant(1)
-        z_weave_gpsimd(0, 0, h_grp[1])
-        for rb in range(4):
-            z_narrow_out(1, 0, rb)
+
+        echo_widen(0, "vector", pieces=2)
+        echo_widen(1, "scalar")
+        echo_widen(2, "vector", pieces=2)
+        for i in (3, 5, 6, 7):
+            echo_widen(i, "scalar")
+        nc.scalar.activation(out=gain[:], in_=taper_bf[:], func=ACT.Copy)
+
+        echo_turn(0)
+        echo_turn(2)
+        echo_out(0)
+        echo_widen(4, "vector")
+        echo_turn(1)
+        cs_turn(0)
+        for i in range(3, 7):
+            echo_turn(i)
+        echo_out(2)
+        echo_quantise(0)
+        cs_out(0)
+        echo_out(1)
+        z_wide_mm(0, 0)
+        echo_out(3)
+        echo_quantise(1, 2)
+        echo_turn(7)
+        cs_turn(1)
+        echo_quantise(3)
+        h_weave(0, "scalar", slice(0, P // 2))
+        z_wide_out(0, 0)
+        cs_out(1)
+
+        z_wide(1, 0)
+        echo_out(4)
+        z_wide(2, 0)
+        z_wide(3, 0)
+        echo_out(5)
+        z_wide(0, 1)
+        echo_out(6)
+        z_wide(1, 1)
+        echo_quantise(4, 2)
+        echo_out(7)
+        z_wide_mm(2, 1)
+        z_wide_mm(3, 1)
+        cs_turn(2)
+        cs_turn(3)
+        h_weave(0, "scalar", slice(P // 2, P))
+        cs_out(2)
+        cs_out(3)
+        z_wide_out(2, 1)
+        z_wide_out(3, 1)
+        echo_quantise(6)
+        echo_quantise(7)
+        h_quantise(0)
+        cs_quantise(0)
+        h_weave(1, "vector")
+        cs_quantise(1)
+        h_quantise(1)
+
+        for slots in ((0, 1), (2, 3)):
+            for b in range(4):
+                z_narrow_mm(0, b, slots)
+        z_weave(0, cs_pair_woven(1))
+        cs_sort(4)
         for s in range(2):
             for part in range(2):
                 f_bank(s, 0, part)
+        z_narrow_out(0, 0)
+        z_narrow_out(0, 1)
+        z_narrow_mm(1, 0)
+        z_narrow_mm(1, 1)
+        cs_sort(5)
         for s in range(2):
+            z_narrow_out(0 if s == 0 else 1, 2 if s == 0 else 0)
             for part in range(2):
-                f_bank(s, 1, part, "v" if s + part == 0 else "s")
-        z_quant(1, 0)
-        z_quant(0, 0)
-        f_quant(0)
-        c_quant_pair(1)
-        f_quant(1)
-        z_weave_gpsimd(0, 1, f_grp[1])
-        for rb in range(4):
-            z_narrow_mm(1, 1, rb)
-            z_narrow_out(1, 1, rb)
+                f_bank(s, 1, part)
+            z_narrow_out(0 if s == 0 else 1, 3 if s == 0 else 1)
+        cs_sort(6)
+        cs_sort(7)
+        z_narrow_mm(1, 2)
+        z_narrow_mm(1, 3)
+        z_quantise(1, 0)
+        z_quantise(0, 0)
+        f_quantise(0)
+        f_quantise(1)
+        z_weave(1, f_woven[0][:])
+        z_narrow_out(1, 2)
+        z_narrow_out(1, 3)
+        for part in range(2):
+            f_bank(2, 0, part, "vector")
         for s in range(4, STRIPS):
-            c_sort(s)
+            cs_turn(s)
+            cs_out(s)
 
-        units = [(0, 0), (1, 0), (0, 1), (1, 1)] + [(s, half) for s in range(2, 8) for half in range(2)]
-        units = [(s, W512 * half, W512) for s, half in units]
-        units = units[:-1] + [(7, 512, 256), (7, 768, 256)]
-        for n, y in enumerate(units):
-            y_mm(*y)
-            if n == 1:
-                for s in range(4, STRIPS):
-                    cs_part(s, "v" if s == 4 else "s")
-                z_quant(1, 1)
-                z_quant(0, 1)
-                for g in range(2):
-                    for part in range(2):
-                        f_bank(2, g, part, "v")
-                c_quant_pair(2)
-                f_quant(2)
-            if n == 2:
-                c_quant_pair(3)
-            if n in (4, 6, 8, 10, 12):
-                f_quant(n // 2 + 1)
-            if 2 <= n < 12:
-                s, g = divmod(n + 4, 2)
-                f_bank(s, g, 0, "s")
-                f_bank(s, g, 1, "v")
-            if 2 <= n <= 7:
-                y_sum(*units[n - 2])
-            if n >= 7:
-                y_sum(*units[n - 1])
+        units = [(s, half) for half in range(2) for s in range(EARLY_STRIPS)]
+        units = units + [(s, half) for s in range(EARLY_STRIPS, STRIPS) for half in range(2)]
+        units = [(s, half * BANK, BANK) for s, half in units]
+        units = units[:-1] + [(STRIPS - 1, BANK + at, BANK // 2) for at in (0, BANK // 2)]
+
+        y_unit(*units[0])
+        f_bank(2, 1, 0, "vector")
+        f_bank(2, 1, 1)
+        y_unit(*units[1])
+        f_quantise(2)
+        z_quantise(1, 1)
+        z_quantise(0, 1)
+        cs_quantise(2)
+        for g in range(2):
+            for part in range(2):
+                f_bank(3, g, part, ("scalar", "vector")[g])
+        y_unit(*units[2])
+        cs_quantise(3)
+
+        later = [(s, g) for s in range(4, STRIPS) for g in range(2)]
+        summed = 0
+        for n in range(3, len(units)):
+            y_unit(*units[n])
+            step = n - 3
+            if step % 2 == 0 and step <= len(later):
+                f_quantise(3 + step // 2)
+            if step < len(later):
+                f_bank(*later[step], 0, "scalar")
+                f_bank(*later[step], 1, "vector")
+            lag = SUM_LAG if step < len(later) else 1
+            for unit in units[summed : n - lag + 1]:
+                y_sum(*unit)
+            summed = n - lag + 1
         y_sum(*units[-1])

@@ -22,6 +22,7 @@ STRIPS = D // P
 TILES = T // P
 ECHO_LOADS = ((0, 1), (1, 1), (2, 1), (3, 1), (4, 2), (6, 2))
 EARLY_STRIPS = 3
+FIRST_PAIRED = 6
 SUM_LAG = 2
 
 FLOPS = 2 * (2 * D * J * T + T * L * R + 2 * D * T * R)
@@ -65,6 +66,7 @@ def tile_isar_split_real_image_s11_kernel(
         e_wide = {}
         cs_sorted = {}
         f_woven = {}
+        f_pairs = {}
         z_woven = {}
         z_rows = {}
         banks = {}
@@ -116,6 +118,19 @@ def tile_isar_split_real_image_s11_kernel(
             ordered = work.tile([P, 2, 2, P], F32, name="cs_sorted", align_bytes=64)
             cs_sorted[s] = ordered
             nc.scalar.copy(out=ordered[:], in_=cs_raw[s].bitcast(F32).rearrange("p a (m u) -> p a u m", u=2))
+
+        def cs_sort_pair(c, into):
+            nc.gpsimd.tensor_scalar(
+                out=into.rearrange("p (u w) e -> p w u e", u=2),
+                in0=cs_pair[c - 1][:].rearrange("p a j (m u e) -> p (a j m) u e", u=2, e=2),
+                scalar1=1.0,
+                scalar2=0.0,
+                op0=ALU.mult,
+                op1=ALU.add,
+            )
+            words = into.rearrange("p w e -> p (w e)").bitcast(F32).rearrange("p (u a j m) -> p j a u m", u=2, a=2, j=2)
+            for j in range(2):
+                cs_sorted[2 * c + j] = words[:, j]
 
         def cs_turn(s):
             for part in range(2):
@@ -192,10 +207,37 @@ def tile_isar_split_real_image_s11_kernel(
                     stop=True,
                 )
             if s not in f_woven:
-                fresh = work.tile([P, BANK, 4], BF16, name="f_woven", bufs=5, align_bytes=64)
+                fresh = work.tile([P, BANK, 4], BF16, name="f_woven", bufs=4, align_bytes=64)
                 f_woven[s] = fresh
             at = (2 * g + part) * P
             copy(eng, f_woven[s][:, at : at + P, :], acc[:].rearrange("p (t n) -> p n t", t=4))
+
+        def f_pair_bank(s, g, u, eng):
+            acc = bank("f", s, g, u)
+            for e in range(2):
+                slot = slice((2 * u + e) * P, (2 * u + e + 1) * P)
+                nc.tensor.matmul_mx(
+                    out=acc[:, 2 * P * e : 2 * P * (e + 1)],
+                    lhsT=h_q[g][:, slot].bitcast(FP8X4),
+                    lhsT_scale=h_s[g][:, slot],
+                    rhs=cs_q[s // 2][:, s % 2].bitcast(FP8X4),
+                    rhs_scale=cs_s[s // 2][:, s % 2],
+                    start=True,
+                    stop=True,
+                )
+            if s not in f_pairs:
+                fresh = work.tile([P, 2, 2, 2 * P, 2], BF16, name="f_pairs", bufs=2, align_bytes=64)
+                f_pairs[s] = fresh
+            copy(eng, f_pairs[s][:, g, u], acc[:].rearrange("p (e n) -> p n e", e=2))
+
+        def f_join(s):
+            fresh = work.tile([P, BANK, 4], BF16, name="f_woven", bufs=4, align_bytes=64)
+            f_woven[s] = fresh
+            words = f_pairs[s][:].rearrange("p g u n e -> p (g u n e)").bitcast(F32)
+            nc.vector.tensor_copy(
+                out=fresh[:].rearrange("p n t -> p (n t)").bitcast(F32).rearrange("p (g n u) -> p g n u", g=2, u=2),
+                in_=words.rearrange("p (g u n) -> p g n u", g=2, u=2),
+            )
 
         def f_quantise(s):
             quantise(f_q[s][:], f_s[s][:], f_woven[s][:])
@@ -304,8 +346,8 @@ def tile_isar_split_real_image_s11_kernel(
         nc.sync.dma_start(out=taper_bf[:], in_=taper.rearrange("(g p t) -> p g t", p=P, t=4))
         load_h(0)
         load_strip(1)
-        load_w(1)
         load_pair(1)
+        load_w(1)
         load_h(1)
         load_pair(2)
         load_pair(3)
@@ -335,6 +377,7 @@ def tile_isar_split_real_image_s11_kernel(
         echo_turn(7)
         cs_turn(1)
         echo_quantise(3)
+        cs_sort_pair(1, e_woven[:, 2 * P : 6 * P, :].rearrange("p n (x e) -> p (n x) e", e=2))
         h_weave(0, "scalar", slice(0, P // 2))
         z_wide_out(0, 0)
         cs_out(1)
@@ -425,11 +468,18 @@ def tile_isar_split_real_image_s11_kernel(
         for n in range(3, len(units)):
             y_unit(*units[n])
             step = n - 3
-            if step % 2 == 0 and step <= len(later):
-                f_quantise(3 + step // 2)
+            done = 3 + step // 2 if step % 2 == 0 and step <= len(later) else None
+            if done is not None:
+                (f_quantise if done < FIRST_PAIRED else f_join)(done)
             if step < len(later):
-                f_bank(*later[step], 0, "scalar")
-                f_bank(*later[step], 1, "vector")
+                s, g = later[step]
+                for x, eng in enumerate(("scalar", "vector")):
+                    (f_bank if s < FIRST_PAIRED else f_pair_bank)(s, g, x, eng)
+            elif step == len(later):
+                y_sum(*units[summed])
+                summed = summed + 1
+            if done is not None and done >= FIRST_PAIRED:
+                f_quantise(done)
             lag = SUM_LAG if step < len(later) else 1
             for unit in units[summed : n - lag + 1]:
                 y_sum(*unit)

@@ -22,7 +22,7 @@ STRIPS = D // P
 TILES = T // P
 ECHO_LOADS = ((0, 1), (1, 1), (2, 1), (3, 1), (4, 2), (6, 2))
 EARLY_STRIPS = 3
-FIRST_PAIRED = 6
+PAIRED = (4,)
 SUM_LAG = 2
 
 FLOPS = 2 * (2 * D * J * T + T * L * R + 2 * D * T * R)
@@ -49,12 +49,13 @@ def tile_isar_split_real_image_s11_kernel(
         cs_q = [keep.tile([P, 2, 2 * P], U32, name="cs_q%d" % c, align_bytes=64) for c in range(4)]
         cs_s = [keep.tile([P, 2, 2 * P], U8, name="cs_s%d" % c, align_bytes=64) for c in range(4)]
         h_raw = [keep.tile([P, 4, BANK], BF16, name="h_raw%d" % g, align_bytes=64) for g in range(2)]
-        h_woven = [keep.tile([P, BANK, 4], BF16, name="h_woven%d" % g, align_bytes=64) for g in range(2)]
         h_q = [keep.tile([P, BANK], U32, name="h_q%d" % g, align_bytes=64) for g in range(2)]
         h_s = [keep.tile([P, BANK], U8, name="h_s%d" % g, align_bytes=64) for g in range(2)]
         e_bytes = [keep.tile([P, n, L], U8, name="e_bytes%d" % i, align_bytes=64) for i, n in ECHO_LOADS]
         e_in = [e_bytes[x][:, j, :] for x, (i, n) in enumerate(ECHO_LOADS) for j in range(n)]
         e_woven = keep.tile([P, TILES * 2 * P, 4], BF16, name="e_woven", align_bytes=64)
+        h_woven_last = keep.tile([P, BANK, 4], BF16, name="h_woven_last", align_bytes=64)
+        h_woven = [h_woven_last[:], e_woven[:, 2 * P : 6 * P, :]]
         e_q = keep.tile([P, TILES * 2 * P], U32, name="e_q", align_bytes=64)
         e_s = keep.tile([P, TILES * 2 * P], U8, name="e_s", align_bytes=64)
         w_q = [keep.tile([P, 2, R], U8, name="w_q%d" % half, align_bytes=64) for half in range(2)]
@@ -81,6 +82,8 @@ def tile_isar_split_real_image_s11_kernel(
         def copy(eng, dst, src):
             if eng == "vector":
                 nc.vector.tensor_copy(out=dst, in_=src)
+            elif eng == "gpsimd":
+                nc.gpsimd.tensor_scalar(out=dst, in0=src, scalar1=1.0, scalar2=0.0, op0=ALU.mult, op1=ALU.add)
             else:
                 nc.scalar.copy(out=dst, in_=src)
 
@@ -118,19 +121,6 @@ def tile_isar_split_real_image_s11_kernel(
             ordered = work.tile([P, 2, 2, P], F32, name="cs_sorted", align_bytes=64)
             cs_sorted[s] = ordered
             nc.scalar.copy(out=ordered[:], in_=cs_raw[s].bitcast(F32).rearrange("p a (m u) -> p a u m", u=2))
-
-        def cs_sort_pair(c, into):
-            nc.gpsimd.tensor_scalar(
-                out=into.rearrange("p (u w) e -> p w u e", u=2),
-                in0=cs_pair[c - 1][:].rearrange("p a j (m u e) -> p (a j m) u e", u=2, e=2),
-                scalar1=1.0,
-                scalar2=0.0,
-                op0=ALU.mult,
-                op1=ALU.add,
-            )
-            words = into.rearrange("p w e -> p (w e)").bitcast(F32).rearrange("p (u a j m) -> p j a u m", u=2, a=2, j=2)
-            for j in range(2):
-                cs_sorted[2 * c + j] = words[:, j]
 
         def cs_turn(s):
             for part in range(2):
@@ -346,15 +336,15 @@ def tile_isar_split_real_image_s11_kernel(
         nc.sync.dma_start(out=taper_bf[:], in_=taper.rearrange("(g p t) -> p g t", p=P, t=4))
         load_h(0)
         load_strip(1)
-        load_pair(1)
-        load_w(1)
         load_h(1)
+        load_w(1)
+        load_pair(1)
         load_pair(2)
         load_pair(3)
 
         echo_widen(0, "vector", pieces=2)
         echo_widen(1, "scalar")
-        echo_widen(2, "vector", pieces=2)
+        echo_widen(2, "vector")
         for i in (3, 5, 6, 7):
             echo_widen(i, "scalar")
         nc.scalar.activation(out=gain[:], in_=taper_bf[:], func=ACT.Copy)
@@ -377,7 +367,7 @@ def tile_isar_split_real_image_s11_kernel(
         echo_turn(7)
         cs_turn(1)
         echo_quantise(3)
-        cs_sort_pair(1, e_woven[:, 2 * P : 6 * P, :].rearrange("p n (x e) -> p (n x) e", e=2))
+        h_weave(1, "gpsimd", slice(0, 80))
         h_weave(0, "scalar", slice(0, P // 2))
         z_wide_out(0, 0)
         cs_out(1)
@@ -405,7 +395,7 @@ def tile_isar_split_real_image_s11_kernel(
         echo_quantise(7)
         h_quantise(0)
         cs_quantise(0)
-        h_weave(1, "vector")
+        h_weave(1, "vector", slice(80, P))
         cs_quantise(1)
         h_quantise(1)
 
@@ -451,7 +441,7 @@ def tile_isar_split_real_image_s11_kernel(
 
         y_unit(*units[0])
         f_bank(2, 1, 0, "vector")
-        f_bank(2, 1, 1)
+        f_bank(2, 1, 1, "vector")
         y_unit(*units[1])
         f_quantise(2)
         z_quantise(1, 1)
@@ -470,15 +460,13 @@ def tile_isar_split_real_image_s11_kernel(
             step = n - 3
             done = 3 + step // 2 if step % 2 == 0 and step <= len(later) else None
             if done is not None:
-                (f_quantise if done < FIRST_PAIRED else f_join)(done)
+                (f_join if done in PAIRED else f_quantise)(done)
             if step < len(later):
                 s, g = later[step]
-                for x, eng in enumerate(("scalar", "vector")):
-                    (f_bank if s < FIRST_PAIRED else f_pair_bank)(s, g, x, eng)
-            elif step == len(later):
-                y_sum(*units[summed])
-                summed = summed + 1
-            if done is not None and done >= FIRST_PAIRED:
+                first_engine = "vector" if step == len(later) - 1 else "scalar"
+                for x, eng in enumerate((first_engine, "vector")):
+                    (f_pair_bank if s in PAIRED else f_bank)(s, g, x, eng)
+            if done in PAIRED:
                 f_quantise(done)
             lag = SUM_LAG if step < len(later) else 1
             for unit in units[summed : n - lag + 1]:

@@ -22,8 +22,10 @@ STRIPS = D // P
 TILES = T // P
 ECHO_LOADS = ((0, 1), (1, 1), (2, 1), (3, 1), (4, 2), (6, 2))
 EARLY_STRIPS = 3
-PAIRED = (4,)
+PAIRED_STRIP = 4
 SUM_LAG = 2
+H_GPSIMD = 80
+LAST_PIECES = (256, 256, 256, 128, 128)
 
 FLOPS = 2 * (2 * D * J * T + T * L * R + 2 * D * T * R)
 
@@ -54,8 +56,8 @@ def tile_isar_split_real_image_s11_kernel(
         e_bytes = [keep.tile([P, n, L], U8, name="e_bytes%d" % i, align_bytes=64) for i, n in ECHO_LOADS]
         e_in = [e_bytes[x][:, j, :] for x, (i, n) in enumerate(ECHO_LOADS) for j in range(n)]
         e_woven = keep.tile([P, TILES * 2 * P, 4], BF16, name="e_woven", align_bytes=64)
-        h_woven_last = keep.tile([P, BANK, 4], BF16, name="h_woven_last", align_bytes=64)
-        h_woven = [h_woven_last[:], e_woven[:, 2 * P : 6 * P, :]]
+        h_woven_first = keep.tile([P, BANK, 4], BF16, name="h_woven_first", align_bytes=64)
+        h_woven = [h_woven_first[:], e_woven[:, 2 * P : 6 * P, :]]
         e_q = keep.tile([P, TILES * 2 * P], U32, name="e_q", align_bytes=64)
         e_s = keep.tile([P, TILES * 2 * P], U8, name="e_s", align_bytes=64)
         w_q = [keep.tile([P, 2, R], U8, name="w_q%d" % half, align_bytes=64) for half in range(2)]
@@ -263,14 +265,7 @@ def tile_isar_split_real_image_s11_kernel(
 
         def z_weave(half, into):
             z_woven[0, half] = into
-            nc.gpsimd.tensor_scalar(
-                out=into,
-                in0=z_rows[half][:].rearrange("p t n -> p n t"),
-                scalar1=1.0,
-                scalar2=0.0,
-                op0=ALU.mult,
-                op1=ALU.add,
-            )
+            copy("gpsimd", into, z_rows[half][:].rearrange("p t n -> p n t"))
 
         def z_narrow_mm(half, b, slots=range(4)):
             for t in slots:
@@ -306,13 +301,34 @@ def tile_isar_split_real_image_s11_kernel(
                         start=(g == 0),
                         stop=(g == 1),
                     )
-                square = outs.tile([P, BANK], F32, name="square%d" % part, align_bytes=64)
+                square = outs.tile([P, BANK], F32, name="square%d" % part, bufs=(8, 6)[part], align_bytes=64)
                 nc.scalar.activation(out=square[:, 0:width], in_=acc[:, 0:width], func=ACT.Square)
-                squares[s, first, part] = square
+                squares[s, first, part] = square[:]
+
+        def y_piece(s, first, width):
+            half, at = divmod(first, BANK)
+            cols = slice(at, at + width)
+            acc = bank("y", s, first)
+            for part in range(2):
+                for g in range(2):
+                    bins = slice((2 * g + part) * P, (2 * g + part + 1) * P)
+                    nc.tensor.matmul_mx(
+                        out=acc[:, part * width : (part + 1) * width],
+                        lhsT=f_q[s][:, bins].bitcast(FP8X4),
+                        lhsT_scale=f_s[s][:, bins],
+                        rhs=z_q[g][half][:, cols].bitcast(FP8X4),
+                        rhs_scale=z_s[g][half][:, cols],
+                        start=(g == 0),
+                        stop=(g == 1),
+                    )
+            square = outs.tile([P, BANK], F32, name="square0", bufs=8, align_bytes=64)
+            nc.scalar.activation(out=square[:, 0 : 2 * width], in_=acc[:, 0 : 2 * width], func=ACT.Square)
+            for part in range(2):
+                squares[s, first, part] = square[:, part * width : (part + 1) * width]
 
         def y_sum(s, first, width):
             rows = out.rearrange("(c p j) r -> c j p r", p=P, j=2)[s // 2, s % 2]
-            total = outs.tile([P, BANK], F32, name="total", align_bytes=64)
+            total = outs.tile([P, BANK], F32, name="total", bufs=8, align_bytes=64)
             nc.vector.tensor_tensor(
                 out=total[:, 0:width],
                 in0=squares[s, first, 0][:, 0:width],
@@ -367,7 +383,7 @@ def tile_isar_split_real_image_s11_kernel(
         echo_turn(7)
         cs_turn(1)
         echo_quantise(3)
-        h_weave(1, "gpsimd", slice(0, 80))
+        h_weave(1, "gpsimd", slice(0, H_GPSIMD))
         h_weave(0, "scalar", slice(0, P // 2))
         z_wide_out(0, 0)
         cs_out(1)
@@ -393,9 +409,9 @@ def tile_isar_split_real_image_s11_kernel(
         z_wide_out(3, 1)
         echo_quantise(6)
         echo_quantise(7)
-        h_quantise(0)
         cs_quantise(0)
-        h_weave(1, "vector", slice(80, P))
+        h_quantise(0)
+        h_weave(1, "vector", slice(H_GPSIMD, P))
         cs_quantise(1)
         h_quantise(1)
 
@@ -412,11 +428,11 @@ def tile_isar_split_real_image_s11_kernel(
         z_narrow_mm(1, 0)
         z_narrow_mm(1, 1)
         cs_sort(5)
-        for s in range(2):
-            z_narrow_out(0 if s == 0 else 1, 2 if s == 0 else 0)
+        for s, (half, b) in enumerate(((0, 2), (1, 0))):
+            z_narrow_out(half, b)
             for part in range(2):
                 f_bank(s, 1, part)
-            z_narrow_out(0 if s == 0 else 1, 3 if s == 0 else 1)
+            z_narrow_out(half, b + 1)
         cs_sort(6)
         cs_sort(7)
         z_narrow_mm(1, 2)
@@ -437,11 +453,11 @@ def tile_isar_split_real_image_s11_kernel(
         units = [(s, half) for half in range(2) for s in range(EARLY_STRIPS)]
         units = units + [(s, half) for s in range(EARLY_STRIPS, STRIPS) for half in range(2)]
         units = [(s, half * BANK, BANK) for s, half in units]
-        units = units[:-1] + [(STRIPS - 1, BANK + at, BANK // 2) for at in (0, BANK // 2)]
+        units = units[:-2] + [(STRIPS - 1, sum(LAST_PIECES[:x]), width) for x, width in enumerate(LAST_PIECES)]
 
         y_unit(*units[0])
-        f_bank(2, 1, 0, "vector")
-        f_bank(2, 1, 1, "vector")
+        for part in range(2):
+            f_bank(2, 1, part, "vector")
         y_unit(*units[1])
         f_quantise(2)
         z_quantise(1, 1)
@@ -456,17 +472,17 @@ def tile_isar_split_real_image_s11_kernel(
         later = [(s, g) for s in range(4, STRIPS) for g in range(2)]
         summed = 0
         for n in range(3, len(units)):
-            y_unit(*units[n])
+            (y_unit if units[n][2] == BANK else y_piece)(*units[n])
             step = n - 3
             done = 3 + step // 2 if step % 2 == 0 and step <= len(later) else None
             if done is not None:
-                (f_join if done in PAIRED else f_quantise)(done)
+                (f_join if done == PAIRED_STRIP else f_quantise)(done)
             if step < len(later):
                 s, g = later[step]
                 first_engine = "vector" if step == len(later) - 1 else "scalar"
                 for x, eng in enumerate((first_engine, "vector")):
-                    (f_pair_bank if s in PAIRED else f_bank)(s, g, x, eng)
-            if done in PAIRED:
+                    (f_pair_bank if s == PAIRED_STRIP else f_bank)(s, g, x, eng)
+            if done == PAIRED_STRIP:
                 f_quantise(done)
             lag = SUM_LAG if step < len(later) else 1
             for unit in units[summed : n - lag + 1]:

@@ -23,7 +23,7 @@ TILES = T // P
 ECHO_LOADS = ((0, 1), (1, 1), (2, 1), (3, 1), (4, 2), (6, 2))
 EARLY_STRIPS = 3
 PAIRED_STRIP = 4
-SUM_LAG = 2
+SUM_LAG = 1
 H_GPSIMD = 80
 LAST_PIECES = (256, 256, 256, 128, 128)
 

@@ -22,9 +22,10 @@ STRIPS = D // P
 TILES = T // P
 ECHO_LOADS = ((0, 1), (1, 1), (2, 1), (3, 1), (4, 2), (6, 2))
 EARLY_STRIPS = 3
-PAIRED_STRIP = 4
+PAIRED_SUMS = 8
 SUM_LAG = 1
 H_GPSIMD = 80
+H_SCALAR = 64
 LAST_PIECES = (256, 256, 256, 128, 128)
 
 FLOPS = 2 * (2 * D * J * T + T * L * R + 2 * D * T * R)
@@ -38,7 +39,7 @@ def tile_isar_split_real_image_s11_kernel(
         keep = ctx.enter_context(tc.tile_pool(name="keep", bufs=1))
         work = ctx.enter_context(tc.tile_pool(name="work", bufs=4))
         outs = ctx.enter_context(tc.tile_pool(name="outs", bufs=6))
-        psum = ctx.enter_context(tc.psum_pool(name="psum", bufs=8))
+        psum = ctx.enter_context(tc.psum_pool(name="psum", bufs=1))
 
         ident = keep.tile([P, P], F32, name="ident", align_bytes=64)
         scale = keep.tile([P, 2, 4], F32, name="scale")
@@ -47,38 +48,45 @@ def tile_isar_split_real_image_s11_kernel(
         cs_single = [keep.tile([P, 2, J], BF16, name="cs_single%d" % j, align_bytes=64) for j in range(2)]
         cs_pair = [keep.tile([P, 2, 2, J], BF16, name="cs_pair%d" % c, align_bytes=64) for c in range(1, 4)]
         cs_raw = [cs_single[0][:], cs_single[1][:]] + [cs_pair[c][:, :, j, :] for c in range(3) for j in range(2)]
-        cs_woven = [keep.tile([P, 2, 2 * P, 4], BF16, name="cs_woven%d" % c, align_bytes=64) for c in range(4)]
-        cs_q = [keep.tile([P, 2, 2 * P], U32, name="cs_q%d" % c, align_bytes=64) for c in range(4)]
-        cs_s = [keep.tile([P, 2, 2 * P], U8, name="cs_s%d" % c, align_bytes=64) for c in range(4)]
+        cs_woven = keep.tile([P, STRIPS * 2 * P, 4], BF16, name="cs_woven", align_bytes=64)
+        cs_q = keep.tile([P, STRIPS * 2 * P], U32, name="cs_q", align_bytes=64)
+        cs_s = keep.tile([P, STRIPS * 2 * P], U8, name="cs_s", align_bytes=64)
         h_raw = [keep.tile([P, 4, BANK], BF16, name="h_raw%d" % g, align_bytes=64) for g in range(2)]
         h_q = [keep.tile([P, BANK], U32, name="h_q%d" % g, align_bytes=64) for g in range(2)]
         h_s = [keep.tile([P, BANK], U8, name="h_s%d" % g, align_bytes=64) for g in range(2)]
         e_bytes = [keep.tile([P, n, L], U8, name="e_bytes%d" % i, align_bytes=64) for i, n in ECHO_LOADS]
         e_in = [e_bytes[x][:, j, :] for x, (i, n) in enumerate(ECHO_LOADS) for j in range(n)]
-        e_woven = keep.tile([P, TILES * 2 * P, 4], BF16, name="e_woven", align_bytes=64)
-        h_woven_first = keep.tile([P, BANK, 4], BF16, name="h_woven_first", align_bytes=64)
-        h_woven = [h_woven_first[:], e_woven[:, 2 * P : 6 * P, :]]
+        spare = BANK - (P - H_SCALAR)
+        woven = keep.tile([P, spare + TILES * 2 * P, 4], BF16, name="woven", align_bytes=64)
+        e_at = [spare + 2 * P * ((i - 1) % TILES) for i in range(TILES)]
+        h_woven = [woven[:, 0:BANK, :], woven[:, e_at[2] : e_at[4], :]]
         e_q = keep.tile([P, TILES * 2 * P], U32, name="e_q", align_bytes=64)
         e_s = keep.tile([P, TILES * 2 * P], U8, name="e_s", align_bytes=64)
         w_q = [keep.tile([P, 2, R], U8, name="w_q%d" % half, align_bytes=64) for half in range(2)]
         w_s = keep.tile([P, 2, R], U8, name="w_s", align_bytes=64)
         f_q = [keep.tile([P, BANK], U32, name="f_q%d" % s, align_bytes=64) for s in range(STRIPS)]
         f_s = [keep.tile([P, BANK], U8, name="f_s%d" % s, align_bytes=64) for s in range(STRIPS)]
-        z_q = [[keep.tile([P, BANK], U32, name="z_q%d%d" % (g, r), align_bytes=64) for r in range(2)] for g in range(2)]
-        z_s = [[keep.tile([P, BANK], U8, name="z_s%d%d" % (g, r), align_bytes=64) for r in range(2)] for g in range(2)]
+        z_second = keep.tile([P, R, 4], BF16, name="z_second", align_bytes=64)
+        z_woven = [cs_woven[:, 0:R, :], z_second[:]]
+        z_q = [keep.tile([P, R], U32, name="z_q%d" % half, align_bytes=64) for half in range(2)]
+        z_s = [keep.tile([P, R], U8, name="z_s%d" % half, align_bytes=64) for half in range(2)]
         e_wide = {}
         cs_sorted = {}
-        f_woven = {}
-        f_pairs = {}
-        z_woven = {}
+        f_woven = {0: z_second[:, BANK:R, :]}
         z_rows = {}
         banks = {}
         squares = {}
+        halves = {}
+        free_banks = [psum.tile([P, BANK], F32, name="bank%d" % b) for b in range(8)]
 
         def bank(*key):
             if key not in banks:
-                fresh = psum.tile([P, BANK], F32, name="bank")
-                banks[key] = fresh
+                banks[key] = free_banks[0]
+                free_banks.remove(banks[key])
+            return banks[key]
+
+        def emptied(*key):
+            free_banks.append(banks[key])
             return banks[key]
 
         def copy(eng, dst, src):
@@ -133,28 +141,25 @@ def tile_isar_split_real_image_s11_kernel(
                     nc.tensor.transpose(bank("cs", s)[:, at : at + P], src, ident[:])
 
         def cs_out(s):
-            dst = cs_woven[s // 2][:, s % 2].rearrange("p n t -> p (n t)").bitcast(F32)
+            dst = cs_woven[:, 2 * P * s : 2 * P * (s + 1), :].rearrange("p n t -> p (n t)").bitcast(F32)
             nc.scalar.copy(
                 out=dst.rearrange("p (a m u) -> p a m u", a=2, u=2),
-                in_=bank("cs", s)[:].rearrange("p (a u m) -> p a m u", a=2, u=2),
+                in_=emptied("cs", s)[:].rearrange("p (a u m) -> p a m u", a=2, u=2),
             )
 
-        def cs_pair_woven(c):
-            return cs_woven[c][:].rearrange("p j n t -> p (j n) t")
-
-        def cs_quantise(c):
-            flat = "p j n -> p (j n)"
-            quantise(cs_q[c][:].rearrange(flat), cs_s[c][:].rearrange(flat), cs_pair_woven(c))
+        def cs_quantise(s, count):
+            cols = slice(2 * P * s, 2 * P * (s + count))
+            quantise(cs_q[:, cols], cs_s[:, cols], cs_woven[:, cols, :])
 
         def h_weave(g, eng, ms=slice(0, P)):
             copy(
                 eng,
-                h_woven[g][:].rearrange("p (t m) j -> p m t j", t=4)[:, ms],
+                h_woven[g].rearrange("p (t m) j -> p m t j", t=4)[:, ms],
                 h_raw[g][:].rearrange("p j (m t) -> p m t j", t=4)[:, ms],
             )
 
         def h_quantise(g):
-            quantise(h_q[g][:], h_s[g][:], h_woven[g][:])
+            quantise(h_q[g][:], h_s[g][:], h_woven[g])
 
         def echo_widen(i, eng, pieces=1):
             wide = work.tile([P, L], BF16, name="e_wide", bufs=TILES, align_bytes=64)
@@ -172,67 +177,46 @@ def tile_isar_split_real_image_s11_kernel(
                     nc.tensor.transpose(bank("echo", i)[:, at : at + P], src, ident[:])
 
         def echo_out(i):
-            dst = e_woven[:, 2 * P * i : 2 * P * (i + 1), :]
+            dst = woven[:, e_at[i] : e_at[i] + 2 * P, :]
             nc.vector.tensor_tensor(
                 out=dst.rearrange("p (k m) (u e) -> p k m u e", k=2, u=2),
-                in0=bank("echo", i)[:].bitcast(BF16).rearrange("p (u k m e) -> p k m u e", u=2, k=2, e=2),
+                in0=emptied("echo", i)[:].bitcast(BF16).rearrange("p (u k m e) -> p k m u e", u=2, k=2, e=2),
                 in1=scale[:].rearrange("p k (u e) -> p k u e", u=2).unsqueeze(2).to_broadcast([P, 2, P, 2, 2]),
                 op=ALU.mult,
             )
 
         def echo_quantise(i, count=1):
             cols = slice(2 * P * i, 2 * P * (i + count))
-            quantise(e_q[:, cols], e_s[:, cols], e_woven[:, cols, :])
+            quantise(e_q[:, cols], e_s[:, cols], woven[:, e_at[i] : e_at[i] + 2 * P * count, :])
 
-        def f_bank(s, g, part, eng="scalar"):
+        def f_mm(s, g, part):
             acc = bank("f", s, g, part)
-            bins = slice(part * P, (part + 1) * P)
+            bins = slice((2 * s + part) * P, (2 * s + part + 1) * P)
             for t in range(4):
                 slot = slice(t * P, (t + 1) * P)
                 nc.tensor.matmul_mx(
                     out=acc[:, slot],
                     lhsT=h_q[g][:, slot].bitcast(FP8X4),
                     lhsT_scale=h_s[g][:, slot],
-                    rhs=cs_q[s // 2][:, s % 2, bins].bitcast(FP8X4),
-                    rhs_scale=cs_s[s // 2][:, s % 2, bins],
+                    rhs=cs_q[:, bins].bitcast(FP8X4),
+                    rhs_scale=cs_s[:, bins],
                     start=True,
                     stop=True,
                 )
+
+        def f_out(s, g, part, eng):
             if s not in f_woven:
-                fresh = work.tile([P, BANK, 4], BF16, name="f_woven", bufs=4, align_bytes=64)
-                f_woven[s] = fresh
+                fresh = work.tile([P, BANK, 4], BF16, name="f_woven", bufs=3, align_bytes=64)
+                f_woven[s] = fresh[:]
             at = (2 * g + part) * P
-            copy(eng, f_woven[s][:, at : at + P, :], acc[:].rearrange("p (t n) -> p n t", t=4))
+            copy(eng, f_woven[s][:, at : at + P, :], emptied("f", s, g, part)[:].rearrange("p (t n) -> p n t", t=4))
 
-        def f_pair_bank(s, g, u, eng):
-            acc = bank("f", s, g, u)
-            for e in range(2):
-                slot = slice((2 * u + e) * P, (2 * u + e + 1) * P)
-                nc.tensor.matmul_mx(
-                    out=acc[:, 2 * P * e : 2 * P * (e + 1)],
-                    lhsT=h_q[g][:, slot].bitcast(FP8X4),
-                    lhsT_scale=h_s[g][:, slot],
-                    rhs=cs_q[s // 2][:, s % 2].bitcast(FP8X4),
-                    rhs_scale=cs_s[s // 2][:, s % 2],
-                    start=True,
-                    stop=True,
-                )
-            if s not in f_pairs:
-                fresh = work.tile([P, 2, 2, 2 * P, 2], BF16, name="f_pairs", bufs=2, align_bytes=64)
-                f_pairs[s] = fresh
-            copy(eng, f_pairs[s][:, g, u], acc[:].rearrange("p (e n) -> p n e", e=2))
-
-        def f_join(s):
-            fresh = work.tile([P, BANK, 4], BF16, name="f_woven", bufs=4, align_bytes=64)
-            f_woven[s] = fresh
-            words = f_pairs[s][:].rearrange("p g u n e -> p (g u n e)").bitcast(F32)
-            nc.vector.tensor_copy(
-                out=fresh[:].rearrange("p n t -> p (n t)").bitcast(F32).rearrange("p (g n u) -> p g n u", g=2, u=2),
-                in_=words.rearrange("p (g u n) -> p g n u", g=2, u=2),
-            )
+        def f_bank(s, g, part, eng="scalar"):
+            f_mm(s, g, part)
+            f_out(s, g, part, eng)
 
         def f_quantise(s):
-            quantise(f_q[s][:], f_s[s][:], f_woven[s][:])
+            quantise(f_q[s][:], f_s[s][:], f_woven[s])
 
         def z_passes(acc, g, t, first, width):
             half, at = divmod(first, BANK)
@@ -256,93 +240,108 @@ def tile_isar_split_real_image_s11_kernel(
                 fresh = work.tile([P, 4, BANK], BF16, name="z_rows", bufs=2, align_bytes=64)
                 z_rows[half] = fresh
             nc.scalar.activation(
-                out=z_rows[half][:, t, :], in_=bank("z wide", t, half)[:], func=ACT.Copy, scale=gain[:, 0, t : t + 1]
+                out=z_rows[half][:, t, :], in_=emptied("z wide", t, half)[:], func=ACT.Copy, scale=gain[:, 0, t : t + 1]
             )
 
         def z_wide(t, half):
             z_wide_mm(t, half)
             z_wide_out(t, half)
 
-        def z_weave(half, into):
-            z_woven[0, half] = into
-            copy("gpsimd", into, z_rows[half][:].rearrange("p t n -> p n t"))
+        def z_weave(half):
+            copy("gpsimd", z_woven[half][:, BANK:R, :], z_rows[half][:].rearrange("p t n -> p n t"))
 
         def z_narrow_mm(half, b, slots=range(4)):
             for t in slots:
                 z_passes(bank("z narrow", half, b)[:, t * P : (t + 1) * P], 1, t, half * BANK + b * P, P)
 
         def z_narrow_out(half, b):
-            if (1, half) not in z_woven:
-                fresh = work.tile([P, BANK, 4], BF16, name="z_woven", bufs=2, align_bytes=64)
-                z_woven[1, half] = fresh[:]
             nc.vector.tensor_tensor(
-                out=z_woven[1, half][:, b * P : (b + 1) * P, :],
-                in0=bank("z narrow", half, b)[:].rearrange("p (t n) -> p n t", t=4),
+                out=z_woven[half][:, b * P : (b + 1) * P, :],
+                in0=emptied("z narrow", half, b)[:].rearrange("p (t n) -> p n t", t=4),
                 in1=gain[:, 1, :].unsqueeze(1).to_broadcast([P, P, 4]),
                 op=ALU.mult,
             )
 
-        def z_quantise(g, half):
-            quantise(z_q[g][half][:], z_s[g][half][:], z_woven[g, half])
+        def z_quantise(half):
+            quantise(z_q[half][:], z_s[half][:], z_woven[half])
 
-        def y_unit(s, first, width):
+        units = [(s, half) for half in range(2) for s in range(EARLY_STRIPS)]
+        units = units + [(s, half) for s in range(EARLY_STRIPS, STRIPS) for half in range(2)]
+        units = [(s, half * BANK, BANK) for s, half in units]
+        units = units[:-2] + [(STRIPS - 1, sum(LAST_PIECES[:x]), width) for x, width in enumerate(LAST_PIECES)]
+
+        def shared(name, n, bufs):
+            if (name, n // 2) not in halves:
+                fresh = outs.tile([P, R], F32, name=name, bufs=bufs, align_bytes=64)
+                halves[name, n // 2] = fresh
+            return halves[name, n // 2][:, (n % 2) * BANK :]
+
+        def y_unit(n):
+            s, first, width = units[n]
             half, at = divmod(first, BANK)
-            cols = slice(at, at + width)
             for part in range(2):
                 acc = bank("y", s, first, part)
                 for g in range(2):
                     bins = slice((2 * g + part) * P, (2 * g + part + 1) * P)
+                    cols = slice((1 - g) * BANK + at, (1 - g) * BANK + at + width)
                     nc.tensor.matmul_mx(
                         out=acc[:, 0:width],
                         lhsT=f_q[s][:, bins].bitcast(FP8X4),
                         lhsT_scale=f_s[s][:, bins],
-                        rhs=z_q[g][half][:, cols].bitcast(FP8X4),
-                        rhs_scale=z_s[g][half][:, cols],
+                        rhs=z_q[half][:, cols].bitcast(FP8X4),
+                        rhs_scale=z_s[half][:, cols],
                         start=(g == 0),
                         stop=(g == 1),
                     )
-                square = outs.tile([P, BANK], F32, name="square%d" % part, bufs=(8, 6)[part], align_bytes=64)
-                nc.scalar.activation(out=square[:, 0:width], in_=acc[:, 0:width], func=ACT.Square)
-                squares[s, first, part] = square[:]
+                square = shared("square%d" % part, n, (4, 3)[part])
+                nc.scalar.activation(
+                    out=square[:, 0:width], in_=emptied("y", s, first, part)[:, 0:width], func=ACT.Square
+                )
+                squares[n, part] = square
 
-        def y_piece(s, first, width):
+        def y_piece(n):
+            s, first, width = units[n]
             half, at = divmod(first, BANK)
-            cols = slice(at, at + width)
             acc = bank("y", s, first)
             for part in range(2):
                 for g in range(2):
                     bins = slice((2 * g + part) * P, (2 * g + part + 1) * P)
+                    cols = slice((1 - g) * BANK + at, (1 - g) * BANK + at + width)
                     nc.tensor.matmul_mx(
                         out=acc[:, part * width : (part + 1) * width],
                         lhsT=f_q[s][:, bins].bitcast(FP8X4),
                         lhsT_scale=f_s[s][:, bins],
-                        rhs=z_q[g][half][:, cols].bitcast(FP8X4),
-                        rhs_scale=z_s[g][half][:, cols],
+                        rhs=z_q[half][:, cols].bitcast(FP8X4),
+                        rhs_scale=z_s[half][:, cols],
                         start=(g == 0),
                         stop=(g == 1),
                     )
-            square = outs.tile([P, BANK], F32, name="square0", bufs=8, align_bytes=64)
-            nc.scalar.activation(out=square[:, 0 : 2 * width], in_=acc[:, 0 : 2 * width], func=ACT.Square)
-            for part in range(2):
-                squares[s, first, part] = square[:, part * width : (part + 1) * width]
-
-        def y_sum(s, first, width):
-            rows = out.rearrange("(c p j) r -> c j p r", p=P, j=2)[s // 2, s % 2]
-            total = outs.tile([P, BANK], F32, name="total", bufs=8, align_bytes=64)
-            nc.vector.tensor_tensor(
-                out=total[:, 0:width],
-                in0=squares[s, first, 0][:, 0:width],
-                in1=squares[s, first, 1][:, 0:width],
-                op=ALU.add,
+            square = shared("square0", n, 4)
+            nc.scalar.activation(
+                out=square[:, 0 : 2 * width], in_=emptied("y", s, first)[:, 0 : 2 * width], func=ACT.Square
             )
-            nc.sync.dma_start(out=rows[:, first : first + width], in_=total[:, 0:width])
+            for part in range(2):
+                squares[n, part] = square[:, part * width :]
+
+        def y_sum(n, count):
+            total = shared("total", n, 4)
+            both = count * units[n][2]
+            nc.vector.tensor_tensor(
+                out=total[:, 0:both], in0=squares[n, 0][:, 0:both], in1=squares[n, 1][:, 0:both], op=ALU.add
+            )
+            for x in range(count):
+                s, first, width = units[n + x]
+                rows = out.rearrange("(c p j) r -> c j p r", p=P, j=2)[s // 2, s % 2]
+                nc.sync.dma_start(out=rows[:, first : first + width], in_=total[:, x * width : (x + 1) * width])
 
         ctx.enter_context(tc.manual_schedule())
         make_identity(nc, ident[:])
         nc.vector.memset(w_s[:].bitcast(I32), 0)
 
-        for x in range(4):
-            load_echo(x)
+        load_echo(0)
+        load_echo(1)
+        load_echo(2)
+        load_echo(3)
         nc.sync.dma_start(out=scale[:], in_=echo_scale.rearrange("o (g p t) -> p (o g) t", g=2, t=4))
         load_echo(4)
         load_strip(0)
@@ -383,42 +382,41 @@ def tile_isar_split_real_image_s11_kernel(
         echo_turn(7)
         cs_turn(1)
         echo_quantise(3)
+        h_weave(0, "gpsimd", slice(H_SCALAR, P))
         h_weave(1, "gpsimd", slice(0, H_GPSIMD))
-        h_weave(0, "scalar", slice(0, P // 2))
+        h_weave(0, "scalar", slice(0, H_SCALAR))
         z_wide_out(0, 0)
         cs_out(1)
 
-        z_wide(1, 0)
         echo_out(4)
+        z_wide(1, 0)
+        echo_out(5)
         z_wide(2, 0)
         z_wide(3, 0)
-        echo_out(5)
-        z_wide(0, 1)
         echo_out(6)
+        z_wide(0, 1)
         z_wide(1, 1)
-        echo_quantise(4, 2)
-        echo_out(7)
         z_wide_mm(2, 1)
         z_wide_mm(3, 1)
         cs_turn(2)
         cs_turn(3)
-        h_weave(0, "scalar", slice(P // 2, P))
+        echo_out(7)
+        h_weave(1, "scalar", slice(H_GPSIMD, P))
+        z_wide_out(2, 1)
         cs_out(2)
         cs_out(3)
-        z_wide_out(2, 1)
         z_wide_out(3, 1)
-        echo_quantise(6)
-        echo_quantise(7)
-        cs_quantise(0)
+        echo_quantise(4, 2)
         h_quantise(0)
-        h_weave(1, "vector", slice(H_GPSIMD, P))
-        cs_quantise(1)
+        echo_quantise(6, 2)
+        cs_quantise(0, 2)
+        cs_quantise(2, 2)
         h_quantise(1)
 
         for slots in ((0, 1), (2, 3)):
             for b in range(4):
                 z_narrow_mm(0, b, slots)
-        z_weave(0, cs_pair_woven(1))
+        z_weave(0)
         cs_sort(4)
         for s in range(2):
             for part in range(2):
@@ -437,11 +435,10 @@ def tile_isar_split_real_image_s11_kernel(
         cs_sort(7)
         z_narrow_mm(1, 2)
         z_narrow_mm(1, 3)
-        z_quantise(1, 0)
-        z_quantise(0, 0)
+        z_quantise(0)
         f_quantise(0)
         f_quantise(1)
-        z_weave(1, f_woven[0][:])
+        z_weave(1)
         z_narrow_out(1, 2)
         z_narrow_out(1, 3)
         for part in range(2):
@@ -450,42 +447,36 @@ def tile_isar_split_real_image_s11_kernel(
             cs_turn(s)
             cs_out(s)
 
-        units = [(s, half) for half in range(2) for s in range(EARLY_STRIPS)]
-        units = units + [(s, half) for s in range(EARLY_STRIPS, STRIPS) for half in range(2)]
-        units = [(s, half * BANK, BANK) for s, half in units]
-        units = units[:-2] + [(STRIPS - 1, sum(LAST_PIECES[:x]), width) for x, width in enumerate(LAST_PIECES)]
-
-        y_unit(*units[0])
+        y_unit(0)
         for part in range(2):
             f_bank(2, 1, part, "vector")
-        y_unit(*units[1])
+        y_unit(1)
         f_quantise(2)
-        z_quantise(1, 1)
-        z_quantise(0, 1)
-        cs_quantise(2)
+        z_quantise(1)
+        cs_quantise(4, 2)
         for g in range(2):
             for part in range(2):
                 f_bank(3, g, part, ("scalar", "vector")[g])
-        y_unit(*units[2])
-        cs_quantise(3)
+        y_unit(2)
+        cs_quantise(6, 2)
 
         later = [(s, g) for s in range(4, STRIPS) for g in range(2)]
         summed = 0
         for n in range(3, len(units)):
-            (y_unit if units[n][2] == BANK else y_piece)(*units[n])
+            (y_unit if units[n][2] == BANK else y_piece)(n)
             step = n - 3
             done = 3 + step // 2 if step % 2 == 0 and step <= len(later) else None
             if done is not None:
-                (f_join if done == PAIRED_STRIP else f_quantise)(done)
+                f_quantise(done)
             if step < len(later):
                 s, g = later[step]
                 first_engine = "vector" if step == len(later) - 1 else "scalar"
                 for x, eng in enumerate((first_engine, "vector")):
-                    (f_pair_bank if s == PAIRED_STRIP else f_bank)(s, g, x, eng)
-            if done == PAIRED_STRIP:
-                f_quantise(done)
+                    f_bank(s, g, x, eng)
             lag = SUM_LAG if step < len(later) else 1
-            for unit in units[summed : n - lag + 1]:
-                y_sum(*unit)
-            summed = n - lag + 1
-        y_sum(*units[-1])
+            count = 2 if summed < PAIRED_SUMS else 1
+            while summed + count - 1 <= n - lag:
+                y_sum(summed, count)
+                summed = summed + count
+                count = 2 if summed < PAIRED_SUMS else 1
+        y_sum(len(units) - 1, 1)

@@ -46,9 +46,12 @@ def tile_isar_split_real_image_s11_kernel(
         taper_bf = keep.tile([P, 2, 4], BF16, name="taper_bf")
         gain = keep.tile([P, 2, 4], F32, name="gain")
         cs_single = [keep.tile([P, 2, J], BF16, name="cs_single%d" % j, align_bytes=64) for j in range(2)]
-        cs_pair = [keep.tile([P, 2, 2, J], BF16, name="cs_pair%d" % c, align_bytes=64) for c in range(1, 4)]
-        cs_raw = [cs_single[0][:], cs_single[1][:]] + [cs_pair[c][:, :, j, :] for c in range(3) for j in range(2)]
-        cs_woven = keep.tile([P, STRIPS * 2 * P, 4], BF16, name="cs_woven", align_bytes=64)
+        cs_pair = [keep.tile([P, 2, 2, J], BF16, name="cs_pair%d" % c, align_bytes=64) for c in range(1, 3)]
+        cs_raw = [cs_single[0][:], cs_single[1][:]] + [cs_pair[c][:, :, j, :] for c in range(2) for j in range(2)]
+        cs_quarters = keep.tile([P, 2, 8, P], BF16, name="cs_quarters", align_bytes=64)
+        z_woven = [keep.tile([P, R, 4], BF16, name="z_woven%d" % half, align_bytes=64) for half in range(2)]
+        cs_late = keep.tile([P, R, 4], BF16, name="cs_late", align_bytes=64)
+        cs_woven = [z_woven[0][:, BANK:R], z_woven[1][:, BANK:R], cs_late[:, 0:BANK], cs_late[:, BANK:R]]
         cs_q = keep.tile([P, STRIPS * 2 * P], U32, name="cs_q", align_bytes=64)
         cs_s = keep.tile([P, STRIPS * 2 * P], U8, name="cs_s", align_bytes=64)
         h_raw = [keep.tile([P, 4, BANK], BF16, name="h_raw%d" % g, align_bytes=64) for g in range(2)]
@@ -66,13 +69,12 @@ def tile_isar_split_real_image_s11_kernel(
         w_s = keep.tile([P, 2, R], U8, name="w_s", align_bytes=64)
         f_q = [keep.tile([P, BANK], U32, name="f_q%d" % s, align_bytes=64) for s in range(STRIPS)]
         f_s = [keep.tile([P, BANK], U8, name="f_s%d" % s, align_bytes=64) for s in range(STRIPS)]
-        z_second = keep.tile([P, R, 4], BF16, name="z_second", align_bytes=64)
-        z_woven = [cs_woven[:, 0:R, :], z_second[:]]
         z_q = [keep.tile([P, R], U32, name="z_q%d" % half, align_bytes=64) for half in range(2)]
         z_s = [keep.tile([P, R], U8, name="z_s%d" % half, align_bytes=64) for half in range(2)]
         e_wide = {}
         cs_sorted = {}
-        f_woven = {0: z_second[:, BANK:R, :]}
+        cs_turned = {}
+        f_woven = {}
         z_rows = {}
         banks = {}
         squares = {}
@@ -114,6 +116,12 @@ def tile_isar_split_real_image_s11_kernel(
             rows = cs.rearrange("(a c p j) k -> c p a (j k)", a=2, p=P, j=2)
             nc.sync.dma_start(out=cs_pair[c - 1][:].rearrange("p a j k -> p a (j k)"), in_=rows[c])
 
+        def load_quarters():
+            for part in range(2):
+                rows = cs[part * D + 6 * P : (part + 1) * D, :].rearrange("(c b) (q k) -> q b c k", b=32, q=4)
+                for q in (0, 2, 1, 3):
+                    nc.sync.dma_start(out=cs_quarters[32 * q : 32 * (q + 1), part], in_=rows[q])
+
         def load_h(g):
             rows = h.rearrange("(p j) w -> p j w", j=4)
             nc.sync.dma_start(out=h_raw[g][:], in_=rows[:, :, g * BANK : (g + 1) * BANK])
@@ -128,7 +136,7 @@ def tile_isar_split_real_image_s11_kernel(
                 nc.sync.dma_start(out=w_s[32 * q : 32 * q + 4, :, :].bitcast(I32), in_=rows.rearrange("g q n -> q g n"))
 
         def cs_sort(s):
-            ordered = work.tile([P, 2, 2, P], F32, name="cs_sorted", align_bytes=64)
+            ordered = work.tile([P, 2, 2, P], F32, name="cs_sorted", bufs=2, align_bytes=64)
             cs_sorted[s] = ordered
             nc.scalar.copy(out=ordered[:], in_=cs_raw[s].bitcast(F32).rearrange("p a (m u) -> p a u m", u=2))
 
@@ -140,16 +148,35 @@ def tile_isar_split_real_image_s11_kernel(
                     at = (2 * part + u) * P
                     nc.tensor.transpose(bank("cs", s)[:, at : at + P], src, ident[:])
 
-        def cs_out(s):
-            dst = cs_woven[:, 2 * P * s : 2 * P * (s + 1), :].rearrange("p n t -> p (n t)").bitcast(F32)
-            nc.scalar.copy(
-                out=dst.rearrange("p (a m u) -> p a m u", a=2, u=2),
-                in_=emptied("cs", s)[:].rearrange("p (a u m) -> p a m u", a=2, u=2),
+        def cs_out(s, eng="scalar"):
+            dst = cs_woven[s // 2][:, 2 * P * (s % 2) : 2 * P * (s % 2 + 1), :].rearrange("p n t -> p (n t)").bitcast(F32)
+            copy(
+                eng,
+                dst.rearrange("p (a m u) -> p a m u", a=2, u=2),
+                emptied("cs", s)[:].rearrange("p (a u m) -> p a m u", a=2, u=2),
             )
 
-        def cs_quantise(s, count):
-            cols = slice(2 * P * s, 2 * P * (s + count))
-            quantise(cs_q[:, cols], cs_s[:, cols], cs_woven[:, cols, :])
+        def cs_sort_quarters(s):
+            ordered = work.tile([P, 2, 4, 2, 32], F32, name="quarters_sorted", bufs=2, align_bytes=64)
+            cs_sorted[s] = ordered
+            words = cs_quarters[:, :, 4 * (s - 6) : 4 * (s - 5), :].bitcast(F32)
+            nc.scalar.copy(out=ordered[:], in_=words.rearrange("p a c (w u) -> p a c u w", u=2))
+
+        def cs_blocks(s):
+            turned = work.tile([P, BANK], F32, name="cs_turned", bufs=2, align_bytes=64)
+            cs_turned[s] = turned
+            nc.vector.transpose(out=turned[:], in_=cs_sorted[s][:].rearrange("p a c u w -> p (a c u w)"))
+
+        def cs_join(s):
+            dst = cs_woven[3][:, 2 * P * (s - 6) : 2 * P * (s - 5), :].rearrange("p n t -> p (n t)").bitcast(F32)
+            nc.vector.tensor_copy(
+                out=dst.rearrange("p (c b u) -> p c b u", b=32, u=2),
+                in_=cs_turned[s][:].rearrange("p (c u b) -> p c b u", u=2, b=32),
+            )
+
+        def cs_quantise(c):
+            cols = slice(c * BANK, (c + 1) * BANK)
+            quantise(cs_q[:, cols], cs_s[:, cols], cs_woven[c])
 
         def h_weave(g, eng, ms=slice(0, P)):
             copy(
@@ -206,7 +233,7 @@ def tile_isar_split_real_image_s11_kernel(
 
         def f_out(s, g, part, eng):
             if s not in f_woven:
-                fresh = work.tile([P, BANK, 4], BF16, name="f_woven", bufs=3, align_bytes=64)
+                fresh = work.tile([P, BANK, 4], BF16, name="f_woven", bufs=4, align_bytes=64)
                 f_woven[s] = fresh[:]
             at = (2 * g + part) * P
             copy(eng, f_woven[s][:, at : at + P, :], emptied("f", s, g, part)[:].rearrange("p (t n) -> p n t", t=4))
@@ -263,7 +290,7 @@ def tile_isar_split_real_image_s11_kernel(
             )
 
         def z_quantise(half):
-            quantise(z_q[half][:], z_s[half][:], z_woven[half])
+            quantise(z_q[half][:], z_s[half][:], z_woven[half][:])
 
         units = [(s, half) for half in range(2) for s in range(EARLY_STRIPS)]
         units = units + [(s, half) for s in range(EARLY_STRIPS, STRIPS) for half in range(2)]
@@ -331,7 +358,10 @@ def tile_isar_split_real_image_s11_kernel(
             )
             for x in range(count):
                 s, first, width = units[n + x]
-                rows = out.rearrange("(c p j) r -> c j p r", p=P, j=2)[s // 2, s % 2]
+                if s < 6:
+                    rows = out.rearrange("(c p j) r -> c j p r", p=P, j=2)[s // 2, s % 2]
+                else:
+                    rows = out[s * P : (s + 1) * P, :]
                 nc.sync.dma_start(out=rows[:, first : first + width], in_=total[:, x * width : (x + 1) * width])
 
         ctx.enter_context(tc.manual_schedule())
@@ -345,9 +375,9 @@ def tile_isar_split_real_image_s11_kernel(
         nc.sync.dma_start(out=scale[:], in_=echo_scale.rearrange("o (g p t) -> p (o g) t", g=2, t=4))
         load_echo(4)
         load_strip(0)
-        load_echo(5)
         load_w(0)
         load_w_scales()
+        load_echo(5)
         nc.sync.dma_start(out=taper_bf[:], in_=taper.rearrange("(g p t) -> p g t", p=P, t=4))
         load_h(0)
         load_strip(1)
@@ -355,7 +385,7 @@ def tile_isar_split_real_image_s11_kernel(
         load_w(1)
         load_pair(1)
         load_pair(2)
-        load_pair(3)
+        load_quarters()
 
         echo_widen(0, "vector", pieces=2)
         echo_widen(1, "scalar")
@@ -370,7 +400,7 @@ def tile_isar_split_real_image_s11_kernel(
         echo_widen(4, "vector")
         echo_turn(1)
         cs_turn(0)
-        for i in range(3, 7):
+        for i in range(3, 6):
             echo_turn(i)
         echo_out(2)
         echo_quantise(0)
@@ -379,6 +409,7 @@ def tile_isar_split_real_image_s11_kernel(
         z_wide_mm(0, 0)
         echo_out(3)
         echo_quantise(1, 2)
+        echo_turn(6)
         echo_turn(7)
         cs_turn(1)
         echo_quantise(3)
@@ -409,8 +440,7 @@ def tile_isar_split_real_image_s11_kernel(
         echo_quantise(4, 2)
         h_quantise(0)
         echo_quantise(6, 2)
-        cs_quantise(0, 2)
-        cs_quantise(2, 2)
+        cs_quantise(0)
         h_quantise(1)
 
         for slots in ((0, 1), (2, 3)):
@@ -418,47 +448,51 @@ def tile_isar_split_real_image_s11_kernel(
                 z_narrow_mm(0, b, slots)
         z_weave(0)
         cs_sort(4)
+        cs_sort(5)
         for s in range(2):
             for part in range(2):
-                f_bank(s, 0, part)
-        z_narrow_out(0, 0)
-        z_narrow_out(0, 1)
+                f_mm(s, 0, part)
+        for b in range(4):
+            z_narrow_out(0, b)
         z_narrow_mm(1, 0)
-        z_narrow_mm(1, 1)
-        cs_sort(5)
-        for s, (half, b) in enumerate(((0, 2), (1, 0))):
-            z_narrow_out(half, b)
+        for s in range(2):
+            for part in range(2):
+                f_out(s, 0, part, "scalar")
+        z_narrow_out(1, 0)
+        for s in range(2):
             for part in range(2):
                 f_bank(s, 1, part)
-            z_narrow_out(half, b + 1)
-        cs_sort(6)
-        cs_sort(7)
-        z_narrow_mm(1, 2)
-        z_narrow_mm(1, 3)
+        cs_sort_quarters(6)
+        cs_sort_quarters(7)
+        for b in range(1, 4):
+            z_narrow_mm(1, b)
         z_quantise(0)
         f_quantise(0)
+        cs_quantise(1)
         f_quantise(1)
         z_weave(1)
-        z_narrow_out(1, 2)
-        z_narrow_out(1, 3)
-        for part in range(2):
-            f_bank(2, 0, part, "vector")
-        for s in range(4, STRIPS):
-            cs_turn(s)
-            cs_out(s)
+        for b in range(1, 4):
+            z_narrow_out(1, b)
 
         y_unit(0)
-        for part in range(2):
-            f_bank(2, 1, part, "vector")
-        y_unit(1)
-        f_quantise(2)
-        z_quantise(1)
-        cs_quantise(4, 2)
         for g in range(2):
             for part in range(2):
-                f_bank(3, g, part, ("scalar", "vector")[g])
+                f_bank(2, g, part, "scalar" if g + part == 2 else "vector")
+        y_unit(1)
+        for s in (4, 5):
+            cs_turn(s)
+            cs_out(s)
+        f_quantise(2)
+        z_quantise(1)
+        cs_quantise(2)
+        cs_blocks(6)
+        cs_blocks(7)
+        for g in range(2):
+            for part in range(2):
+                f_bank(3, g, part)
         y_unit(2)
-        cs_quantise(6, 2)
+        cs_join(6)
+        cs_join(7)
 
         later = [(s, g) for s in range(4, STRIPS) for g in range(2)]
         summed = 0
@@ -473,6 +507,8 @@ def tile_isar_split_real_image_s11_kernel(
                 first_engine = "vector" if step == len(later) - 1 else "scalar"
                 for x, eng in enumerate((first_engine, "vector")):
                     f_bank(s, g, x, eng)
+            if step == 1:
+                cs_quantise(3)
             lag = SUM_LAG if step < len(later) else 1
             count = 2 if summed < PAIRED_SUMS else 1
             while summed + count - 1 <= n - lag:

from contextlib import ExitStack

import concourse.mybir as mybir
from concourse.masks import make_identity

D, J, T, L, R = 1024, 512, 1024, 1024, 1024

F32 = mybir.dt.float32
BF16 = mybir.dt.bfloat16
I32 = mybir.dt.int32
U32 = mybir.dt.uint32
U8 = mybir.dt.uint8
FP8 = mybir.dt.float8_e4m3fn
FP8X4 = mybir.dt.float8_e4m3fn_x4
FP4X4 = mybir.dt.float4_e2m1fn_x4
ACT = mybir.ActivationFunctionType
ALU = mybir.AluOpType

P = 128
BANK = 512
STRIPS = D // P
TILES = T // P
ECHO_LOADS = ((0, 1), (1, 1), (2, 1), (3, 1), (4, 2), (6, 2))
EARLY_STRIPS = 3
PAIRED_SUMS = 8
SUM_LAG = 1
H_GPSIMD = 80
H_SCALAR = 64
LAST_PIECES = (256, 256, 256, 128, 128)

FLOPS = 2 * (2 * D * J * T + T * L * R + 2 * D * T * R)


def tile_isar_split_real_image_s11_kernel(
    tc, cs, h, echo_bytes, echo_scale, w_words, w_scales, taper, out
):
    nc = tc.nc
    with ExitStack() as ctx:
        keep = ctx.enter_context(tc.tile_pool(name="keep", bufs=1))
        work = ctx.enter_context(tc.tile_pool(name="work", bufs=4))
        outs = ctx.enter_context(tc.tile_pool(name="outs", bufs=6))
        psum = ctx.enter_context(tc.psum_pool(name="psum", bufs=1))

        ident = keep.tile([P, P], F32, name="ident", align_bytes=64)
        scale = keep.tile([P, 2, 4], F32, name="scale")
        taper_bf = keep.tile([P, 2, 4], BF16, name="taper_bf")
        gain = keep.tile([P, 2, 4], F32, name="gain")
        cs_single = [keep.tile([P, 2, J], BF16, name="cs_single%d" % j, align_bytes=64) for j in range(2)]
        cs_pair = [keep.tile([P, 2, 2, J], BF16, name="cs_pair%d" % c, align_bytes=64) for c in range(1, 3)]
        cs_raw = [cs_single[0][:], cs_single[1][:]] + [cs_pair[c][:, :, j, :] for c in range(2) for j in range(2)]
        cs_quarters = keep.tile([P, 2, 8, P], BF16, name="cs_quarters", align_bytes=64)
        z_woven = [keep.tile([P, R, 4], BF16, name="z_woven%d" % half, align_bytes=64) for half in range(2)]
        cs_late = keep.tile([P, R, 4], BF16, name="cs_late", align_bytes=64)
        cs_woven = [z_woven[0][:, BANK:R], z_woven[1][:, BANK:R], cs_late[:, 0:BANK], cs_late[:, BANK:R]]
        cs_q = keep.tile([P, STRIPS * 2 * P], U32, name="cs_q", align_bytes=64)
        cs_s = keep.tile([P, STRIPS * 2 * P], U8, name="cs_s", align_bytes=64)
        h_raw = [keep.tile([P, 4, BANK], BF16, name="h_raw%d" % g, align_bytes=64) for g in range(2)]
        h_q = [keep.tile([P, BANK], U32, name="h_q%d" % g, align_bytes=64) for g in range(2)]
        h_s = [keep.tile([P, BANK], U8, name="h_s%d" % g, align_bytes=64) for g in range(2)]
        e_bytes = [keep.tile([P, n, L], U8, name="e_bytes%d" % i, align_bytes=64) for i, n in ECHO_LOADS]
        e_in = [e_bytes[x][:, j, :] for x, (i, n) in enumerate(ECHO_LOADS) for j in range(n)]
        spare = BANK - (P - H_SCALAR)
        woven = keep.tile([P, spare + TILES * 2 * P, 4], BF16, name="woven", align_bytes=64)
        e_at = [spare + 2 * P * ((i - 1) % TILES) for i in range(TILES)]
        h_woven = [woven[:, 0:BANK, :], woven[:, e_at[2] : e_at[4], :]]
        e_q = keep.tile([P, TILES * 2 * P], U32, name="e_q", align_bytes=64)
        e_s = keep.tile([P, TILES * 2 * P], U8, name="e_s", align_bytes=64)
        w_q = [keep.tile([P, 2, R], U8, name="w_q%d" % half, align_bytes=64) for half in range(2)]
        w_s = keep.tile([P, 2, R], U8, name="w_s", align_bytes=64)
        f_q = [keep.tile([P, BANK], U32, name="f_q%d" % s, align_bytes=64) for s in range(STRIPS)]
        f_s = [keep.tile([P, BANK], U8, name="f_s%d" % s, align_bytes=64) for s in range(STRIPS)]
        z_q = [keep.tile([P, R], U32, name="z_q%d" % half, align_bytes=64) for half in range(2)]
        z_s = [keep.tile([P, R], U8, name="z_s%d" % half, align_bytes=64) for half in range(2)]
        e_wide = {}
        cs_sorted = {}
        cs_turned = {}
        f_woven = {}
        z_rows = {}
        banks = {}
        squares = {}
        halves = {}
        free_banks = [psum.tile([P, BANK], F32, name="bank%d" % b) for b in range(8)]

        def bank(*key):
            if key not in banks:
                banks[key] = free_banks[0]
                free_banks.remove(banks[key])
            return banks[key]

        def emptied(*key):
            free_banks.append(banks[key])
            return banks[key]

        def copy(eng, dst, src):
            if eng == "vector":
                nc.vector.tensor_copy(out=dst, in_=src)
            elif eng == "gpsimd":
                nc.gpsimd.tensor_scalar(out=dst, in0=src, scalar1=1.0, scalar2=0.0, op0=ALU.mult, op1=ALU.add)
            else:
                nc.scalar.copy(out=dst, in_=src)

        def quantise(codes, scales, woven):
            nc.vector.quantize_mx(out=codes.bitcast(FP8X4), scales=scales, in_=woven.rearrange("p n t -> p (n t)"))

        def load_echo(x):
            i, n = ECHO_LOADS[x]
            g, t = divmod(i, 4)
            rows = echo_bytes[g * BANK : (g + 1) * BANK, :].rearrange("(m t) k -> m t k", t=4)
            nc.sync.dma_start(out=e_bytes[x][:], in_=rows[:, t : t + n, :])

        def load_strip(j):
            rows = cs.rearrange("(a c p j) k -> c j p a k", a=2, p=P, j=2)
            nc.sync.dma_start(out=cs_single[j][:], in_=rows[0, j])

        def load_pair(c):
            rows = cs.rearrange("(a c p j) k -> c p a (j k)", a=2, p=P, j=2)
            nc.sync.dma_start(out=cs_pair[c - 1][:].rearrange("p a j k -> p a (j k)"), in_=rows[c])

        def load_quarters():
            for part in range(2):
                rows = cs[part * D + 6 * P : (part + 1) * D, :].rearrange("(c b) (q k) -> q b c k", b=32, q=4)
                for q in (0, 2, 1, 3):
                    nc.sync.dma_start(out=cs_quarters[32 * q : 32 * (q + 1), part], in_=rows[q])

        def load_h(g):
            rows = h.rearrange("(p j) w -> p j w", j=4)
            nc.sync.dma_start(out=h_raw[g][:], in_=rows[:, :, g * BANK : (g + 1) * BANK])

        def load_w(half):
            words = w_words[:, :, half * R : (half + 1) * R].bitcast(I32)
            nc.sync.dma_start(out=w_q[half][:].bitcast(I32), in_=words.rearrange("g p n -> p g n"))

        def load_w_scales():
            for q in (0, 2, 1, 3):
                rows = w_scales[:, 4 * q : 4 * q + 4, :].bitcast(I32)
                nc.sync.dma_start(out=w_s[32 * q : 32 * q + 4, :, :].bitcast(I32), in_=rows.rearrange("g q n -> q g n"))

        def cs_sort(s):
            ordered = work.tile([P, 2, 2, P], F32, name="cs_sorted", bufs=2, align_bytes=64)
            cs_sorted[s] = ordered
            nc.scalar.copy(out=ordered[:], in_=cs_raw[s].bitcast(F32).rearrange("p a (m u) -> p a u m", u=2))

        def cs_turn(s):
            for part in range(2):
                words = cs_raw[s][:, part, :].bitcast(F32)
                for u in range(2):
                    src = cs_sorted[s][:, part, u, :] if s in cs_sorted else words[:, u : 2 * P : 2]
                    at = (2 * part + u) * P
                    nc.tensor.transpose(bank("cs", s)[:, at : at + P], src, ident[:])

        def cs_out(s, eng="scalar"):
            dst = cs_woven[s // 2][:, 2 * P * (s % 2) : 2 * P * (s % 2 + 1), :].rearrange("p n t -> p (n t)").bitcast(F32)
            copy(
                eng,
                dst.rearrange("p (a m u) -> p a m u", a=2, u=2),
                emptied("cs", s)[:].rearrange("p (a u m) -> p a m u", a=2, u=2),
            )

        def cs_sort_quarters(s):
            ordered = work.tile([P, 2, 4, 2, 32], F32, name="quarters_sorted", bufs=2, align_bytes=64)
            cs_sorted[s] = ordered
            words = cs_quarters[:, :, 4 * (s - 6) : 4 * (s - 5), :].bitcast(F32)
            nc.scalar.copy(out=ordered[:], in_=words.rearrange("p a c (w u) -> p a c u w", u=2))

        def cs_blocks(s):
            turned = work.tile([P, BANK], F32, name="cs_turned", bufs=2, align_bytes=64)
            cs_turned[s] = turned
            nc.vector.transpose(out=turned[:], in_=cs_sorted[s][:].rearrange("p a c u w -> p (a c u w)"))

        def cs_join(s):
            dst = cs_woven[3][:, 2 * P * (s - 6) : 2 * P * (s - 5), :].rearrange("p n t -> p (n t)").bitcast(F32)
            nc.vector.tensor_copy(
                out=dst.rearrange("p (c b u) -> p c b u", b=32, u=2),
                in_=cs_turned[s][:].rearrange("p (c u b) -> p c b u", u=2, b=32),
            )

        def cs_quantise(c):
            cols = slice(c * BANK, (c + 1) * BANK)
            quantise(cs_q[:, cols], cs_s[:, cols], cs_woven[c])

        def h_weave(g, eng, ms=slice(0, P)):
            copy(
                eng,
                h_woven[g].rearrange("p (t m) j -> p m t j", t=4)[:, ms],
                h_raw[g][:].rearrange("p j (m t) -> p m t j", t=4)[:, ms],
            )

        def h_quantise(g):
            quantise(h_q[g][:], h_s[g][:], h_woven[g])

        def echo_widen(i, eng, pieces=1):
            wide = work.tile([P, L], BF16, name="e_wide", bufs=TILES, align_bytes=64)
            e_wide[i] = wide
            for at in range(0, L, L // pieces):
                ks = slice(at, at + L // pieces)
                copy(eng, wide[:, ks], e_in[i][:, ks].bitcast(FP8))

        def echo_turn(i):
            words = e_wide[i][:].bitcast(F32)
            for k in range(2):
                for u in range(2):
                    at = (2 * u + k) * P
                    src = words[:, 2 * P * k + u : 2 * P * (k + 1) : 2]
                    nc.tensor.transpose(bank("echo", i)[:, at : at + P], src, ident[:])

        def echo_out(i):
            dst = woven[:, e_at[i] : e_at[i] + 2 * P, :]
            nc.vector.tensor_tensor(
                out=dst.rearrange("p (k m) (u e) -> p k m u e", k=2, u=2),
                in0=emptied("echo", i)[:].bitcast(BF16).rearrange("p (u k m e) -> p k m u e", u=2, k=2, e=2),
                in1=scale[:].rearrange("p k (u e) -> p k u e", u=2).unsqueeze(2).to_broadcast([P, 2, P, 2, 2]),
                op=ALU.mult,
            )

        def echo_quantise(i, count=1):
            cols = slice(2 * P * i, 2 * P * (i + count))
            quantise(e_q[:, cols], e_s[:, cols], woven[:, e_at[i] : e_at[i] + 2 * P * count, :])

        def f_mm(s, g, part):
            acc = bank("f", s, g, part)
            bins = slice((2 * s + part) * P, (2 * s + part + 1) * P)
            for t in range(4):
                slot = slice(t * P, (t + 1) * P)
                nc.tensor.matmul_mx(
                    out=acc[:, slot],
                    lhsT=h_q[g][:, slot].bitcast(FP8X4),
                    lhsT_scale=h_s[g][:, slot],
                    rhs=cs_q[:, bins].bitcast(FP8X4),
                    rhs_scale=cs_s[:, bins],
                    start=True,
                    stop=True,
                )

        def f_out(s, g, part, eng):
            if s not in f_woven:
                fresh = work.tile([P, BANK, 4], BF16, name="f_woven", bufs=4, align_bytes=64)
                f_woven[s] = fresh[:]
            at = (2 * g + part) * P
            copy(eng, f_woven[s][:, at : at + P, :], emptied("f", s, g, part)[:].rearrange("p (t n) -> p n t", t=4))

        def f_bank(s, g, part, eng="scalar"):
            f_mm(s, g, part)
            f_out(s, g, part, eng)

        def f_quantise(s):
            quantise(f_q[s][:], f_s[s][:], f_woven[s])

        def z_passes(acc, g, t, first, width):
            half, at = divmod(first, BANK)
            for k in range(2):
                cols = slice((2 * (4 * g + t) + k) * P, (2 * (4 * g + t) + k + 1) * P)
                nc.tensor.matmul_mx(
                    out=acc,
                    lhsT=e_q[:, cols].bitcast(FP8X4),
                    lhsT_scale=e_s[:, cols],
                    rhs=w_q[half][:, k, 2 * at : 2 * (at + width)].bitcast(FP4X4),
                    rhs_scale=w_s[:, k, first : first + width],
                    start=(k == 0),
                    stop=(k == 1),
                )

        def z_wide_mm(t, half):
            z_passes(bank("z wide", t, half)[:], 0, t, half * BANK, BANK)

        def z_wide_out(t, half):
            if half not in z_rows:
                fresh = work.tile([P, 4, BANK], BF16, name="z_rows", bufs=2, align_bytes=64)
                z_rows[half] = fresh
            nc.scalar.activation(
                out=z_rows[half][:, t, :], in_=emptied("z wide", t, half)[:], func=ACT.Copy, scale=gain[:, 0, t : t + 1]
            )

        def z_wide(t, half):
            z_wide_mm(t, half)
            z_wide_out(t, half)

        def z_weave(half):
            copy("gpsimd", z_woven[half][:, BANK:R, :], z_rows[half][:].rearrange("p t n -> p n t"))

        def z_narrow_mm(half, b, slots=range(4)):
            for t in slots:
                z_passes(bank("z narrow", half, b)[:, t * P : (t + 1) * P], 1, t, half * BANK + b * P, P)

        def z_narrow_out(half, b):
            nc.vector.tensor_tensor(
                out=z_woven[half][:, b * P : (b + 1) * P, :],
                in0=emptied("z narrow", half, b)[:].rearrange("p (t n) -> p n t", t=4),
                in1=gain[:, 1, :].unsqueeze(1).to_broadcast([P, P, 4]),
                op=ALU.mult,
            )

        def z_quantise(half):
            quantise(z_q[half][:], z_s[half][:], z_woven[half][:])

        units = [(s, half) for half in range(2) for s in range(EARLY_STRIPS)]
        units = units + [(s, half) for s in range(EARLY_STRIPS, STRIPS) for half in range(2)]
        units = [(s, half * BANK, BANK) for s, half in units]
        units = units[:-2] + [(STRIPS - 1, sum(LAST_PIECES[:x]), width) for x, width in enumerate(LAST_PIECES)]

        def shared(name, n, bufs):
            if (name, n // 2) not in halves:
                fresh = outs.tile([P, R], F32, name=name, bufs=bufs, align_bytes=64)
                halves[name, n // 2] = fresh
            return halves[name, n // 2][:, (n % 2) * BANK :]

        def y_unit(n):
            s, first, width = units[n]
            half, at = divmod(first, BANK)
            for part in range(2):
                acc = bank("y", s, first, part)
                for g in range(2):
                    bins = slice((2 * g + part) * P, (2 * g + part + 1) * P)
                    cols = slice((1 - g) * BANK + at, (1 - g) * BANK + at + width)
                    nc.tensor.matmul_mx(
                        out=acc[:, 0:width],
                        lhsT=f_q[s][:, bins].bitcast(FP8X4),
                        lhsT_scale=f_s[s][:, bins],
                        rhs=z_q[half][:, cols].bitcast(FP8X4),
                        rhs_scale=z_s[half][:, cols],
                        start=(g == 0),
                        stop=(g == 1),
                    )
                square = shared("square%d" % part, n, (4, 3)[part])
                nc.scalar.activation(
                    out=square[:, 0:width], in_=emptied("y", s, first, part)[:, 0:width], func=ACT.Square
                )
                squares[n, part] = square

        def y_piece(n):
            s, first, width = units[n]
            half, at = divmod(first, BANK)
            acc = bank("y", s, first)
            for part in range(2):
                for g in range(2):
                    bins = slice((2 * g + part) * P, (2 * g + part + 1) * P)
                    cols = slice((1 - g) * BANK + at, (1 - g) * BANK + at + width)
                    nc.tensor.matmul_mx(
                        out=acc[:, part * width : (part + 1) * width],
                        lhsT=f_q[s][:, bins].bitcast(FP8X4),
                        lhsT_scale=f_s[s][:, bins],
                        rhs=z_q[half][:, cols].bitcast(FP8X4),
                        rhs_scale=z_s[half][:, cols],
                        start=(g == 0),
                        stop=(g == 1),
                    )
            square = shared("square0", n, 4)
            nc.scalar.activation(
                out=square[:, 0 : 2 * width], in_=emptied("y", s, first)[:, 0 : 2 * width], func=ACT.Square
            )
            for part in range(2):
                squares[n, part] = square[:, part * width :]

        def y_sum(n, count):
            total = shared("total", n, 4)
            both = count * units[n][2]
            nc.vector.tensor_tensor(
                out=total[:, 0:both], in0=squares[n, 0][:, 0:both], in1=squares[n, 1][:, 0:both], op=ALU.add
            )
            for x in range(count):
                s, first, width = units[n + x]
                if s < 6:
                    rows = out.rearrange("(c p j) r -> c j p r", p=P, j=2)[s // 2, s % 2]
                else:
                    rows = out[s * P : (s + 1) * P, :]
                nc.sync.dma_start(out=rows[:, first : first + width], in_=total[:, x * width : (x + 1) * width])

        ctx.enter_context(tc.manual_schedule())
        make_identity(nc, ident[:])
        nc.vector.memset(w_s[:].bitcast(I32), 0)

        load_echo(0)
        load_echo(1)
        load_echo(2)
        load_echo(3)
        nc.sync.dma_start(out=scale[:], in_=echo_scale.rearrange("o (g p t) -> p (o g) t", g=2, t=4))
        load_echo(4)
        load_strip(0)
        load_w(0)
        load_w_scales()
        load_echo(5)
        nc.sync.dma_start(out=taper_bf[:], in_=taper.rearrange("(g p t) -> p g t", p=P, t=4))
        load_h(0)
        load_strip(1)
        load_h(1)
        load_w(1)
        load_pair(1)
        load_pair(2)
        load_quarters()

        echo_widen(0, "vector", pieces=2)
        echo_widen(1, "scalar")
        echo_widen(2, "vector")
        for i in (3, 5, 6, 7):
            echo_widen(i, "scalar")
        nc.scalar.activation(out=gain[:], in_=taper_bf[:], func=ACT.Copy)

        echo_turn(0)
        echo_turn(2)
        echo_out(0)
        echo_widen(4, "vector")
        echo_turn(1)
        cs_turn(0)
        for i in range(3, 6):
            echo_turn(i)
        echo_out(2)
        echo_quantise(0)
        cs_out(0)
        echo_out(1)
        z_wide_mm(0, 0)
        echo_out(3)
        echo_quantise(1, 2)
        echo_turn(6)
        echo_turn(7)
        cs_turn(1)
        echo_quantise(3)
        h_weave(0, "gpsimd", slice(H_SCALAR, P))
        h_weave(1, "gpsimd", slice(0, H_GPSIMD))
        h_weave(0, "scalar", slice(0, H_SCALAR))
        z_wide_out(0, 0)
        cs_out(1)

        echo_out(4)
        z_wide(1, 0)
        echo_out(5)
        z_wide(2, 0)
        z_wide(3, 0)
        echo_out(6)
        z_wide(0, 1)
        z_wide(1, 1)
        z_wide_mm(2, 1)
        z_wide_mm(3, 1)
        cs_turn(2)
        cs_turn(3)
        echo_out(7)
        h_weave(1, "scalar", slice(H_GPSIMD, P))
        z_wide_out(2, 1)
        cs_out(2)
        cs_out(3)
        z_wide_out(3, 1)
        echo_quantise(4, 2)
        h_quantise(0)
        echo_quantise(6, 2)
        cs_quantise(0)
        h_quantise(1)

        for slots in ((0, 1), (2, 3)):
            for b in range(4):
                z_narrow_mm(0, b, slots)
        z_weave(0)
        cs_sort(4)
        cs_sort(5)
        for s in range(2):
            for part in range(2):
                f_mm(s, 0, part)
        for b in range(4):
            z_narrow_out(0, b)
        z_narrow_mm(1, 0)
        for s in range(2):
            for part in range(2):
                f_out(s, 0, part, "scalar")
        z_narrow_out(1, 0)
        for s in range(2):
            for part in range(2):
                f_bank(s, 1, part)
        cs_sort_quarters(6)
        cs_sort_quarters(7)
        for b in range(1, 4):
            z_narrow_mm(1, b)
        z_quantise(0)
        f_quantise(0)
        cs_quantise(1)
        f_quantise(1)
        z_weave(1)
        for b in range(1, 4):
            z_narrow_out(1, b)

        y_unit(0)
        for g in range(2):
            for part in range(2):
                f_bank(2, g, part, "scalar" if g + part == 2 else "vector")
        y_unit(1)
        for s in (4, 5):
            cs_turn(s)
            cs_out(s)
        f_quantise(2)
        z_quantise(1)
        cs_quantise(2)
        cs_blocks(6)
        cs_blocks(7)
        for g in range(2):
            for part in range(2):
                f_bank(3, g, part)
        y_unit(2)
        cs_join(6)
        cs_join(7)

        later = [(s, g) for s in range(4, STRIPS) for g in range(2)]
        summed = 0
        for n in range(3, len(units)):
            (y_unit if units[n][2] == BANK else y_piece)(n)
            step = n - 3
            done = 3 + step // 2 if step % 2 == 0 and step <= len(later) else None
            if done is not None:
                f_quantise(done)
            if step < len(later):
                s, g = later[step]
                first_engine = "vector" if step == len(later) - 1 else "scalar"
                for x, eng in enumerate((first_engine, "vector")):
                    f_bank(s, g, x, eng)
            if step == 1:
                cs_quantise(3)
            lag = SUM_LAG if step < len(later) else 1
            count = 2 if summed < PAIRED_SUMS else 1
            while summed + count - 1 <= n - lag:
                y_sum(summed, count)
                summed = summed + count
                count = 2 if summed < PAIRED_SUMS else 1
        y_sum(len(units) - 1, 1)
